import numpy as np
import ml_dtypes


def mxq(x, axis, fmt="e4m3"):
    dtype, down = {"e4m3": (ml_dtypes.float8_e4m3fn, 7), "e5m2": (ml_dtypes.float8_e5m2, 14)}[fmt]
    v = np.moveaxis(np.asarray(x, np.float32).astype(ml_dtypes.bfloat16).astype(np.float64), axis, -1)
    blocks = v.reshape(v.shape[:-1] + (-1, 32))
    amax = np.abs(blocks).max(-1, keepdims=True)
    byte = np.maximum(np.where(amax > 0, np.frexp(amax)[1] - 1 + 127, 0) - down, 1)
    scale = np.exp2(byte - 127.0)
    codes = (blocks / scale).astype(np.float32).astype(dtype).astype(np.float64)
    return np.moveaxis((codes * scale).reshape(v.shape), -1, axis)


WIDE = False


def mx_kscale(k):
    if not WIDE:
        return np.ones(k)
    levels = np.array([10, -10, 5, -5, 0])
    if k % 512:
        return np.exp2(np.random.permutation(np.resize(levels, k // 32))).repeat(32)
    a = np.empty((k // 512, 16))
    for p in range(k // 512):
        a[p, :8] = np.random.permutation(np.resize(levels, 8))
        for g in range(8):
            far = levels[np.abs(levels - a[p, g]) >= 10]
            a[p, g + 8] = far[np.random.randint(len(far))]
    return np.exp2(a.ravel()).repeat(32)


def f64(x):
    return np.asarray(x).astype(np.float64)


def striped(idx):
    return np.tile(idx.reshape(-1, 16).T, (8, 1)).astype(np.uint16)


def unstriped(offs):
    return offs[:16].T.reshape(-1).astype(np.int64)


E2M1 = np.array([0.0, 0.5, 1.0, 1.5, 2.0, 3.0, 4.0, 6.0, -0.0, -0.5, -1.0, -1.5, -2.0, -3.0, -4.0, -6.0])


def pack_weight(w, fmt):
    k, n = w.shape
    w = f64(np.asarray(w, np.float32).astype(ml_dtypes.bfloat16)).reshape(k // 32, 32, n)
    amax = np.abs(w).max(1)
    if fmt == "e4m3":
        byte = np.frexp(amax)[1] - 1 + 127 - 7
    else:
        mant, ex = np.frexp(amax / 6.0)
        byte = np.where(mant > 0.5, ex, ex - 1) + 127
    byte = np.clip(np.where(amax > 0, byte, 1), 1, 254)
    scaled = (w * np.exp2(127.0 - byte)[:, None, :]).reshape(k, n).astype(np.float32)
    by_word = np.ascontiguousarray(scaled.reshape(k // 512, 128, 4, n).transpose(0, 1, 3, 2))
    if fmt == "e4m3":
        words = by_word.astype(ml_dtypes.float8_e4m3fn).view(np.uint8)
    else:
        c = by_word.astype(ml_dtypes.float4_e2m1fn).view(np.uint8) & 0xF
        words = (c[..., 0::2] | (c[..., 1::2] << 4)).reshape(k // 512, 128, 2 * n)
    return np.ascontiguousarray(words), np.ascontiguousarray(byte.astype(np.uint8).reshape(k // 512, 16, n))


def unpack_weight(words, scales, fmt):
    g, _, n = scales.shape
    words = np.ascontiguousarray(words).reshape(g, 128, n, -1)
    if fmt == "e4m3":
        vals = words.view(ml_dtypes.float8_e4m3fn).astype(np.float64)
    else:
        nib = np.empty((g, 128, n, 4), np.uint8)
        nib[..., 0::2] = words & 0xF
        nib[..., 1::2] = words >> 4
        vals = E2M1[nib]
    vals = vals * np.repeat(np.exp2(scales.astype(np.float64) - 127.0), 8, axis=1)[..., None]
    return vals.transpose(0, 1, 3, 2).reshape(g * 512, n)


def gelu(v):
    return 0.5 * v * (1.0 + np.tanh(np.sqrt(2.0 / np.pi) * (v + 0.044715 * v**3)))


K, H, N, T, S, T2, P = 512, 1536, 640, 2048, 1024, 2048, 1024


def setup_inputs():
    n = np.random.standard_normal
    s = mx_kscale(K)[:, None]
    u = mx_kscale(H)[:, None]
    tab_words, tab_scales = pack_weight(n((K, T)) * s, "e4m3")
    wr_words, wr_scales = pack_weight(n((K, H)) / np.sqrt(K) * u.T / s, "e2m1")
    wq = (n((K, H)) / np.sqrt(K) * u.T / s).astype(np.float32)
    nv = (np.random.uniform(0.3, 1.0, H) * u[:, 0] ** 2).astype(np.float32)
    wgs = np.exp(0.3 * n((128, S))).astype(np.float32)
    err = (0.7 * n((H, P)) * u).astype(np.float32)
    wm_words, wm_scales = pack_weight(n((H, N)) / np.sqrt(H) / u, "e4m3")
    return {"tab_words": tab_words, "tab_scales": tab_scales,
            "offs": striped(np.random.permutation(T)[:S]),
            "wr_words": wr_words, "wr_scales": wr_scales, "wq": wq, "nv": nv,
            "wgs": wgs, "offs2": striped(np.random.permutation(T2)[:S]),
            "offs3": striped(np.random.permutation(T2)[:P]), "err": err,
            "wm_words": wm_words, "wm_scales": wm_scales}


def reference(tab_words, tab_scales, offs, wr_words, wr_scales, wq, nv, wgs, offs2, offs3, err, wm_words, wm_scales):
    v = unpack_weight(tab_words, tab_scales, "e4m3")[:, unstriped(offs)]
    wr = unpack_weight(wr_words, wr_scales, "e2m1")
    re = wr.T @ v
    im = mxq(f64(wq), 0, "e4m3").T @ v
    h = np.sqrt(np.square(re) + np.square(im) + f64(nv)[:, None])
    page = np.zeros((H, T2))
    page[:, unstriped(offs2)] = np.tile(f64(wgs), (H // 128, 1)) * h
    x = page[:, unstriped(offs3)]
    z = x + f64(err)
    wm = unpack_weight(wm_words, wm_scales, "e4m3")
    return wm.T @ mxq(z, 0, "e4m3")

@@ -1,0 +1,310 @@
+from contextlib import ExitStack
+
+import concourse.mybir as mybir
+from concourse.masks import make_identity
+
+K, H, N, T, S, T2, M = 512, 1536, 640, 2048, 1024, 2048, 1024
+FLOPS = 2 * K * H * S * 2 + 2 * H * N * M
+
+F32 = mybir.dt.float32
+BF16 = mybir.dt.bfloat16
+I32 = mybir.dt.int32
+U32 = mybir.dt.uint32
+U16 = mybir.dt.uint16
+U8 = mybir.dt.uint8
+E4M3 = mybir.dt.float8_e4m3fn_x4
+E2M1 = mybir.dt.float4_e2m1fn_x4
+ACT = mybir.ActivationFunctionType
+ALU = mybir.AluOpType
+
+P = 128
+PASS = 512
+LIST_ROWS = 16
+H_SLOTS = 8
+CHUNKS = ((0, 256), (256, 256), (512, 256), (768, 128), (896, 128))
+
+
+def tile_list_pilot_envelope_reliability_kernel(
+    tc, tab_words, tab_scales, offs, wr_words, wr_scales, wq, nv, wgs, offs2, offs3, err, wm_words, wm_scales, out
+):
+    nc = tc.nc
+    with ExitStack() as ctx:
+        sb = ctx.enter_context(tc.tile_pool(name="sb", bufs=1))
+        ps = ctx.enter_context(tc.psum_pool(name="ps", bufs=1))
+
+        def tile(name, width, dtype):
+            return sb.tile([P, width], dtype, name=name, align_bytes=64)
+
+        def tiles(name, count, width, dtype):
+            return [tile("%s%d" % (name, i), width, dtype) for i in range(count)]
+
+        pilots = tile("pilots", S // LIST_ROWS, U16)
+        slots = tile("slots", S // LIST_ROWS, U16)
+        carriers = tile("carriers", M // LIST_ROWS, U16)
+        tab_w = tile("tab_w", T, I32)
+        tab_s = tile("tab_s", T, U8)
+        v_w = tile("v_w", S, U32)
+        v_s = tile("v_s", S, U8)
+        wr_w = tiles("wr_w", 3, 2 * PASS, U8)
+        wr_s = tile("wr_s", H, U8)
+        wq_w = tiles("wq_w", 3, PASS, U32)
+        wq_s = tiles("wq_s", 3, PASS, U8)
+        wm_w = tile("wm_w", 3 * N, I32)
+        wm_s = tile("wm_s", 3 * N, U8)
+        nv_first = tile("nv_first", 1, F32)
+        nv_rest = tile("nv_rest", 7, F32)
+        nv_last = tile("nv_last", 4, F32)
+        ident = tile("ident", P, F32)
+        wgs_nat = tile("wgs_nat", S, F32)
+        wgs_four = tile("wgs_four", 4 * S, F32)
+        pages = tiles("page", 4, T2, F32)
+        env = tiles("env", H_SLOTS, S, F32)
+        sq = tiles("sq", 4, 2 * PASS, F32)
+        err_t = tiles("err_t", 2, 4 * M, F32)
+        pick_pair = tile("pick_pair", 2 * M, F32)
+        pick = [pick_pair[:, 0:M], pick_pair[:, M : 2 * M]] + [one[:] for one in tiles("pick", 6, M, F32)]
+        z_rows = tiles("z_rows", 2, PASS, BF16)
+        stage = tile("stage", 4 * M, BF16)
+        z_w = tiles("z_w", 3, M, U32)
+        z_s = tiles("z_s", 3, M, U8)
+        banks = [ps.tile([P, PASS], F32, name="bank%d" % i) for i in range(8)]
+
+        def load_scale_rows(plane, rows):
+            for q in range(4):
+                nc.sync.dma_start(out=plane[32 * q : 32 * q + 4, :].bitcast(I32), in_=rows[4 * q : 4 * q + 4, :].bitcast(I32))
+
+        wq_parts = [(0, 128, pick[0][:, 0:512]), (128, 128, pick[0][:, 512:1024])]
+        wq_parts = wq_parts + [(256 * i, 256, pick[i]) for i in range(1, 6)]
+        wq_k = wq.rearrange("(p i) c -> p i c", i=4)
+
+        def load_wq(part):
+            c0, width, raw = wq_parts[part]
+            nc.sync.dma_start(out=raw.rearrange("p (i c) -> p i c", i=4), in_=wq_k[:, :, c0 : c0 + width])
+
+        def interleave(engine_copy, dst, src):
+            engine_copy(out=dst.rearrange("p (c x i) -> p c i x", x=4, i=4), in_=src.rearrange("p (i c x) -> p c i x", i=4, x=4))
+
+        def quantise_wq(parts, rounded):
+            first = wq_parts[parts[0]][0]
+            total = 0
+            for part in parts:
+                c0, width, raw = wq_parts[part]
+                interleave(nc.scalar.copy, rounded[:, 4 * (c0 - first) : 4 * (c0 - first + width)], raw)
+                total = total + width
+            a, c = divmod(first, PASS)
+            nc.vector.quantize_mx(out=wq_w[a][:, c : c + total].bitcast(E4M3), scales=wq_s[a][:, c : c + total], in_=rounded[:, 0 : 4 * total])
+
+        nc.vector.memset(tab_s[:].bitcast(I32), 0)
+        nc.gpsimd.memset(wr_s[:].bitcast(I32), 0)
+        nc.sync.dma_start(pilots[:], offs)
+        nc.sync.dma_start(slots[:], offs2)
+        with nc.allow_non_contiguous_dma(reason="one noise power a partition"):
+            nc.sync.dma_start(out=nv_first[:], in_=nv[0:P].rearrange("(b p) -> p b", p=P))
+        nc.sync.dma_start(out=wgs_nat[:, 0:256], in_=wgs[:, 0:256])
+        nc.sync.dma_start(out=wr_w[0][:].bitcast(I32), in_=wr_words[0][:, 0 : 2 * PASS].bitcast(I32))
+        load_wq(0)
+        nc.sync.dma_start(carriers[:], offs3)
+        nc.sync.dma_start(out=tab_w[:], in_=tab_words[0].rearrange("p t i -> p (t i)").bitcast(I32))
+        load_scale_rows(tab_s, tab_scales[0])
+        load_scale_rows(wr_s, wr_scales[0])
+        load_wq(1)
+        nc.sync.dma_start(out=wgs_nat[:, 256:1024], in_=wgs[:, 256:1024])
+        with nc.allow_non_contiguous_dma(reason="one noise power a partition"):
+            nc.sync.dma_start(out=nv_rest[:], in_=nv[P : 8 * P].rearrange("(b p) -> p b", p=P))
+        load_wq(2)
+        for a in (1, 2):
+            nc.sync.dma_start(out=wr_w[a][:].bitcast(I32), in_=wr_words[0][:, 2 * PASS * a : 2 * PASS * (a + 1)].bitcast(I32))
+        for part in range(3, 7):
+            load_wq(part)
+        nc.sync.dma_start(out=nv_last[:], in_=nv[2 * PASS : 3 * PASS].rearrange("(p t) -> p t", t=4))
+        for q in range(4):
+            nc.sync.dma_start(out=wgs_four[32 * q : 32 * q + 32, :], in_=wgs.rearrange("(r t) j -> r (t j)", t=4))
+        for a in (0, 1):
+            nc.sync.dma_start(
+                out=err_t[a][:].rearrange("p (t m) -> p t m", t=4),
+                in_=err[PASS * a : PASS * (a + 1), :].rearrange("(t p) m -> p t m", p=P),
+            )
+        nc.sync.dma_start(out=wm_w[:].rearrange("p (a c) -> p a c", a=3), in_=wm_words.rearrange("a p c i -> p a (c i)").bitcast(I32))
+        make_identity(nc, ident[:])
+        nc.vector.memset(pages[0][:], 0.0)
+        for page in pages[1:]:
+            nc.gpsimd.memset(page[:], 0.0)
+        nc.gpsimd.memset(wm_s[:].bitcast(I32), 0)
+        for q in range(4):
+            nc.sync.dma_start(
+                out=wm_s[32 * q : 32 * q + 4, :].bitcast(I32).rearrange("p (a c) -> p a c", a=3),
+                in_=wm_scales[:, 4 * q : 4 * q + 4, :].rearrange("a r c -> r a c").bitcast(I32),
+            )
+
+        def entries(lst, j0, width):
+            return lst[:, j0 // LIST_ROWS : (j0 + width) // LIST_ROWS]
+
+        def gather_words(j0, width):
+            nc.vector.tensor_copy(out=v_w[:, j0 : j0 + width], in_=tab_w[:].bitcast(U32).indirect(entries(pilots, j0, width)))
+
+        def gather_scales(j0, width):
+            nc.vector.tensor_copy(out=v_s[:, j0 : j0 + width], in_=tab_s[:].indirect(entries(pilots, j0, width)))
+
+        def first_products(out_re, out_im, j0, c0, width):
+            a, c = divmod(c0, PASS)
+            lhs = v_w[:, j0 : j0 + P].bitcast(E4M3)
+            lhs_s = v_s[:, j0 : j0 + P]
+            nc.tensor.matmul_mx(
+                out=out_im, lhsT=lhs, lhsT_scale=lhs_s,
+                rhs=wq_w[a][:, c : c + width].bitcast(E4M3), rhs_scale=wq_s[a][:, c : c + width], start=True, stop=True,
+            )
+            nc.tensor.matmul_mx(
+                out=out_re, lhsT=lhs, lhsT_scale=lhs_s,
+                rhs=wr_w[a][:, 2 * c : 2 * (c + width)].bitcast(E2M1), rhs_scale=wr_s[:, c0 : c0 + width], start=True, stop=True,
+            )
+
+        def add_turned(dst, first, second):
+            nc.tensor.matmul(out=dst, lhsT=first, rhs=ident[:], is_transpose=True, start=True, stop=False)
+            nc.tensor.matmul(out=dst, lhsT=second, rhs=ident[:], is_transpose=True, start=False, stop=True)
+
+        def envelope_rows(b, j0, width, product_banks, bank_sum, squares):
+            per_bank = width // (2 * P)
+            for n, bank in enumerate(product_banks):
+                for i in range(per_bank):
+                    first_products(bank[:, 2 * P * i : 2 * P * i + P], bank[:, 2 * P * i + P : 2 * P * (i + 1)], j0 + P * (per_bank * n + i), P * b, P)
+                nc.scalar.activation(out=squares[:, width * n : width * (n + 1)], in_=bank[:, 0:width], func=ACT.Square)
+            for i in range(width // P):
+                add_turned(bank_sum[:, P * i : P * (i + 1)], squares[:, 2 * P * i : 2 * P * i + P], squares[:, 2 * P * i + P : 2 * P * (i + 1)])
+            bias = nv_first[:, 0:1] if b == 0 else nv_rest[:, b - 1 : b]
+            nc.scalar.activation(out=env[b % H_SLOTS][:, j0 : j0 + width], in_=bank_sum[:, 0:width], func=ACT.Sqrt, bias=bias)
+
+        def envelope_last_pass(j0):
+            for i in range(4):
+                bank_re, bank_im = banks[2 * (i % 2)], banks[2 * (i % 2) + 1]
+                first_products(bank_re[:], bank_im[:], j0 + P * i, 2 * PASS, PASS)
+                for half, bank in enumerate((bank_re, bank_im)):
+                    nc.scalar.activation(
+                        out=sq[i][:, PASS * half : PASS * (half + 1)].rearrange("j (t p) -> j t p", t=4),
+                        in_=bank[:].rearrange("j (p t) -> j t p", t=4), func=ACT.Square,
+                    )
+            for t in range(4):
+                bank_sum = banks[4 + t % 2]
+                for i in range(4):
+                    add_turned(bank_sum[:, P * i : P * (i + 1)], sq[i][:, P * t : P * (t + 1)], sq[i][:, PASS + P * t : PASS + P * (t + 1)])
+                nc.scalar.activation(
+                    out=env[(8 + t) % H_SLOTS][:, j0 : j0 + PASS], in_=bank_sum[:], func=ACT.Sqrt, bias=nv_last[:, t : t + 1]
+                )
+
+        def scatter(b, j0, width):
+            t = b % 4
+            weights = wgs_nat[:, j0 : j0 + width] if b < 8 else wgs_four[:, S * t + j0 : S * t + j0 + width]
+            nc.vector.tensor_tensor(
+                out=pages[t][:].indirect(entries(slots, j0, width)), in0=env[b % H_SLOTS][:, j0 : j0 + width], in1=weights, op=ALU.mult
+            )
+
+        def gather_pass(a):
+            for t in range(4):
+                nc.vector.tensor_copy(out=pick[4 * a + t], in_=pages[t][:].indirect(carriers[:]))
+
+        def quantise_z(a, m0, width, grouped):
+            nc.vector.quantize_mx(out=z_w[a][:, m0 : m0 + width].bitcast(E4M3), scales=z_s[a][:, m0 : m0 + width], in_=grouped)
+
+        def add_errors_on_tensor(a, grouped):
+            words = grouped.bitcast(F32)
+            for pair in range(4):
+                bank_back = banks[6 + pair % 2]
+                for i in range(2):
+                    m0 = 2 * P * pair + P * i
+                    bank_sum = banks[4 + i]
+                    for t in range(4):
+                        add_turned(bank_sum[:, P * t : P * (t + 1)], err_t[a][:, M * t + m0 : M * t + m0 + P], pick[4 * a + t][:, m0 : m0 + P])
+                    nc.scalar.copy(
+                        out=z_rows[i][:].rearrange("m (u p e) -> m u p e", u=2, e=2),
+                        in_=bank_sum[:].rearrange("m (p u e) -> m u p e", u=2, e=2),
+                    )
+                    for u in range(2):
+                        nc.tensor.transpose(
+                            bank_back[:, P * (2 * i + u) : P * (2 * i + u + 1)], z_rows[i][:].bitcast(F32)[:, P * u : P * (u + 1)], ident[:]
+                        )
+                nc.scalar.copy(
+                    out=words[:, PASS * pair : PASS * (pair + 1)].rearrange("p (i m u) -> p i m u", i=2, u=2),
+                    in_=bank_back[:].rearrange("p (i u m) -> p i m u", i=2, u=2),
+                )
+            quantise_z(a, 0, M, grouped)
+
+        quantise_wq([0], stage[:])
+        for j0 in (0, 256):
+            gather_scales(j0, 256)
+            gather_words(j0, 256)
+        gather_scales(512, 512)
+        gather_words(512, 256)
+        gather_words(768, 256)
+        later_parts = {0: ([1], sq[0][:, 256:512]), 3: ([2], sq[3][:]), 5: ([3, 4], sq[1][:]), 7: ([5, 6], sq[3][:])}
+        steps = [(0, 0, 256), (0, 256, 256), (0, 512, 512)] + [(b, j0, PASS) for b in range(1, 8) for j0 in (0, PASS)]
+        for step, (b, j0, width) in enumerate(steps):
+            if step == 2:
+                envelope_rows(b, j0, width, [banks[2], banks[4]], banks[6], sq[step % 4])
+            else:
+                envelope_rows(b, j0, width, banks[2 * (step % 2) : 2 * (step % 2) + 2], banks[4 + step % 2], sq[step % 4])
+            if b == 0:
+                scatter(0, j0, width)
+            elif b < 4 and j0 > 0:
+                scatter(b, 0, S)
+            if step in later_parts:
+                quantise_wq(later_parts[step][0], later_parts[step][1].bitcast(BF16))
+        gather_pass(0)
+        for b in range(4, 8):
+            scatter(b, 0, S)
+        for j0 in (0, PASS):
+            envelope_last_pass(j0)
+        gather_pass(1)
+        for b in range(8, 12):
+            scatter(b, 0, S)
+        add_errors_on_tensor(0, stage[:])
+        nc.sync.dma_start(out=err_t[0][:], in_=err[2 * PASS : 3 * PASS, :].rearrange("(p t) m -> p (t m)", t=4))
+        add_errors_on_tensor(1, pick_pair[:].bitcast(BF16))
+
+        picked = [pick[0], pick[1], pick[2], pick[3][:, 0:512], pick[3][:, 512:1024]]
+        grouped = [pick[2][:, 0:512], pick[3][:, 0:512], pick[3][:, 512:1024], pick[4][:, 0:256], pick[5][:, 0:256]]
+        bank_sets = [banks[0:3], [banks[3], banks[6], banks[7]], banks[0:3], [banks[3], banks[6]], [banks[7], banks[0]]]
+        results = [err_t[1][:, 0:1280], err_t[1][:, 1280:2560], err_t[1][:, 2560:3840], env[4][:, 0:640], env[5][:, 0:640]]
+        out_n = out.rearrange("(i p) m -> p i m", p=P)
+
+        def gather_chunk(c):
+            m0, width = CHUNKS[c]
+            for t in range(4):
+                nc.vector.tensor_tensor(
+                    out=picked[c][:, width * t : width * (t + 1)], in0=pages[t][:].indirect(entries(carriers, m0, width)),
+                    in1=err_t[0][:, M * t + m0 : M * t + m0 + width], op=ALU.add,
+                )
+
+        def round_chunk(c, engine_copy):
+            interleave(engine_copy, grouped[c].bitcast(BF16), picked[c])
+
+        def finish_chunk(c):
+            m0, width = CHUNKS[c]
+            quantise_z(2, m0, width, grouped[c].bitcast(BF16))
+            per_bank = 2 if width == 256 else 3
+            for a in (1, 0, 2):
+                for i in range(5):
+                    bank, place = divmod(i, per_bank)
+                    nc.tensor.matmul_mx(
+                        out=bank_sets[c][bank][:, width * place : width * (place + 1)],
+                        lhsT=wm_w[:, N * a + P * i : N * a + P * (i + 1)].bitcast(E4M3), lhsT_scale=wm_s[:, N * a + P * i : N * a + P * (i + 1)],
+                        rhs=z_w[a][:, m0 : m0 + width].bitcast(E4M3), rhs_scale=z_s[a][:, m0 : m0 + width],
+                        start=(a == 1 and place == 0), stop=(a == 2 and (place == per_bank - 1 or i == 4)),
+                    )
+            for bank, i0 in enumerate(range(0, 5, per_bank)):
+                i1 = min(5, i0 + per_bank)
+                part = results[c][:, width * i0 : width * i1]
+                on_vector = c == len(CHUNKS) - 1 and bank == 1
+                engine_copy = nc.vector.tensor_copy if on_vector else nc.scalar.copy
+                engine_copy(out=part, in_=bank_sets[c][bank][:, 0 : width * (i1 - i0)])
+                if c == len(CHUNKS) - 1:
+                    queue = nc.sync if on_vector else nc.scalar
+                    queue.dma_start(out=out_n[:, i0:i1, m0 : m0 + width], in_=part.rearrange("p (i m) -> p i m", m=width))
+            if c < len(CHUNKS) - 1:
+                nc.sync.dma_start(out=out_n[:, :, m0 : m0 + width], in_=results[c].rearrange("p (i m) -> p i m", i=5))
+
+        last = len(CHUNKS) - 1
+        for c in range(len(CHUNKS)):
+            gather_chunk(c)
+            if c > 0:
+                finish_chunk(c - 1)
+            round_chunk(c, nc.vector.tensor_copy if c == last else nc.scalar.copy)
+        finish_chunk(last)

@@ -57,7 +57,8 @@ def tile_list_pilot_envelope_reliability_kernel(
         ident = tile("ident", P, F32)
         wgs_nat = tile("wgs_nat", S, F32)
         wgs_four = tile("wgs_four", 4 * S, F32)
-        pages = tiles("page", 4, T2, F32)
+        pages = tiles("page", 2, T2, F32)
+        first_sq = [sb.tile([P, PASS], F32, name="first_sq%d" % i, tag="late_page%d" % i, align_bytes=64) for i in range(2)]
         env = tiles("env", H_SLOTS, S, F32)
         sq = tiles("sq", 4, 2 * PASS, F32)
         err_t = tiles("err_t", 2, 4 * M, F32)
@@ -94,18 +95,22 @@ def tile_list_pilot_envelope_reliability_kernel(
             a, c = divmod(first, PASS)
             nc.vector.quantize_mx(out=wq_w[a][:, c : c + total].bitcast(E4M3), scales=wq_s[a][:, c : c + total], in_=rounded[:, 0 : 4 * total])
 
+        warm = tile("warm", 2, F32)
         nc.vector.memset(tab_s[:].bitcast(I32), 0)
         nc.gpsimd.memset(wr_s[:].bitcast(I32), 0)
+        nc.vector.memset(warm[:, 0:1], 1.0)
+        nc.scalar.activation(out=warm[:, 1:2], in_=warm[:, 0:1], func=ACT.Sqrt)
         nc.sync.dma_start(pilots[:], offs)
         nc.sync.dma_start(slots[:], offs2)
+        nc.sync.dma_start(carriers[:], offs3)
         with nc.allow_non_contiguous_dma(reason="one noise power a partition"):
             nc.sync.dma_start(out=nv_first[:], in_=nv[0:P].rearrange("(b p) -> p b", p=P))
-        nc.sync.dma_start(out=wgs_nat[:, 0:256], in_=wgs[:, 0:256])
-        nc.sync.dma_start(out=wr_w[0][:].bitcast(I32), in_=wr_words[0][:, 0 : 2 * PASS].bitcast(I32))
+        nc.sync.dma_start(out=nv_last[:], in_=nv[2 * PASS : 3 * PASS].rearrange("(p t) -> p t", t=4))
         load_wq(0)
-        nc.sync.dma_start(carriers[:], offs3)
-        nc.sync.dma_start(out=tab_w[:], in_=tab_words[0].rearrange("p t i -> p (t i)").bitcast(I32))
+        nc.sync.dma_start(out=wr_w[0][:].bitcast(I32), in_=wr_words[0][:, 0 : 2 * PASS].bitcast(I32))
+        nc.sync.dma_start(out=wgs_nat[:, 0:256], in_=wgs[:, 0:256])
         load_scale_rows(tab_s, tab_scales[0])
+        nc.sync.dma_start(out=tab_w[:], in_=tab_words[0].rearrange("p t i -> p (t i)").bitcast(I32))
         load_scale_rows(wr_s, wr_scales[0])
         load_wq(1)
         nc.sync.dma_start(out=wgs_nat[:, 256:1024], in_=wgs[:, 256:1024])
@@ -116,7 +121,6 @@ def tile_list_pilot_envelope_reliability_kernel(
             nc.sync.dma_start(out=wr_w[a][:].bitcast(I32), in_=wr_words[0][:, 2 * PASS * a : 2 * PASS * (a + 1)].bitcast(I32))
         for part in range(3, 7):
             load_wq(part)
-        nc.sync.dma_start(out=nv_last[:], in_=nv[2 * PASS : 3 * PASS].rearrange("(p t) -> p t", t=4))
         for q in range(4):
             nc.sync.dma_start(out=wgs_four[32 * q : 32 * q + 32, :], in_=wgs.rearrange("(r t) j -> r (t j)", t=4))
         for a in (0, 1):
@@ -126,9 +130,8 @@ def tile_list_pilot_envelope_reliability_kernel(
             )
         nc.sync.dma_start(out=wm_w[:].rearrange("p (a c) -> p a c", a=3), in_=wm_words.rearrange("a p c i -> p a (c i)").bitcast(I32))
         make_identity(nc, ident[:])
-        nc.vector.memset(pages[0][:], 0.0)
-        for page in pages[1:]:
-            nc.gpsimd.memset(page[:], 0.0)
+        for page in pages:
+            nc.vector.memset(page[:], 0.0)
         nc.gpsimd.memset(wm_s[:].bitcast(I32), 0)
         for q in range(4):
             nc.sync.dma_start(
@@ -228,25 +231,27 @@ def tile_list_pilot_envelope_reliability_kernel(
             quantise_z(a, 0, M, grouped)
 
         quantise_wq([0], stage[:])
-        for j0 in (0, 256):
-            gather_scales(j0, 256)
+        gather_scales(0, S)
+        for j0 in range(0, S, 256):
             gather_words(j0, 256)
-        gather_scales(512, 512)
-        gather_words(512, 256)
-        gather_words(768, 256)
-        later_parts = {0: ([1], sq[0][:, 256:512]), 3: ([2], sq[3][:]), 5: ([3, 4], sq[1][:]), 7: ([5, 6], sq[3][:])}
+        later_parts = {0: ([1], first_sq[0][:, 256:512]), 3: ([2], sq[3][:]), 5: ([3, 4], sq[1][:]), 7: ([5, 6], sq[3][:])}
         steps = [(0, 0, 256), (0, 256, 256), (0, 512, 512)] + [(b, j0, PASS) for b in range(1, 8) for j0 in (0, PASS)]
         for step, (b, j0, width) in enumerate(steps):
             if step == 2:
                 envelope_rows(b, j0, width, [banks[2], banks[4]], banks[6], sq[step % 4])
             else:
-                envelope_rows(b, j0, width, banks[2 * (step % 2) : 2 * (step % 2) + 2], banks[4 + step % 2], sq[step % 4])
+                squares = first_sq[step] if step < 2 else sq[step % 4]
+                envelope_rows(b, j0, width, banks[2 * (step % 2) : 2 * (step % 2) + 2], banks[4 + step % 2], squares)
             if b == 0:
                 scatter(0, j0, width)
             elif b < 4 and j0 > 0:
                 scatter(b, 0, S)
             if step in later_parts:
                 quantise_wq(later_parts[step][0], later_parts[step][1].bitcast(BF16))
+            if step < 2:
+                late_page = sb.tile([P, T2], F32, name="page%d" % (2 + step), tag="late_page%d" % step, align_bytes=64)
+                nc.gpsimd.memset(late_page[:], 0.0)
+                pages.append(late_page)
         gather_pass(0)
         for b in range(4, 8):
             scatter(b, 0, S)

@@ -176,19 +176,19 @@ def tile_list_pilot_envelope_reliability_kernel(
             bias = nv_first[:, 0:1] if b == 0 else nv_rest[:, b - 1 : b]
             nc.scalar.activation(out=env[b % H_SLOTS][:, j0 : j0 + width], in_=bank_sum[:, 0:width], func=ACT.Sqrt, bias=bias)
 
-        def envelope_last_pass(j0):
+        def envelope_last_pass(j0, squares):
             for i in range(4):
                 bank_re, bank_im = banks[2 * (i % 2)], banks[2 * (i % 2) + 1]
                 first_products(bank_re[:], bank_im[:], j0 + P * i, 2 * PASS, PASS)
                 for half, bank in enumerate((bank_re, bank_im)):
                     nc.scalar.activation(
-                        out=sq[i][:, PASS * half : PASS * (half + 1)].rearrange("j (t p) -> j t p", t=4),
+                        out=squares[i][:, PASS * half : PASS * (half + 1)].rearrange("j (t p) -> j t p", t=4),
                         in_=bank[:].rearrange("j (p t) -> j t p", t=4), func=ACT.Square,
                     )
             for t in range(4):
                 bank_sum = banks[4 + t % 2]
                 for i in range(4):
-                    add_turned(bank_sum[:, P * i : P * (i + 1)], sq[i][:, P * t : P * (t + 1)], sq[i][:, PASS + P * t : PASS + P * (t + 1)])
+                    add_turned(bank_sum[:, P * i : P * (i + 1)], squares[i][:, P * t : P * (t + 1)], squares[i][:, PASS + P * t : PASS + P * (t + 1)])
                 nc.scalar.activation(
                     out=env[(8 + t) % H_SLOTS][:, j0 : j0 + PASS], in_=bank_sum[:], func=ACT.Sqrt, bias=nv_last[:, t : t + 1]
                 )
@@ -234,13 +234,13 @@ def tile_list_pilot_envelope_reliability_kernel(
         gather_scales(0, S)
         for j0 in range(0, S, 256):
             gather_words(j0, 256)
-        later_parts = {0: ([1], first_sq[0][:, 256:512]), 3: ([2], sq[3][:]), 5: ([3, 4], sq[1][:]), 7: ([5, 6], sq[3][:])}
+        later_parts = {0: ([1], first_sq[0][:, 256:512]), 3: ([2], sq[3][:]), 6: ([3, 4], sq[2][:]), 8: ([5, 6], sq[0][:])}
         steps = [(0, 0, 256), (0, 256, 256), (0, 512, 512)] + [(b, j0, PASS) for b in range(1, 8) for j0 in (0, PASS)]
         for step, (b, j0, width) in enumerate(steps):
             if step == 2:
                 envelope_rows(b, j0, width, [banks[2], banks[4]], banks[6], sq[step % 4])
             else:
-                squares = first_sq[step] if step < 2 else sq[step % 4]
+                squares = first_sq[step] if step < 2 else pick[step - 8] if 9 <= step <= 11 else sq[step % 4]
                 envelope_rows(b, j0, width, banks[2 * (step % 2) : 2 * (step % 2) + 2], banks[4 + step % 2], squares)
             if b == 0:
                 scatter(0, j0, width)
@@ -255,8 +255,8 @@ def tile_list_pilot_envelope_reliability_kernel(
         gather_pass(0)
         for b in range(4, 8):
             scatter(b, 0, S)
-        for j0 in (0, PASS):
-            envelope_last_pass(j0)
+        envelope_last_pass(0, pick[4:8])
+        envelope_last_pass(PASS, sq)
         gather_pass(1)
         for b in range(8, 12):
             scatter(b, 0, S)

@@ -21,6 +21,7 @@ P = 128
 PASS = 512
 LIST_ROWS = 16
 H_SLOTS = 8
+FIRST_PIECES = ((0, 256), (256, 256), (512, 512))
 CHUNKS = ((0, 256), (256, 256), (512, 256), (768, 128), (896, 128))
 
 
@@ -51,8 +52,8 @@ def tile_list_pilot_envelope_reliability_kernel(
         wq_s = tiles("wq_s", 3, PASS, U8)
         wm_w = tile("wm_w", 3 * N, I32)
         wm_s = tile("wm_s", 3 * N, U8)
-        nv_first = tile("nv_first", 1, F32)
-        nv_rest = tile("nv_rest", 7, F32)
+        nv_first = tile("nv_first", 2, F32)
+        nv_rest = tile("nv_rest", 6, F32)
         nv_last = tile("nv_last", 4, F32)
         ident = tile("ident", P, F32)
         wgs_nat = tile("wgs_nat", S, F32)
@@ -62,8 +63,8 @@ def tile_list_pilot_envelope_reliability_kernel(
         env = tiles("env", H_SLOTS, S, F32)
         sq = tiles("sq", 4, 2 * PASS, F32)
         err_t = tiles("err_t", 2, 4 * M, F32)
-        pick_pair = tile("pick_pair", 2 * M, F32)
-        pick = [pick_pair[:, 0:M], pick_pair[:, M : 2 * M]] + [one[:] for one in tiles("pick", 6, M, F32)]
+        pick_three = tile("pick_three", 3 * M, F32)
+        pick = [pick_three[:, M * i : M * (i + 1)] for i in range(3)] + [one[:] for one in tiles("pick", 5, M, F32)]
         z_rows = tiles("z_rows", 2, PASS, BF16)
         stage = tile("stage", 4 * M, BF16)
         z_w = tiles("z_w", 3, M, U32)
@@ -74,8 +75,7 @@ def tile_list_pilot_envelope_reliability_kernel(
             for q in range(4):
                 nc.sync.dma_start(out=plane[32 * q : 32 * q + 4, :].bitcast(I32), in_=rows[4 * q : 4 * q + 4, :].bitcast(I32))
 
-        wq_parts = [(0, 128, pick[0][:, 0:512]), (128, 128, pick[0][:, 512:1024])]
-        wq_parts = wq_parts + [(256 * i, 256, pick[i]) for i in range(1, 6)]
+        wq_parts = [(256 * i, 256, pick[i]) for i in range(6)]
         wq_k = wq.rearrange("(p i) c -> p i c", i=4)
 
         def load_wq(part):
@@ -103,23 +103,22 @@ def tile_list_pilot_envelope_reliability_kernel(
         nc.sync.dma_start(pilots[:], offs)
         nc.sync.dma_start(slots[:], offs2)
         nc.sync.dma_start(carriers[:], offs3)
-        with nc.allow_non_contiguous_dma(reason="one noise power a partition"):
-            nc.sync.dma_start(out=nv_first[:], in_=nv[0:P].rearrange("(b p) -> p b", p=P))
-        nc.sync.dma_start(out=nv_last[:], in_=nv[2 * PASS : 3 * PASS].rearrange("(p t) -> p t", t=4))
-        load_wq(0)
         nc.sync.dma_start(out=wr_w[0][:].bitcast(I32), in_=wr_words[0][:, 0 : 2 * PASS].bitcast(I32))
         nc.sync.dma_start(out=wgs_nat[:, 0:256], in_=wgs[:, 0:256])
+        load_wq(0)
+        with nc.allow_non_contiguous_dma(reason="one noise power a partition"):
+            nc.sync.dma_start(out=nv_first[:], in_=nv[0 : 2 * P].rearrange("(b p) -> p b", p=P))
+        nc.sync.dma_start(out=nv_last[:], in_=nv[2 * PASS : 3 * PASS].rearrange("(p t) -> p t", t=4))
         load_scale_rows(tab_s, tab_scales[0])
         nc.sync.dma_start(out=tab_w[:], in_=tab_words[0].rearrange("p t i -> p (t i)").bitcast(I32))
         load_scale_rows(wr_s, wr_scales[0])
-        load_wq(1)
         nc.sync.dma_start(out=wgs_nat[:, 256:1024], in_=wgs[:, 256:1024])
+        load_wq(1)
         with nc.allow_non_contiguous_dma(reason="one noise power a partition"):
-            nc.sync.dma_start(out=nv_rest[:], in_=nv[P : 8 * P].rearrange("(b p) -> p b", p=P))
-        load_wq(2)
+            nc.sync.dma_start(out=nv_rest[:], in_=nv[2 * P : 8 * P].rearrange("(b p) -> p b", p=P))
         for a in (1, 2):
             nc.sync.dma_start(out=wr_w[a][:].bitcast(I32), in_=wr_words[0][:, 2 * PASS * a : 2 * PASS * (a + 1)].bitcast(I32))
-        for part in range(3, 7):
+        for part in range(2, 6):
             load_wq(part)
         for q in range(4):
             nc.sync.dma_start(out=wgs_four[32 * q : 32 * q + 32, :], in_=wgs.rearrange("(r t) j -> r (t j)", t=4))
@@ -173,7 +172,7 @@ def tile_list_pilot_envelope_reliability_kernel(
                 nc.scalar.activation(out=squares[:, width * n : width * (n + 1)], in_=bank[:, 0:width], func=ACT.Square)
             for i in range(width // P):
                 add_turned(bank_sum[:, P * i : P * (i + 1)], squares[:, 2 * P * i : 2 * P * i + P], squares[:, 2 * P * i + P : 2 * P * (i + 1)])
-            bias = nv_first[:, 0:1] if b == 0 else nv_rest[:, b - 1 : b]
+            bias = nv_first[:, b : b + 1] if b < 2 else nv_rest[:, b - 2 : b - 1]
             nc.scalar.activation(out=env[b % H_SLOTS][:, j0 : j0 + width], in_=bank_sum[:, 0:width], func=ACT.Sqrt, bias=bias)
 
         def envelope_last_pass(j0, squares):
@@ -232,18 +231,18 @@ def tile_list_pilot_envelope_reliability_kernel(
 
         quantise_wq([0], stage[:])
         gather_scales(0, S)
-        for j0 in range(0, S, 256):
-            gather_words(j0, 256)
-        later_parts = {0: ([1], first_sq[0][:, 256:512]), 3: ([2], sq[3][:]), 6: ([3, 4], sq[2][:]), 8: ([5, 6], sq[0][:])}
-        steps = [(0, 0, 256), (0, 256, 256), (0, 512, 512)] + [(b, j0, PASS) for b in range(1, 8) for j0 in (0, PASS)]
+        for j0, width in FIRST_PIECES:
+            gather_words(j0, width)
+        later_parts = {2: ([1], sq[2][:, 256:768]), 7: ([2, 3], sq[3][:]), 9: ([4, 5], sq[1][:])}
+        steps = [(b, j0, width) for j0, width in FIRST_PIECES for b in (0, 1)]
+        steps = steps + [(b, j0, PASS) for b in range(2, 8) for j0 in (0, PASS)]
         for step, (b, j0, width) in enumerate(steps):
-            if step == 2:
-                envelope_rows(b, j0, width, [banks[2], banks[4]], banks[6], sq[step % 4])
-            else:
-                squares = first_sq[step] if step < 2 else pick[step - 8] if 9 <= step <= 11 else sq[step % 4]
-                envelope_rows(b, j0, width, banks[2 * (step % 2) : 2 * (step % 2) + 2], banks[4 + step % 2], squares)
-            if b == 0:
-                scatter(0, j0, width)
+            squares = first_sq[step] if step < 2 else pick[step - 10] if 10 <= step < 14 else sq[step % 4]
+            product_banks = banks[4:6] if step == 4 else banks[2 * (step % 2) : 2 * (step % 2) + 2]
+            bank_sum = banks[6 + step % 2] if 2 <= step < 6 else banks[4 + step % 2]
+            envelope_rows(b, j0, width, product_banks, bank_sum, squares)
+            if b < 2:
+                scatter(b, j0, width)
             elif b < 4 and j0 > 0:
                 scatter(b, 0, S)
             if step in later_parts:
@@ -262,10 +261,10 @@ def tile_list_pilot_envelope_reliability_kernel(
             scatter(b, 0, S)
         add_errors_on_tensor(0, stage[:])
         nc.sync.dma_start(out=err_t[0][:], in_=err[2 * PASS : 3 * PASS, :].rearrange("(p t) m -> p (t m)", t=4))
-        add_errors_on_tensor(1, pick_pair[:].bitcast(BF16))
+        add_errors_on_tensor(1, pick_three[:, 128 : 128 + 2 * M].bitcast(BF16))
 
         picked = [pick[0], pick[1], pick[2], pick[3][:, 0:512], pick[3][:, 512:1024]]
-        grouped = [pick[2][:, 0:512], pick[3][:, 0:512], pick[3][:, 512:1024], pick[4][:, 0:256], pick[5][:, 0:256]]
+        grouped = [pick[2][:, 384:896], pick[3][:, 0:512], pick[3][:, 512:1024], pick[4][:, 0:256], pick[5][:, 0:256]]
         bank_sets = [banks[0:3], [banks[3], banks[6], banks[7]], banks[0:3], [banks[3], banks[6]], [banks[7], banks[0]]]
         results = [err_t[1][:, 0:1280], err_t[1][:, 1280:2560], err_t[1][:, 2560:3840], env[4][:, 0:640], env[5][:, 0:640]]
         out_n = out.rearrange("(i p) m -> p i m", p=P)
@@ -297,12 +296,10 @@ def tile_list_pilot_envelope_reliability_kernel(
             for bank, i0 in enumerate(range(0, 5, per_bank)):
                 i1 = min(5, i0 + per_bank)
                 part = results[c][:, width * i0 : width * i1]
-                on_vector = c == len(CHUNKS) - 1 and bank == 1
-                engine_copy = nc.vector.tensor_copy if on_vector else nc.scalar.copy
+                engine_copy = nc.vector.tensor_copy if c == len(CHUNKS) - 1 else nc.scalar.copy
                 engine_copy(out=part, in_=bank_sets[c][bank][:, 0 : width * (i1 - i0)])
                 if c == len(CHUNKS) - 1:
-                    queue = nc.sync if on_vector else nc.scalar
-                    queue.dma_start(out=out_n[:, i0:i1, m0 : m0 + width], in_=part.rearrange("p (i m) -> p i m", m=width))
+                    nc.sync.dma_start(out=out_n[:, i0:i1, m0 : m0 + width], in_=part.rearrange("p (i m) -> p i m", m=width))
             if c < len(CHUNKS) - 1:
                 nc.sync.dma_start(out=out_n[:, :, m0 : m0 + width], in_=results[c].rearrange("p (i m) -> p i m", i=5))
 

@@ -201,7 +201,9 @@ def tile_list_pilot_envelope_reliability_kernel(
 
         def gather_pass(a):
             for t in range(4):
-                nc.vector.tensor_copy(out=pick[4 * a + t], in_=pages[t][:].indirect(carriers[:]))
+                nc.vector.tensor_tensor(
+                    out=pick[4 * a + t], in0=pages[t][:].indirect(carriers[:]), in1=err_t[a][:, M * t : M * (t + 1)], op=ALU.add
+                )
 
         def quantise_z(a, m0, width, grouped):
             nc.vector.quantize_mx(out=z_w[a][:, m0 : m0 + width].bitcast(E4M3), scales=z_s[a][:, m0 : m0 + width], in_=grouped)
@@ -214,7 +216,7 @@ def tile_list_pilot_envelope_reliability_kernel(
                     m0 = 2 * P * pair + P * i
                     bank_sum = banks[4 + i]
                     for t in range(4):
-                        add_turned(bank_sum[:, P * t : P * (t + 1)], err_t[a][:, M * t + m0 : M * t + m0 + P], pick[4 * a + t][:, m0 : m0 + P])
+                        nc.tensor.transpose(bank_sum[:, P * t : P * (t + 1)], pick[4 * a + t][:, m0 : m0 + P], ident[:])
                     nc.scalar.copy(
                         out=z_rows[i][:].rearrange("m (u p e) -> m u p e", u=2, e=2),
                         in_=bank_sum[:].rearrange("m (p u e) -> m u p e", u=2, e=2),

@@ -20,9 +20,17 @@ ALU = mybir.AluOpType
 P = 128
 PASS = 512
 LIST_ROWS = 16
-H_SLOTS = 8
 FIRST_PIECES = ((0, 256), (256, 256), (512, 512))
+WQ_PARTS = ((0, 256), (256, 256), (512, 512), (1024, 512))
+WR_PARTS = ((0, 512), (512, 512), (1024, 512))
 CHUNKS = ((0, 256), (256, 256), (512, 256), (768, 128), (896, 128))
+PLACES = (
+    ((0, 0), (0, 256), (1, 0), (1, 256), (2, 0)),
+    ((3, 0), (3, 256), (4, 0), (4, 256), (2, 256)),
+    ((5, 0), (5, 256), (6, 0), (6, 256), (7, 0)),
+    ((0, 0), (0, 128), (0, 256), (0, 384), (7, 256)),
+    ((1, 0), (1, 128), (1, 256), (3, 0), (3, 128)),
+)
 
 
 def tile_list_pilot_envelope_reliability_kernel(
@@ -36,101 +44,99 @@ def tile_list_pilot_envelope_reliability_kernel(
         def tile(name, width, dtype):
             return sb.tile([P, width], dtype, name=name, align_bytes=64)
 
-        def tiles(name, count, width, dtype):
-            return [tile("%s%d" % (name, i), width, dtype) for i in range(count)]
+        def quarter(big, i, width=M, start=0):
+            return big[:, M * i + start : M * i + start + width]
 
         pilots = tile("pilots", S // LIST_ROWS, U16)
         slots = tile("slots", S // LIST_ROWS, U16)
         carriers = tile("carriers", M // LIST_ROWS, U16)
-        tab_w = tile("tab_w", T, I32)
+        tab_w = sb.tile([P, T], I32, name="tab_w", tag="late_page0", align_bytes=64)
         tab_s = tile("tab_s", T, U8)
         v_w = tile("v_w", S, U32)
         v_s = tile("v_s", S, U8)
-        wr_w = tiles("wr_w", 3, 2 * PASS, U8)
+        wr_w = [tile("wr_w%d" % c0, 2 * width, U8) for c0, width in WR_PARTS]
         wr_s = tile("wr_s", H, U8)
-        wq_w = tiles("wq_w", 3, PASS, U32)
-        wq_s = tiles("wq_s", 3, PASS, U8)
+        wq_w = [tile("wq_w%d" % c0, width, U32) for c0, width in WQ_PARTS]
+        wq_s = [tile("wq_s%d" % c0, width, U8) for c0, width in WQ_PARTS]
         wm_w = tile("wm_w", 3 * N, I32)
         wm_s = tile("wm_s", 3 * N, U8)
-        nv_first = tile("nv_first", 2, F32)
-        nv_rest = tile("nv_rest", 6, F32)
-        nv_last = tile("nv_last", 4, F32)
+        nv_nat = tile("nv_nat", 4, F32)
+        nv_four = [tile("nv_four%d" % a, 4, F32) for a in (1, 2)]
         ident = tile("ident", P, F32)
         wgs_nat = tile("wgs_nat", S, F32)
-        wgs_four = tile("wgs_four", 4 * S, F32)
-        pages = tiles("page", 2, T2, F32)
-        first_sq = [sb.tile([P, PASS], F32, name="first_sq%d" % i, tag="late_page%d" % i, align_bytes=64) for i in range(2)]
-        env = tiles("env", H_SLOTS, S, F32)
-        sq = tiles("sq", 4, 2 * PASS, F32)
-        err_t = tiles("err_t", 2, 4 * M, F32)
-        pick_three = tile("pick_three", 3 * M, F32)
-        pick = [pick_three[:, M * i : M * (i + 1)] for i in range(3)] + [one[:] for one in tiles("pick", 5, M, F32)]
-        z_rows = tiles("z_rows", 2, PASS, BF16)
-        stage = tile("stage", 4 * M, BF16)
-        z_w = tiles("z_w", 3, M, U32)
-        z_s = tiles("z_s", 3, M, U8)
+        wgs_four = tile("wgs_four", 5 * S, F32)
+        pages = [tile("page0", T2, F32)]
+        early = [sb.tile([P, M], F32, name="early%d" % i, tag="late_page%d" % (i + 1), align_bytes=64) for i in range(2)]
+        env_a = tile("env_a", 4 * S, F32)
+        env_b = tile("env_b", 4 * S, F32)
+        err_a = tile("err_a", 4 * M, F32)
+        err_b = tile("err_b", 4 * M, F32)
+        buf_a = tile("buf_a", 4 * M, F32)
+        buf_b = tile("buf_b", 4 * M, F32)
+        buf_c = tile("buf_c", 4 * M, F32)
+        buf_d = tile("buf_d", 2 * M, F32)
+        wq_first = tile("wq_first", 8 * P, BF16)
+        z_rows = [tile("z_rows%d" % i, PASS, BF16) for i in range(2)]
+        z_w = [tile("z_w%d" % a, M, U32) for a in range(3)]
+        z_s = [tile("z_s%d" % a, M, U8) for a in range(3)]
         banks = [ps.tile([P, PASS], F32, name="bank%d" % i) for i in range(8)]
 
         def load_scale_rows(plane, rows):
             for q in range(4):
                 nc.sync.dma_start(out=plane[32 * q : 32 * q + 4, :].bitcast(I32), in_=rows[4 * q : 4 * q + 4, :].bitcast(I32))
 
-        wq_parts = [(256 * i, 256, pick[i]) for i in range(6)]
+        wq_raw = [buf_c[:, 0:1024], buf_c[:, 1024:2048], env_b[:, 0:2048], env_b[:, 2048:4096]]
         wq_k = wq.rearrange("(p i) c -> p i c", i=4)
 
         def load_wq(part):
-            c0, width, raw = wq_parts[part]
-            nc.sync.dma_start(out=raw.rearrange("p (i c) -> p i c", i=4), in_=wq_k[:, :, c0 : c0 + width])
+            c0, width = WQ_PARTS[part]
+            nc.sync.dma_start(out=wq_raw[part].rearrange("p (i c) -> p i c", i=4), in_=wq_k[:, :, c0 : c0 + width])
+
+        def load_wr(part):
+            c0, width = WR_PARTS[part]
+            nc.sync.dma_start(out=wr_w[part][:].bitcast(I32), in_=wr_words[0][:, 2 * c0 : 2 * (c0 + width)].bitcast(I32))
 
         def interleave(engine_copy, dst, src):
             engine_copy(out=dst.rearrange("p (c x i) -> p c i x", x=4, i=4), in_=src.rearrange("p (i c x) -> p c i x", i=4, x=4))
 
-        def quantise_wq(parts, rounded):
-            first = wq_parts[parts[0]][0]
-            total = 0
-            for part in parts:
-                c0, width, raw = wq_parts[part]
-                interleave(nc.scalar.copy, rounded[:, 4 * (c0 - first) : 4 * (c0 - first + width)], raw)
-                total = total + width
-            a, c = divmod(first, PASS)
-            nc.vector.quantize_mx(out=wq_w[a][:, c : c + total].bitcast(E4M3), scales=wq_s[a][:, c : c + total], in_=rounded[:, 0 : 4 * total])
+        def quantise_wq(part, rounded):
+            interleave(nc.scalar.copy, rounded, wq_raw[part])
+            nc.vector.quantize_mx(out=wq_w[part][:].bitcast(E4M3), scales=wq_s[part][:], in_=rounded)
 
         warm = tile("warm", 2, F32)
-        nc.vector.memset(tab_s[:].bitcast(I32), 0)
-        nc.gpsimd.memset(wr_s[:].bitcast(I32), 0)
         nc.vector.memset(warm[:, 0:1], 1.0)
+        nc.vector.memset(wr_s[:].bitcast(I32), 0)
         nc.scalar.activation(out=warm[:, 1:2], in_=warm[:, 0:1], func=ACT.Sqrt)
         nc.sync.dma_start(pilots[:], offs)
-        nc.sync.dma_start(slots[:], offs2)
-        nc.sync.dma_start(carriers[:], offs3)
-        nc.sync.dma_start(out=wr_w[0][:].bitcast(I32), in_=wr_words[0][:, 0 : 2 * PASS].bitcast(I32))
-        nc.sync.dma_start(out=wgs_nat[:, 0:256], in_=wgs[:, 0:256])
+        for q in range(4):
+            nc.sync.dma_start(
+                out=tab_s[32 * q : 32 * q + 32, :].bitcast(I32),
+                in_=tab_scales[0][4 * q : 4 * q + 4, :].bitcast(I32).partition_broadcast(8),
+            )
         load_wq(0)
-        with nc.allow_non_contiguous_dma(reason="one noise power a partition"):
-            nc.sync.dma_start(out=nv_first[:], in_=nv[0 : 2 * P].rearrange("(b p) -> p b", p=P))
-        nc.sync.dma_start(out=nv_last[:], in_=nv[2 * PASS : 3 * PASS].rearrange("(p t) -> p t", t=4))
-        load_scale_rows(tab_s, tab_scales[0])
+        load_wr(0)
         nc.sync.dma_start(out=tab_w[:], in_=tab_words[0].rearrange("p t i -> p (t i)").bitcast(I32))
         load_scale_rows(wr_s, wr_scales[0])
-        nc.sync.dma_start(out=wgs_nat[:, 256:1024], in_=wgs[:, 256:1024])
-        load_wq(1)
         with nc.allow_non_contiguous_dma(reason="one noise power a partition"):
-            nc.sync.dma_start(out=nv_rest[:], in_=nv[2 * P : 8 * P].rearrange("(b p) -> p b", p=P))
+            nc.sync.dma_start(out=nv_nat[:], in_=nv[0:PASS].rearrange("(b p) -> p b", p=P))
+        nc.sync.dma_start(out=wgs_nat[:, 0:256], in_=wgs[:, 0:256])
+        nc.sync.dma_start(slots[:], offs2)
+        load_wq(1)
+        nc.sync.dma_start(out=wgs_nat[:, 256:1024], in_=wgs[:, 256:1024])
+        load_wq(2)
+        nc.sync.dma_start(carriers[:], offs3)
+        nc.sync.dma_start(out=err_a[:].rearrange("p (t m) -> p t m", t=4), in_=err[0:PASS, :].rearrange("(t p) m -> p t m", p=P))
+        load_wr(1)
         for a in (1, 2):
-            nc.sync.dma_start(out=wr_w[a][:].bitcast(I32), in_=wr_words[0][:, 2 * PASS * a : 2 * PASS * (a + 1)].bitcast(I32))
-        for part in range(2, 6):
-            load_wq(part)
+            nc.sync.dma_start(out=nv_four[a - 1][:], in_=nv[PASS * a : PASS * (a + 1)].rearrange("(p t) -> p t", t=4))
+        load_wq(3)
         for q in range(4):
-            nc.sync.dma_start(out=wgs_four[32 * q : 32 * q + 32, :], in_=wgs.rearrange("(r t) j -> r (t j)", t=4))
-        for a in (0, 1):
-            nc.sync.dma_start(
-                out=err_t[a][:].rearrange("p (t m) -> p t m", t=4),
-                in_=err[PASS * a : PASS * (a + 1), :].rearrange("(t p) m -> p t m", p=P),
-            )
+            nc.sync.dma_start(out=wgs_four[32 * q : 32 * q + 32, 0 : 4 * S], in_=wgs.rearrange("(r t) j -> r (t j)", t=4))
+        load_wr(2)
+        nc.sync.dma_start(out=err_b[:], in_=err[PASS : 2 * PASS, :].rearrange("(p t) m -> p (t m)", t=4))
         nc.sync.dma_start(out=wm_w[:].rearrange("p (a c) -> p a c", a=3), in_=wm_words.rearrange("a p c i -> p a (c i)").bitcast(I32))
         make_identity(nc, ident[:])
-        for page in pages:
-            nc.vector.memset(page[:], 0.0)
+        nc.vector.memset(pages[0][:], 0.0)
         nc.gpsimd.memset(wm_s[:].bitcast(I32), 0)
         for q in range(4):
             nc.sync.dma_start(
@@ -141,23 +147,22 @@ def tile_list_pilot_envelope_reliability_kernel(
         def entries(lst, j0, width):
             return lst[:, j0 // LIST_ROWS : (j0 + width) // LIST_ROWS]
 
-        def gather_words(j0, width):
-            nc.vector.tensor_copy(out=v_w[:, j0 : j0 + width], in_=tab_w[:].bitcast(U32).indirect(entries(pilots, j0, width)))
-
-        def gather_scales(j0, width):
-            nc.vector.tensor_copy(out=v_s[:, j0 : j0 + width], in_=tab_s[:].indirect(entries(pilots, j0, width)))
+        def columns(parts, c0):
+            part = max(i for i in range(len(parts)) if parts[i][0] <= c0)
+            return part, c0 - parts[part][0]
 
         def first_products(out_re, out_im, j0, c0, width):
-            a, c = divmod(c0, PASS)
             lhs = v_w[:, j0 : j0 + P].bitcast(E4M3)
             lhs_s = v_s[:, j0 : j0 + P]
+            part, c = columns(WQ_PARTS, c0)
             nc.tensor.matmul_mx(
                 out=out_im, lhsT=lhs, lhsT_scale=lhs_s,
-                rhs=wq_w[a][:, c : c + width].bitcast(E4M3), rhs_scale=wq_s[a][:, c : c + width], start=True, stop=True,
+                rhs=wq_w[part][:, c : c + width].bitcast(E4M3), rhs_scale=wq_s[part][:, c : c + width], start=True, stop=True,
             )
+            part, c = columns(WR_PARTS, c0)
             nc.tensor.matmul_mx(
                 out=out_re, lhsT=lhs, lhsT_scale=lhs_s,
-                rhs=wr_w[a][:, 2 * c : 2 * (c + width)].bitcast(E2M1), rhs_scale=wr_s[:, c0 : c0 + width], start=True, stop=True,
+                rhs=wr_w[part][:, 2 * c : 2 * (c + width)].bitcast(E2M1), rhs_scale=wr_s[:, c0 : c0 + width], start=True, stop=True,
             )
 
         def add_turned(dst, first, second):
@@ -172,54 +177,54 @@ def tile_list_pilot_envelope_reliability_kernel(
                 nc.scalar.activation(out=squares[:, width * n : width * (n + 1)], in_=bank[:, 0:width], func=ACT.Square)
             for i in range(width // P):
                 add_turned(bank_sum[:, P * i : P * (i + 1)], squares[:, 2 * P * i : 2 * P * i + P], squares[:, 2 * P * i + P : 2 * P * (i + 1)])
-            bias = nv_first[:, b : b + 1] if b < 2 else nv_rest[:, b - 2 : b - 1]
-            nc.scalar.activation(out=env[b % H_SLOTS][:, j0 : j0 + width], in_=bank_sum[:, 0:width], func=ACT.Sqrt, bias=bias)
+            nc.scalar.activation(out=quarter(env_a, b, width, j0), in_=bank_sum[:, 0:width], func=ACT.Sqrt, bias=nv_nat[:, b : b + 1])
 
-        def envelope_last_pass(j0, squares):
+        def squares_of_pass(a, j0, view):
             for i in range(4):
                 bank_re, bank_im = banks[2 * (i % 2)], banks[2 * (i % 2) + 1]
-                first_products(bank_re[:], bank_im[:], j0 + P * i, 2 * PASS, PASS)
+                first_products(bank_re[:], bank_im[:], j0 + P * i, PASS * a, PASS)
                 for half, bank in enumerate((bank_re, bank_im)):
-                    nc.scalar.activation(
-                        out=squares[i][:, PASS * half : PASS * (half + 1)].rearrange("j (t p) -> j t p", t=4),
-                        in_=bank[:].rearrange("j (p t) -> j t p", t=4), func=ACT.Square,
-                    )
-            for t in range(4):
-                bank_sum = banks[4 + t % 2]
-                for i in range(4):
-                    add_turned(bank_sum[:, P * i : P * (i + 1)], squares[i][:, P * t : P * (t + 1)], squares[i][:, PASS + P * t : PASS + P * (t + 1)])
-                nc.scalar.activation(
-                    out=env[(8 + t) % H_SLOTS][:, j0 : j0 + PASS], in_=bank_sum[:], func=ACT.Sqrt, bias=nv_last[:, t : t + 1]
-                )
+                    nc.scalar.activation(out=view[:, i, half, :, :], in_=bank[:].rearrange("j (p t) -> j t p", t=4), func=ACT.Square)
 
-        def scatter(b, j0, width):
-            t = b % 4
-            weights = wgs_nat[:, j0 : j0 + width] if b < 8 else wgs_four[:, S * t + j0 : S * t + j0 + width]
+        def sum_of_squares(t, view):
+            for i in range(4):
+                add_turned(banks[4 + t % 2][:, P * i : P * (i + 1)], view[:, i, 0, t, :], view[:, i, 1, t, :])
+
+        def root(a, t, dst):
+            nc.scalar.activation(out=dst, in_=banks[4 + t % 2][:], func=ACT.Sqrt, bias=nv_four[a - 1][:, t : t + 1])
+
+        def by_pilots(buf):
+            return buf[:].rearrange("j (i h t p) -> j i h t p", i=4, h=2, t=4)
+
+        def by_rows(buf):
+            return buf[:].rearrange("j (t i h p) -> j i h t p", i=4, h=2, t=4)
+
+        def scatter(t, j0, width, values, weights):
+            nc.vector.tensor_tensor(out=pages[t][:].indirect(entries(slots, j0, width)), in0=values, in1=weights, op=ALU.mult)
+
+        def scatter_four(t, j0, values):
+            scatter(t, j0, PASS, values, quarter(wgs_four, t, PASS, j0))
+
+        def gather(t, m0, width, dst, errors):
             nc.vector.tensor_tensor(
-                out=pages[t][:].indirect(entries(slots, j0, width)), in0=env[b % H_SLOTS][:, j0 : j0 + width], in1=weights, op=ALU.mult
+                out=dst, in0=pages[t][:].indirect(entries(carriers, m0, width)), in1=quarter(errors, t, width, m0), op=ALU.add
             )
-
-        def gather_pass(a):
-            for t in range(4):
-                nc.vector.tensor_tensor(
-                    out=pick[4 * a + t], in0=pages[t][:].indirect(carriers[:]), in1=err_t[a][:, M * t : M * (t + 1)], op=ALU.add
-                )
 
         def quantise_z(a, m0, width, grouped):
             nc.vector.quantize_mx(out=z_w[a][:, m0 : m0 + width].bitcast(E4M3), scales=z_s[a][:, m0 : m0 + width], in_=grouped)
 
-        def add_errors_on_tensor(a, grouped):
+        def turn_first_pass(z_nat, grouped):
             words = grouped.bitcast(F32)
             for pair in range(4):
                 bank_back = banks[6 + pair % 2]
                 for i in range(2):
                     m0 = 2 * P * pair + P * i
-                    bank_sum = banks[4 + i]
+                    bank_in = banks[4 + i]
                     for t in range(4):
-                        nc.tensor.transpose(bank_sum[:, P * t : P * (t + 1)], pick[4 * a + t][:, m0 : m0 + P], ident[:])
+                        nc.tensor.transpose(bank_in[:, P * t : P * (t + 1)], z_nat[t][:, m0 : m0 + P], ident[:])
                     nc.scalar.copy(
                         out=z_rows[i][:].rearrange("m (u p e) -> m u p e", u=2, e=2),
-                        in_=bank_sum[:].rearrange("m (p u e) -> m u p e", u=2, e=2),
+                        in_=bank_in[:].rearrange("m (p u e) -> m u p e", u=2, e=2),
                     )
                     for u in range(2):
                         nc.tensor.transpose(
@@ -229,86 +234,151 @@ def tile_list_pilot_envelope_reliability_kernel(
                     out=words[:, PASS * pair : PASS * (pair + 1)].rearrange("p (i m u) -> p i m u", i=2, u=2),
                     in_=bank_back[:].rearrange("p (i u m) -> p i m u", i=2, u=2),
                 )
-            quantise_z(a, 0, M, grouped)
+            quantise_z(0, 0, M, grouped)
 
-        quantise_wq([0], stage[:])
-        gather_scales(0, S)
+        def late_page(i):
+            page = sb.tile([P, T2], F32, name="page%d" % (1 + i), tag="late_page%d" % i, align_bytes=64)
+            nc.gpsimd.memset(page[:], 0.0)
+            pages.append(page)
+
+        nc.vector.tensor_copy(out=v_s[:], in_=tab_s[:].indirect(pilots[:]))
+        quantise_wq(0, wq_first[:])
         for j0, width in FIRST_PIECES:
-            gather_words(j0, width)
-        later_parts = {2: ([1], sq[2][:, 256:768]), 7: ([2, 3], sq[3][:]), 9: ([4, 5], sq[1][:])}
-        steps = [(b, j0, width) for j0, width in FIRST_PIECES for b in (0, 1)]
-        steps = steps + [(b, j0, PASS) for b in range(2, 8) for j0 in (0, PASS)]
+            nc.vector.tensor_copy(out=v_w[:, j0 : j0 + width], in_=tab_w[:].bitcast(U32).indirect(entries(pilots, j0, width)))
+        late_page(0)
+        steps = [(0, j0, width) for j0, width in FIRST_PIECES] + [(b, j0, PASS) for b in range(1, 4) for j0 in (0, PASS)]
+        squares = [
+            quarter(buf_b, 0), early[0][:], quarter(buf_b, 2), early[1][:], quarter(buf_b, 3),
+            quarter(buf_d, 0), quarter(buf_b, 1), quarter(buf_d, 1), quarter(buf_b, 2),
+        ]
+        z_nat = [quarter(buf_d, 0), quarter(buf_d, 1), quarter(buf_a, 0), quarter(buf_a, 1)]
         for step, (b, j0, width) in enumerate(steps):
-            squares = first_sq[step] if step < 2 else pick[step - 10] if 10 <= step < 14 else sq[step % 4]
-            product_banks = banks[4:6] if step == 4 else banks[2 * (step % 2) : 2 * (step % 2) + 2]
-            bank_sum = banks[6 + step % 2] if 2 <= step < 6 else banks[4 + step % 2]
-            envelope_rows(b, j0, width, product_banks, bank_sum, squares)
-            if b < 2:
-                scatter(b, j0, width)
-            elif b < 4 and j0 > 0:
-                scatter(b, 0, S)
-            if step in later_parts:
-                quantise_wq(later_parts[step][0], later_parts[step][1].bitcast(BF16))
-            if step < 2:
-                late_page = sb.tile([P, T2], F32, name="page%d" % (2 + step), tag="late_page%d" % step, align_bytes=64)
-                nc.gpsimd.memset(late_page[:], 0.0)
-                pages.append(late_page)
-        gather_pass(0)
-        for b in range(4, 8):
-            scatter(b, 0, S)
-        envelope_last_pass(0, pick[4:8])
-        envelope_last_pass(PASS, sq)
-        gather_pass(1)
-        for b in range(8, 12):
-            scatter(b, 0, S)
-        add_errors_on_tensor(0, stage[:])
-        nc.sync.dma_start(out=err_t[0][:], in_=err[2 * PASS : 3 * PASS, :].rearrange("(p t) m -> p (t m)", t=4))
-        add_errors_on_tensor(1, pick_three[:, 128 : 128 + 2 * M].bitcast(BF16))
+            envelope_rows(b, j0, width, banks[2 * (step % 2) : 2 * (step % 2) + 2], banks[4 + step % 2], squares[step])
+            scatter(b, j0, width, quarter(env_a, b, width, j0), wgs_nat[:, j0 : j0 + width])
+            if step == 2:
+                quantise_wq(1, squares[1][:, 0:512].bitcast(BF16))
+                late_page(1)
+            if step == 4:
+                quantise_wq(2, squares[3].bitcast(BF16))
+                late_page(2)
+            if step == 6:
+                quantise_wq(3, squares[6].bitcast(BF16))
+            if step in (5, 7):
+                gather(b - 2, 0, M, z_nat[b - 2], err_a)
 
-        picked = [pick[0], pick[1], pick[2], pick[3][:, 0:512], pick[3][:, 512:1024]]
-        grouped = [pick[2][:, 384:896], pick[3][:, 0:512], pick[3][:, 512:1024], pick[4][:, 0:256], pick[5][:, 0:256]]
-        bank_sets = [banks[0:3], [banks[3], banks[6], banks[7]], banks[0:3], [banks[3], banks[6]], [banks[7], banks[0]]]
-        results = [err_t[1][:, 0:1280], err_t[1][:, 1280:2560], err_t[1][:, 2560:3840], env[4][:, 0:640], env[5][:, 0:640]]
-        out_n = out.rearrange("(i p) m -> p i m", p=P)
-
-        def gather_chunk(c):
-            m0, width = CHUNKS[c]
+        for half, buf in enumerate((buf_a, buf_b)):
+            view = by_pilots(buf)
+            squares_of_pass(1, PASS * half, view)
             for t in range(4):
-                nc.vector.tensor_tensor(
-                    out=picked[c][:, width * t : width * (t + 1)], in0=pages[t][:].indirect(entries(carriers, m0, width)),
-                    in1=err_t[0][:, M * t + m0 : M * t + m0 + width], op=ALU.add,
-                )
+                sum_of_squares(t, view)
+                root(1, t, quarter(env_b, t, PASS, PASS * half))
+            for t in range(4):
+                if half == 0 and t == 2:
+                    gather(2, 0, M, z_nat[2], err_a)
+                    gather(3, 0, M, z_nat[3], err_a)
+                scatter_four(t, PASS * half, quarter(env_b, t, PASS, PASS * half))
+        for t in range(4):
+            gather(t, 0, M, quarter(buf_b, t), err_b)
+        nc.sync.dma_start(out=err_a[:], in_=err[2 * PASS : 3 * PASS, :].rearrange("(p t) m -> p (t m)", t=4))
+
+        view = by_pilots(buf_c)
+        squares_of_pass(2, 0, view)
+        for t in range(4):
+            sum_of_squares(t, view)
+            if t < 3:
+                root(2, t, quarter(env_a, t, PASS))
+                scatter_four(t, 0, quarter(env_a, t, PASS))
+            else:
+                root(2, t, quarter(wgs_four, 4, PASS))
+        turn_first_pass(z_nat, buf_a[:, 2 * M : 4 * M].bitcast(BF16))
+        view = by_rows(buf_c)
+        squares_of_pass(2, PASS, view)
+        for t in range(2):
+            sum_of_squares(t, view)
+        grouped_1 = buf_c[:, 0 : 2 * M].bitcast(BF16)
+        interleave(nc.scalar.copy, grouped_1, buf_b[:])
+        quantise_z(1, 0, M, grouped_1)
+        for t in range(4):
+            if t >= 2:
+                sum_of_squares(t, view)
+            if t < 3:
+                root(2, t, quarter(buf_b, t, PASS))
+                scatter_four(t, PASS, quarter(buf_b, t, PASS))
+            else:
+                root(2, t, quarter(wgs_four, 4, PASS, PASS))
+                scatter(t, 0, S, quarter(wgs_four, 4), quarter(wgs_four, 3))
+
+        picked = [quarter(wgs_four, 3, M, PASS), quarter(wgs_four, 3), quarter(wgs_four, 3, M, PASS), quarter(wgs_four, 3, PASS), quarter(wgs_four, 3, PASS, PASS)]
+        grouped = [buf_a[:, 2 * M + 2 * m0 : 2 * M + 2 * (m0 + width)].bitcast(BF16) for m0, width in CHUNKS]
+        out_n = out.rearrange("(i p) m -> p i m", p=P)
+        open_banks = []
+
+        def products(c, tiles_i, passes, closing):
+            m0, width = CHUNKS[c]
+            for a in passes:
+                for i in tiles_i:
+                    bank, col = PLACES[c][i]
+                    start = bank not in open_banks
+                    if start:
+                        open_banks.append(bank)
+                    stop = a == 2 and i in closing
+                    if stop:
+                        open_banks.remove(bank)
+                    nc.tensor.matmul_mx(
+                        out=banks[bank][:, col : col + width],
+                        lhsT=wm_w[:, N * a + P * i : N * a + P * (i + 1)].bitcast(E4M3), lhsT_scale=wm_s[:, N * a + P * i : N * a + P * (i + 1)],
+                        rhs=z_w[a][:, m0 : m0 + width].bitcast(E4M3), rhs_scale=z_s[a][:, m0 : m0 + width], start=start, stop=stop,
+                    )
+
+        def store(engine_copy, bank, staged, i0, count, m0, width):
+            engine_copy(out=staged, in_=banks[bank][:, 0 : count * width])
+            nc.sync.dma_start(out=out_n[:, i0 : i0 + count, m0 : m0 + width], in_=staged.rearrange("p (i m) -> p i m", i=count))
+
+        def gather_chunk(c, row_tiles):
+            m0, width = CHUNKS[c]
+            for t in row_tiles:
+                gather(t, m0, width, picked[c][:, width * t : width * (t + 1)], err_a)
+
+        def last_pass(c, closing):
+            m0, width = CHUNKS[c]
+            quantise_z(2, m0, width, grouped[c])
+            products(c, range(5), (2,), closing)
 
         def round_chunk(c, engine_copy):
-            interleave(engine_copy, grouped[c].bitcast(BF16), picked[c])
+            interleave(engine_copy, grouped[c], picked[c])
 
-        def finish_chunk(c):
-            m0, width = CHUNKS[c]
-            quantise_z(2, m0, width, grouped[c].bitcast(BF16))
-            per_bank = 2 if width == 256 else 3
-            for a in (1, 0, 2):
-                for i in range(5):
-                    bank, place = divmod(i, per_bank)
-                    nc.tensor.matmul_mx(
-                        out=bank_sets[c][bank][:, width * place : width * (place + 1)],
-                        lhsT=wm_w[:, N * a + P * i : N * a + P * (i + 1)].bitcast(E4M3), lhsT_scale=wm_s[:, N * a + P * i : N * a + P * (i + 1)],
-                        rhs=z_w[a][:, m0 : m0 + width].bitcast(E4M3), rhs_scale=z_s[a][:, m0 : m0 + width],
-                        start=(a == 1 and place == 0), stop=(a == 2 and (place == per_bank - 1 or i == 4)),
-                    )
-            for bank, i0 in enumerate(range(0, 5, per_bank)):
-                i1 = min(5, i0 + per_bank)
-                part = results[c][:, width * i0 : width * i1]
-                engine_copy = nc.vector.tensor_copy if c == len(CHUNKS) - 1 else nc.scalar.copy
-                engine_copy(out=part, in_=bank_sets[c][bank][:, 0 : width * (i1 - i0)])
-                if c == len(CHUNKS) - 1:
-                    nc.sync.dma_start(out=out_n[:, i0:i1, m0 : m0 + width], in_=part.rearrange("p (i m) -> p i m", m=width))
-            if c < len(CHUNKS) - 1:
-                nc.sync.dma_start(out=out_n[:, :, m0 : m0 + width], in_=results[c].rearrange("p (i m) -> p i m", i=5))
-
-        last = len(CHUNKS) - 1
-        for c in range(len(CHUNKS)):
-            gather_chunk(c)
-            if c > 0:
-                finish_chunk(c - 1)
-            round_chunk(c, nc.vector.tensor_copy if c == last else nc.scalar.copy)
-        finish_chunk(last)
+        staged = [err_b[:, PASS * n : PASS * (n + 1)] for n in range(8)] + [buf_d[:, PASS * n : PASS * (n + 1)] for n in range(4)]
+        for c in range(3):
+            products(c, range(5), (0, 1), ())
+        products(3, (4,), (0, 1), ())
+        gather_chunk(0, range(4))
+        round_chunk(0, nc.scalar.copy)
+        gather_chunk(1, (0, 1))
+        last_pass(0, (1, 3))
+        store(nc.scalar.copy, 0, staged[0], 0, 2, 0, 256)
+        gather_chunk(1, (2, 3))
+        round_chunk(1, nc.scalar.copy)
+        store(nc.scalar.copy, 1, staged[1], 2, 2, 0, 256)
+        products(3, range(4), (0, 1), ())
+        products(4, range(3), (0, 1), ())
+        gather_chunk(2, (2, 3))
+        last_pass(1, (1, 3, 4))
+        store(nc.scalar.copy, 3, staged[2], 0, 2, 256, 256)
+        gather_chunk(2, (0, 1))
+        round_chunk(2, nc.scalar.copy)
+        store(nc.scalar.copy, 4, staged[3], 2, 2, 256, 256)
+        products(4, (3, 4), (0, 1), ())
+        gather_chunk(3, range(4))
+        round_chunk(3, nc.scalar.copy)
+        store(nc.scalar.copy, 2, staged[4], 4, 1, 0, PASS)
+        last_pass(2, (1, 3))
+        gather_chunk(4, range(4))
+        store(nc.scalar.copy, 5, staged[5], 0, 2, 512, 256)
+        store(nc.scalar.copy, 6, staged[6], 2, 2, 512, 256)
+        last_pass(3, (3, 4))
+        round_chunk(4, nc.vector.tensor_copy)
+        last_pass(4, (2, 4))
+        store(nc.vector.tensor_copy, 0, staged[7], 0, 4, 768, 128)
+        store(nc.scalar.copy, 7, staged[8][:, 0:384], 4, 1, 512, 384)
+        store(nc.scalar.copy, 1, staged[9][:, 0:384], 0, 3, 896, 128)
+        store(nc.vector.tensor_copy, 3, staged[10][:, 0:256], 3, 2, 896, 128)

@@ -21,8 +21,8 @@ P = 128
 PASS = 512
 LIST_ROWS = 16
 FIRST_PIECES = ((0, 256), (256, 256), (512, 512))
-WQ_PARTS = ((0, 256), (256, 256), (512, 512), (1024, 512))
-WR_PARTS = ((0, 512), (512, 512), (1024, 512))
+WQ_PARTS = ((0, 128), (128, 128), (256, 256), (512, 512), (1024, 512))
+WR_PARTS = ((0, 128), (128, 384), (512, 512), (1024, 512))
 CHUNKS = ((0, 256), (256, 256), (512, 256), (768, 128), (896, 128))
 PLACES = (
     ((0, 0), (0, 256), (1, 0), (1, 256), (2, 0)),
@@ -65,17 +65,18 @@ def tile_list_pilot_envelope_reliability_kernel(
         ident = tile("ident", P, F32)
         wgs_nat = tile("wgs_nat", S, F32)
         wgs_four = tile("wgs_four", 5 * S, F32)
-        pages = [tile("page0", T2, F32)]
-        early = [sb.tile([P, M], F32, name="early%d" % i, tag="late_page%d" % (i + 1), align_bytes=64) for i in range(2)]
+        pages = [tile("page%d" % i, T2, F32) for i in range(2)]
+        early = [tile("early0", PASS, F32), tile("early1", M, F32), sb.tile([P, M], F32, name="early2", tag="late_page1", align_bytes=64)]
         env_a = tile("env_a", 4 * S, F32)
         env_b = tile("env_b", 4 * S, F32)
         err_a = tile("err_a", 4 * M, F32)
         err_b = tile("err_b", 4 * M, F32)
         buf_a = tile("buf_a", 4 * M, F32)
-        buf_b = tile("buf_b", 4 * M, F32)
+        buf_b_long = tile("buf_b_long", PASS + 4 * M, F32)
+        buf_b = buf_b_long[:, PASS : PASS + 4 * M]
         buf_c = tile("buf_c", 4 * M, F32)
         buf_d = tile("buf_d", 2 * M, F32)
-        wq_first = tile("wq_first", 8 * P, BF16)
+        wq_first = tile("wq_first", 4 * P, BF16)
         z_rows = [tile("z_rows%d" % i, PASS, BF16) for i in range(2)]
         z_w = [tile("z_w%d" % a, M, U32) for a in range(3)]
         z_s = [tile("z_s%d" % a, M, U8) for a in range(3)]
@@ -85,7 +86,7 @@ def tile_list_pilot_envelope_reliability_kernel(
             for q in range(4):
                 nc.sync.dma_start(out=plane[32 * q : 32 * q + 4, :].bitcast(I32), in_=rows[4 * q : 4 * q + 4, :].bitcast(I32))
 
-        wq_raw = [buf_c[:, 0:1024], buf_c[:, 1024:2048], env_b[:, 0:2048], env_b[:, 2048:4096]]
+        wq_raw = [buf_c[:, 0:512], buf_c[:, 512:1024], buf_c[:, 1024:2048], env_b[:, 0:2048], env_b[:, 2048:4096]]
         wq_k = wq.rearrange("(p i) c -> p i c", i=4)
 
         def load_wq(part):
@@ -119,24 +120,27 @@ def tile_list_pilot_envelope_reliability_kernel(
         load_scale_rows(wr_s, wr_scales[0])
         with nc.allow_non_contiguous_dma(reason="one noise power a partition"):
             nc.sync.dma_start(out=nv_nat[:], in_=nv[0:PASS].rearrange("(b p) -> p b", p=P))
+        load_wq(1)
         nc.sync.dma_start(out=wgs_nat[:, 0:256], in_=wgs[:, 0:256])
         nc.sync.dma_start(slots[:], offs2)
-        load_wq(1)
         nc.sync.dma_start(out=wgs_nat[:, 256:1024], in_=wgs[:, 256:1024])
         load_wq(2)
+        load_wr(1)
+        load_wq(3)
         nc.sync.dma_start(carriers[:], offs3)
         nc.sync.dma_start(out=err_a[:].rearrange("p (t m) -> p t m", t=4), in_=err[0:PASS, :].rearrange("(t p) m -> p t m", p=P))
-        load_wr(1)
+        load_wr(2)
         for a in (1, 2):
             nc.sync.dma_start(out=nv_four[a - 1][:], in_=nv[PASS * a : PASS * (a + 1)].rearrange("(p t) -> p t", t=4))
-        load_wq(3)
+        load_wq(4)
         for q in range(4):
             nc.sync.dma_start(out=wgs_four[32 * q : 32 * q + 32, 0 : 4 * S], in_=wgs.rearrange("(r t) j -> r (t j)", t=4))
-        load_wr(2)
+        load_wr(3)
         nc.sync.dma_start(out=err_b[:], in_=err[PASS : 2 * PASS, :].rearrange("(p t) m -> p (t m)", t=4))
         nc.sync.dma_start(out=wm_w[:].rearrange("p (a c) -> p a c", a=3), in_=wm_words.rearrange("a p c i -> p a (c i)").bitcast(I32))
         make_identity(nc, ident[:])
-        nc.vector.memset(pages[0][:], 0.0)
+        for page in pages:
+            nc.vector.memset(page[:], 0.0)
         nc.gpsimd.memset(wm_s[:].bitcast(I32), 0)
         for q in range(4):
             nc.sync.dma_start(
@@ -194,16 +198,16 @@ def tile_list_pilot_envelope_reliability_kernel(
             nc.scalar.activation(out=dst, in_=banks[4 + t % 2][:], func=ACT.Sqrt, bias=nv_four[a - 1][:, t : t + 1])
 
         def by_pilots(buf):
-            return buf[:].rearrange("j (i h t p) -> j i h t p", i=4, h=2, t=4)
+            return buf.rearrange("j (i h t p) -> j i h t p", i=4, h=2, t=4)
 
         def by_rows(buf):
-            return buf[:].rearrange("j (t i h p) -> j i h t p", i=4, h=2, t=4)
+            return buf.rearrange("j (t i h p) -> j i h t p", i=4, h=2, t=4)
 
         def scatter(t, j0, width, values, weights):
             nc.vector.tensor_tensor(out=pages[t][:].indirect(entries(slots, j0, width)), in0=values, in1=weights, op=ALU.mult)
 
-        def scatter_four(t, j0, values):
-            scatter(t, j0, PASS, values, quarter(wgs_four, t, PASS, j0))
+        def scatter_four(t, values):
+            scatter(t, 0, S, values, quarter(wgs_four, t))
 
         def gather(t, m0, width, dst, errors):
             nc.vector.tensor_tensor(
@@ -237,8 +241,8 @@ def tile_list_pilot_envelope_reliability_kernel(
             quantise_z(0, 0, M, grouped)
 
         def late_page(i):
-            page = sb.tile([P, T2], F32, name="page%d" % (1 + i), tag="late_page%d" % i, align_bytes=64)
-            nc.gpsimd.memset(page[:], 0.0)
+            page = sb.tile([P, T2], F32, name="page%d" % (2 + i), tag="late_page%d" % i, align_bytes=64)
+            nc.vector.memset(page[:], 0.0)
             pages.append(page)
 
         nc.vector.tensor_copy(out=v_s[:], in_=tab_s[:].indirect(pilots[:]))
@@ -248,65 +252,60 @@ def tile_list_pilot_envelope_reliability_kernel(
         late_page(0)
         steps = [(0, j0, width) for j0, width in FIRST_PIECES] + [(b, j0, PASS) for b in range(1, 4) for j0 in (0, PASS)]
         squares = [
-            quarter(buf_b, 0), early[0][:], quarter(buf_b, 2), early[1][:], quarter(buf_b, 3),
+            quarter(buf_b, 0), early[0][:], early[2][:], early[1][:], quarter(buf_b, 3),
             quarter(buf_d, 0), quarter(buf_b, 1), quarter(buf_d, 1), quarter(buf_b, 2),
         ]
         z_nat = [quarter(buf_d, 0), quarter(buf_d, 1), quarter(buf_a, 0), quarter(buf_a, 1)]
         for step, (b, j0, width) in enumerate(steps):
             envelope_rows(b, j0, width, banks[2 * (step % 2) : 2 * (step % 2) + 2], banks[4 + step % 2], squares[step])
-            scatter(b, j0, width, quarter(env_a, b, width, j0), wgs_nat[:, j0 : j0 + width])
+            if b < 2:
+                scatter(b, j0, width, quarter(env_a, b, width, j0), wgs_nat[:, j0 : j0 + width])
+            elif j0 > 0:
+                scatter(b, 0, S, quarter(env_a, b), wgs_nat[:])
+            if step == 0:
+                quantise_wq(1, squares[0][:, 0:256].bitcast(BF16))
             if step == 2:
-                quantise_wq(1, squares[1][:, 0:512].bitcast(BF16))
+                quantise_wq(2, squares[1][:, 0:512].bitcast(BF16))
                 late_page(1)
             if step == 4:
-                quantise_wq(2, squares[3].bitcast(BF16))
-                late_page(2)
+                quantise_wq(3, squares[3].bitcast(BF16))
             if step == 6:
-                quantise_wq(3, squares[6].bitcast(BF16))
+                quantise_wq(4, squares[6].bitcast(BF16))
             if step in (5, 7):
                 gather(b - 2, 0, M, z_nat[b - 2], err_a)
 
-        for half, buf in enumerate((buf_a, buf_b)):
+        for half, buf in enumerate((buf_a[:], buf_b)):
             view = by_pilots(buf)
             squares_of_pass(1, PASS * half, view)
             for t in range(4):
                 sum_of_squares(t, view)
                 root(1, t, quarter(env_b, t, PASS, PASS * half))
-            for t in range(4):
-                if half == 0 and t == 2:
-                    gather(2, 0, M, z_nat[2], err_a)
-                    gather(3, 0, M, z_nat[3], err_a)
-                scatter_four(t, PASS * half, quarter(env_b, t, PASS, PASS * half))
+                if half == 1:
+                    scatter_four(t, quarter(env_b, t))
+            if half == 0:
+                gather(2, 0, M, z_nat[2], err_a)
+                gather(3, 0, M, z_nat[3], err_a)
         for t in range(4):
             gather(t, 0, M, quarter(buf_b, t), err_b)
         nc.sync.dma_start(out=err_a[:], in_=err[2 * PASS : 3 * PASS, :].rearrange("(p t) m -> p (t m)", t=4))
 
-        view = by_pilots(buf_c)
+        env_last = [quarter(env_a, 0), quarter(env_a, 1), buf_b_long[:, 0:S], quarter(wgs_four, 4)]
+        view = by_pilots(buf_c[:])
         squares_of_pass(2, 0, view)
         for t in range(4):
             sum_of_squares(t, view)
-            if t < 3:
-                root(2, t, quarter(env_a, t, PASS))
-                scatter_four(t, 0, quarter(env_a, t, PASS))
-            else:
-                root(2, t, quarter(wgs_four, 4, PASS))
+            root(2, t, env_last[t][:, 0:PASS])
         turn_first_pass(z_nat, buf_a[:, 2 * M : 4 * M].bitcast(BF16))
-        view = by_rows(buf_c)
+        view = by_rows(buf_c[:])
         squares_of_pass(2, PASS, view)
-        for t in range(2):
-            sum_of_squares(t, view)
         grouped_1 = buf_c[:, 0 : 2 * M].bitcast(BF16)
-        interleave(nc.scalar.copy, grouped_1, buf_b[:])
-        quantise_z(1, 0, M, grouped_1)
         for t in range(4):
-            if t >= 2:
-                sum_of_squares(t, view)
-            if t < 3:
-                root(2, t, quarter(buf_b, t, PASS))
-                scatter_four(t, PASS, quarter(buf_b, t, PASS))
-            else:
-                root(2, t, quarter(wgs_four, 4, PASS, PASS))
-                scatter(t, 0, S, quarter(wgs_four, 4), quarter(wgs_four, 3))
+            if t == 2:
+                interleave(nc.scalar.copy, grouped_1, buf_b)
+                quantise_z(1, 0, M, grouped_1)
+            sum_of_squares(t, view)
+            root(2, t, env_last[t][:, PASS:S])
+            scatter_four(t, env_last[t])
 
         picked = [quarter(wgs_four, 3, M, PASS), quarter(wgs_four, 3), quarter(wgs_four, 3, M, PASS), quarter(wgs_four, 3, PASS), quarter(wgs_four, 3, PASS, PASS)]
         grouped = [buf_a[:, 2 * M + 2 * m0 : 2 * M + 2 * (m0 + width)].bitcast(BF16) for m0, width in CHUNKS]

@@ -50,7 +50,7 @@ def tile_list_pilot_envelope_reliability_kernel(
         pilots = tile("pilots", S // LIST_ROWS, U16)
         slots = tile("slots", S // LIST_ROWS, U16)
         carriers = tile("carriers", M // LIST_ROWS, U16)
-        tab_w = sb.tile([P, T], I32, name="tab_w", tag="late_page0", align_bytes=64)
+        tab_w = sb.tile([P, T], I32, name="tab_w", tag="words_then_page", align_bytes=64)
         tab_s = tile("tab_s", T, U8)
         v_w = tile("v_w", S, U32)
         v_s = tile("v_s", S, U8)
@@ -60,13 +60,14 @@ def tile_list_pilot_envelope_reliability_kernel(
         wq_s = [tile("wq_s%d" % c0, width, U8) for c0, width in WQ_PARTS]
         wm_w = tile("wm_w", 3 * N, I32)
         wm_s = tile("wm_s", 3 * N, U8)
-        nv_nat = tile("nv_nat", 4, F32)
+        nv_first = tile("nv_first", 1, F32)
+        nv_nat = tile("nv_nat", 3, F32)
         nv_four = [tile("nv_four%d" % a, 4, F32) for a in (1, 2)]
         ident = tile("ident", P, F32)
         wgs_nat = tile("wgs_nat", S, F32)
-        wgs_four = tile("wgs_four", 5 * S, F32)
-        pages = [tile("page%d" % i, T2, F32) for i in range(2)]
-        early = [tile("early0", PASS, F32), tile("early1", M, F32), sb.tile([P, M], F32, name="early2", tag="late_page1", align_bytes=64)]
+        wgs_four = tile("wgs_four", 4 * S, F32)
+        pages = [tile("page0", T2, F32)]
+        early = [tile("early0", PASS, F32), tile("early1", M, F32)]
         env_a = tile("env_a", 4 * S, F32)
         env_b = tile("env_b", 4 * S, F32)
         err_a = tile("err_a", 4 * M, F32)
@@ -75,7 +76,7 @@ def tile_list_pilot_envelope_reliability_kernel(
         buf_b_long = tile("buf_b_long", PASS + 4 * M, F32)
         buf_b = buf_b_long[:, PASS : PASS + 4 * M]
         buf_c = tile("buf_c", 4 * M, F32)
-        buf_d = tile("buf_d", 2 * M, F32)
+        buf_d = tile("buf_d", 4 * M, F32)
         wq_first = tile("wq_first", 4 * P, BF16)
         z_rows = [tile("z_rows%d" % i, PASS, BF16) for i in range(2)]
         z_w = [tile("z_w%d" % a, M, U32) for a in range(3)]
@@ -86,7 +87,7 @@ def tile_list_pilot_envelope_reliability_kernel(
             for q in range(4):
                 nc.sync.dma_start(out=plane[32 * q : 32 * q + 4, :].bitcast(I32), in_=rows[4 * q : 4 * q + 4, :].bitcast(I32))
 
-        wq_raw = [buf_c[:, 0:512], buf_c[:, 512:1024], buf_c[:, 1024:2048], env_b[:, 0:2048], env_b[:, 2048:4096]]
+        wq_raw = [buf_c[:, 0:512], buf_c[:, 512:1024], buf_c[:, 1024:2048], buf_d[:, 0:2048], buf_d[:, 2048:4096]]
         wq_k = wq.rearrange("(p i) c -> p i c", i=4)
 
         def load_wq(part):
@@ -119,13 +120,15 @@ def tile_list_pilot_envelope_reliability_kernel(
         nc.sync.dma_start(out=tab_w[:], in_=tab_words[0].rearrange("p t i -> p (t i)").bitcast(I32))
         load_scale_rows(wr_s, wr_scales[0])
         with nc.allow_non_contiguous_dma(reason="one noise power a partition"):
-            nc.sync.dma_start(out=nv_nat[:], in_=nv[0:PASS].rearrange("(b p) -> p b", p=P))
+            nc.sync.dma_start(out=nv_first[:], in_=nv[0:P].rearrange("(b p) -> p b", p=P))
+        nc.sync.dma_start(slots[:], offs2)
         load_wq(1)
         nc.sync.dma_start(out=wgs_nat[:, 0:256], in_=wgs[:, 0:256])
-        nc.sync.dma_start(slots[:], offs2)
         nc.sync.dma_start(out=wgs_nat[:, 256:1024], in_=wgs[:, 256:1024])
         load_wq(2)
         load_wr(1)
+        with nc.allow_non_contiguous_dma(reason="one noise power a partition"):
+            nc.sync.dma_start(out=nv_nat[:], in_=nv[P:PASS].rearrange("(b p) -> p b", p=P))
         load_wq(3)
         nc.sync.dma_start(carriers[:], offs3)
         nc.sync.dma_start(out=err_a[:].rearrange("p (t m) -> p t m", t=4), in_=err[0:PASS, :].rearrange("(t p) m -> p t m", p=P))
@@ -134,13 +137,12 @@ def tile_list_pilot_envelope_reliability_kernel(
             nc.sync.dma_start(out=nv_four[a - 1][:], in_=nv[PASS * a : PASS * (a + 1)].rearrange("(p t) -> p t", t=4))
         load_wq(4)
         for q in range(4):
-            nc.sync.dma_start(out=wgs_four[32 * q : 32 * q + 32, 0 : 4 * S], in_=wgs.rearrange("(r t) j -> r (t j)", t=4))
+            nc.sync.dma_start(out=wgs_four[32 * q : 32 * q + 32, :], in_=wgs.rearrange("(r t) j -> r (t j)", t=4))
         load_wr(3)
         nc.sync.dma_start(out=err_b[:], in_=err[PASS : 2 * PASS, :].rearrange("(p t) m -> p (t m)", t=4))
         nc.sync.dma_start(out=wm_w[:].rearrange("p (a c) -> p a c", a=3), in_=wm_words.rearrange("a p c i -> p a (c i)").bitcast(I32))
         make_identity(nc, ident[:])
-        for page in pages:
-            nc.vector.memset(page[:], 0.0)
+        nc.vector.memset(pages[0][:].bitcast(I32), 0)
         nc.gpsimd.memset(wm_s[:].bitcast(I32), 0)
         for q in range(4):
             nc.sync.dma_start(
@@ -181,7 +183,7 @@ def tile_list_pilot_envelope_reliability_kernel(
                 nc.scalar.activation(out=squares[:, width * n : width * (n + 1)], in_=bank[:, 0:width], func=ACT.Square)
             for i in range(width // P):
                 add_turned(bank_sum[:, P * i : P * (i + 1)], squares[:, 2 * P * i : 2 * P * i + P], squares[:, 2 * P * i + P : 2 * P * (i + 1)])
-            nc.scalar.activation(out=quarter(env_a, b, width, j0), in_=bank_sum[:, 0:width], func=ACT.Sqrt, bias=nv_nat[:, b : b + 1])
+            nc.scalar.activation(out=quarter(env_a, b, width, j0), in_=bank_sum[:, 0:width], func=ACT.Sqrt, bias=nv_first[:] if b == 0 else nv_nat[:, b - 1 : b])
 
         def squares_of_pass(a, j0, view):
             for i in range(4):
@@ -204,14 +206,14 @@ def tile_list_pilot_envelope_reliability_kernel(
             return buf.rearrange("j (t i h p) -> j i h t p", i=4, h=2, t=4)
 
         def scatter(t, j0, width, values, weights):
-            nc.vector.tensor_tensor(out=pages[t][:].indirect(entries(slots, j0, width)), in0=values, in1=weights, op=ALU.mult)
+            nc.vector.tensor_tensor(out=pages[t % 2][:].indirect(entries(slots, j0, width)), in0=values, in1=weights, op=ALU.mult)
 
         def scatter_four(t, values):
             scatter(t, 0, S, values, quarter(wgs_four, t))
 
         def gather(t, m0, width, dst, errors):
             nc.vector.tensor_tensor(
-                out=dst, in0=pages[t][:].indirect(entries(carriers, m0, width)), in1=quarter(errors, t, width, m0), op=ALU.add
+                out=dst, in0=pages[t % 2][:].indirect(entries(carriers, m0, width)), in1=quarter(errors, t, width, m0), op=ALU.add
             )
 
         def quantise_z(a, m0, width, grouped):
@@ -240,24 +242,23 @@ def tile_list_pilot_envelope_reliability_kernel(
                 )
             quantise_z(0, 0, M, grouped)
 
-        def late_page(i):
-            page = sb.tile([P, T2], F32, name="page%d" % (2 + i), tag="late_page%d" % i, align_bytes=64)
-            nc.vector.memset(page[:], 0.0)
-            pages.append(page)
-
         nc.vector.tensor_copy(out=v_s[:], in_=tab_s[:].indirect(pilots[:]))
         quantise_wq(0, wq_first[:])
         for j0, width in FIRST_PIECES:
             nc.vector.tensor_copy(out=v_w[:, j0 : j0 + width], in_=tab_w[:].bitcast(U32).indirect(entries(pilots, j0, width)))
-        late_page(0)
+        pages.append(sb.tile([P, T2], F32, name="page1", tag="words_then_page", align_bytes=64))
+        nc.vector.memset(pages[1][:].bitcast(I32), 0)
         steps = [(0, j0, width) for j0, width in FIRST_PIECES] + [(b, j0, PASS) for b in range(1, 4) for j0 in (0, PASS)]
         squares = [
-            quarter(buf_b, 0), early[0][:], early[2][:], early[1][:], quarter(buf_b, 3),
-            quarter(buf_d, 0), quarter(buf_b, 1), quarter(buf_d, 1), quarter(buf_b, 2),
+            quarter(buf_b, 0), early[0][:], quarter(buf_b, 2), quarter(buf_b, 3), early[1][:],
+            quarter(buf_b, 1), quarter(buf_b, 0), quarter(buf_b, 2), quarter(buf_c, 3),
         ]
-        z_nat = [quarter(buf_d, 0), quarter(buf_d, 1), quarter(buf_a, 0), quarter(buf_a, 1)]
+        z_nat = [quarter(buf_d, t) for t in range(4)]
         for step, (b, j0, width) in enumerate(steps):
-            envelope_rows(b, j0, width, banks[2 * (step % 2) : 2 * (step % 2) + 2], banks[4 + step % 2], squares[step])
+            if step == 2:
+                envelope_rows(b, j0, width, [banks[4], banks[1]], banks[6], squares[step])
+            else:
+                envelope_rows(b, j0, width, banks[2 * (step % 2) : 2 * (step % 2) + 2], banks[4 + step % 2], squares[step])
             if b < 2:
                 scatter(b, j0, width, quarter(env_a, b, width, j0), wgs_nat[:, j0 : j0 + width])
             elif j0 > 0:
@@ -266,13 +267,13 @@ def tile_list_pilot_envelope_reliability_kernel(
                 quantise_wq(1, squares[0][:, 0:256].bitcast(BF16))
             if step == 2:
                 quantise_wq(2, squares[1][:, 0:512].bitcast(BF16))
-                late_page(1)
             if step == 4:
-                quantise_wq(3, squares[3].bitcast(BF16))
-            if step == 6:
-                quantise_wq(4, squares[6].bitcast(BF16))
-            if step in (5, 7):
-                gather(b - 2, 0, M, z_nat[b - 2], err_a)
+                quantise_wq(3, squares[4].bitcast(BF16))
+            if step == 8:
+                quantise_wq(4, squares[8].bitcast(BF16))
+            if step in (4, 8):
+                gather(b - 1, 0, M, z_nat[b - 1], err_a)
+                gather(b, 0, M, z_nat[b], err_a)
 
         for half, buf in enumerate((buf_a[:], buf_b)):
             view = by_pilots(buf)
@@ -280,16 +281,14 @@ def tile_list_pilot_envelope_reliability_kernel(
             for t in range(4):
                 sum_of_squares(t, view)
                 root(1, t, quarter(env_b, t, PASS, PASS * half))
-                if half == 1:
-                    scatter_four(t, quarter(env_b, t))
-            if half == 0:
-                gather(2, 0, M, z_nat[2], err_a)
-                gather(3, 0, M, z_nat[3], err_a)
-        for t in range(4):
-            gather(t, 0, M, quarter(buf_b, t), err_b)
+        for pair in ((0, 1), (2, 3)):
+            for t in pair:
+                scatter_four(t, quarter(env_b, t))
+            for t in pair:
+                gather(t, 0, M, quarter(buf_b, t), err_b)
         nc.sync.dma_start(out=err_a[:], in_=err[2 * PASS : 3 * PASS, :].rearrange("(p t) m -> p (t m)", t=4))
 
-        env_last = [quarter(env_a, 0), quarter(env_a, 1), buf_b_long[:, 0:S], quarter(wgs_four, 4)]
+        env_last = [quarter(env_a, 0), quarter(env_a, 1), buf_b_long[:, 0:S], quarter(env_a, 3)]
         view = by_pilots(buf_c[:])
         squares_of_pass(2, 0, view)
         for t in range(4):
@@ -301,13 +300,15 @@ def tile_list_pilot_envelope_reliability_kernel(
         grouped_1 = buf_c[:, 0 : 2 * M].bitcast(BF16)
         for t in range(4):
             if t == 2:
+                gather(0, 0, M, quarter(env_b, 0), err_a)
+                gather(1, 0, M, quarter(env_b, 1), err_a)
                 interleave(nc.scalar.copy, grouped_1, buf_b)
                 quantise_z(1, 0, M, grouped_1)
             sum_of_squares(t, view)
             root(2, t, env_last[t][:, PASS:S])
             scatter_four(t, env_last[t])
 
-        picked = [quarter(wgs_four, 3, M, PASS), quarter(wgs_four, 3), quarter(wgs_four, 3, M, PASS), quarter(wgs_four, 3, PASS), quarter(wgs_four, 3, PASS, PASS)]
+        places = (0, 256, 0, 256, 384)
         grouped = [buf_a[:, 2 * M + 2 * m0 : 2 * M + 2 * (m0 + width)].bitcast(BF16) for m0, width in CHUNKS]
         out_n = out.rearrange("(i p) m -> p i m", p=P)
         open_banks = []
@@ -333,10 +334,10 @@ def tile_list_pilot_envelope_reliability_kernel(
             engine_copy(out=staged, in_=banks[bank][:, 0 : count * width])
             nc.sync.dma_start(out=out_n[:, i0 : i0 + count, m0 : m0 + width], in_=staged.rearrange("p (i m) -> p i m", i=count))
 
-        def gather_chunk(c, row_tiles):
+        def gather_chunk(c):
             m0, width = CHUNKS[c]
-            for t in row_tiles:
-                gather(t, m0, width, picked[c][:, width * t : width * (t + 1)], err_a)
+            for t in (2, 3):
+                gather(t, m0, width, quarter(env_b, t, width, places[c]), err_a)
 
         def last_pass(c, closing):
             m0, width = CHUNKS[c]
@@ -344,39 +345,45 @@ def tile_list_pilot_envelope_reliability_kernel(
             products(c, range(5), (2,), closing)
 
         def round_chunk(c, engine_copy):
-            interleave(engine_copy, grouped[c], picked[c])
+            m0, width = CHUNKS[c]
+            if places[c] == m0:
+                src = env_b[:].rearrange("p (i j m) -> p i j m", i=2, j=2)[:, :, :, m0 : m0 + width]
+            else:
+                span = 2 * M + places[c] - m0
+                src = env_b[:, m0 : m0 + 2 * span].rearrange("p (i g y) -> p i g y", i=2, y=width)[:, :, 0 : M // width + 1 : M // width, :]
+            engine_copy(
+                out=grouped[c].rearrange("p (c x i j) -> p c i j x", x=4, i=2, j=2), in_=src.rearrange("p i j (c x) -> p c i j x", x=4)
+            )
 
         staged = [err_b[:, PASS * n : PASS * (n + 1)] for n in range(8)] + [buf_d[:, PASS * n : PASS * (n + 1)] for n in range(4)]
         for c in range(3):
             products(c, range(5), (0, 1), ())
         products(3, (4,), (0, 1), ())
-        gather_chunk(0, range(4))
+        gather_chunk(0)
         round_chunk(0, nc.scalar.copy)
-        gather_chunk(1, (0, 1))
+        gather_chunk(1)
+        round_chunk(1, nc.scalar.copy)
         last_pass(0, (1, 3))
         store(nc.scalar.copy, 0, staged[0], 0, 2, 0, 256)
-        gather_chunk(1, (2, 3))
-        round_chunk(1, nc.scalar.copy)
+        gather_chunk(2)
+        round_chunk(2, nc.scalar.copy)
+        last_pass(1, (1, 3, 4))
         store(nc.scalar.copy, 1, staged[1], 2, 2, 0, 256)
         products(3, range(4), (0, 1), ())
         products(4, range(3), (0, 1), ())
-        gather_chunk(2, (2, 3))
-        last_pass(1, (1, 3, 4))
         store(nc.scalar.copy, 3, staged[2], 0, 2, 256, 256)
-        gather_chunk(2, (0, 1))
-        round_chunk(2, nc.scalar.copy)
-        store(nc.scalar.copy, 4, staged[3], 2, 2, 256, 256)
         products(4, (3, 4), (0, 1), ())
-        gather_chunk(3, range(4))
-        round_chunk(3, nc.scalar.copy)
-        store(nc.scalar.copy, 2, staged[4], 4, 1, 0, PASS)
+        gather_chunk(3)
+        gather_chunk(4)
         last_pass(2, (1, 3))
-        gather_chunk(4, range(4))
-        store(nc.scalar.copy, 5, staged[5], 0, 2, 512, 256)
-        store(nc.scalar.copy, 6, staged[6], 2, 2, 512, 256)
-        last_pass(3, (3, 4))
+        round_chunk(3, nc.vector.tensor_copy)
         round_chunk(4, nc.vector.tensor_copy)
+        last_pass(3, (3, 4))
         last_pass(4, (2, 4))
+        store(nc.scalar.copy, 4, staged[3], 2, 2, 256, 256)
+        store(nc.scalar.copy, 2, staged[4], 4, 1, 0, PASS)
+        store(nc.scalar.copy, 5, staged[5], 0, 2, 512, 256)
+        store(nc.vector.tensor_copy, 6, staged[6], 2, 2, 512, 256)
         store(nc.vector.tensor_copy, 0, staged[7], 0, 4, 768, 128)
         store(nc.scalar.copy, 7, staged[8][:, 0:384], 4, 1, 512, 384)
         store(nc.scalar.copy, 1, staged[9][:, 0:384], 0, 3, 896, 128)

@@ -65,9 +65,9 @@ def tile_list_pilot_envelope_reliability_kernel(
         nv_four = [tile("nv_four%d" % a, 4, F32) for a in (1, 2)]
         ident = tile("ident", P, F32)
         wgs_nat = tile("wgs_nat", S, F32)
-        wgs_four = tile("wgs_four", 4 * S, F32)
+        wgs_four = tile("wgs_four", 5 * S, F32)
         pages = [tile("page0", T2, F32)]
-        early = [tile("early0", PASS, F32), tile("early1", M, F32)]
+        early = [sb.tile([P, M], F32, name="early%d" % i, tag="early_then_page%d" % i, align_bytes=64) for i in range(2)]
         env_a = tile("env_a", 4 * S, F32)
         env_b = tile("env_b", 4 * S, F32)
         err_a = tile("err_a", 4 * M, F32)
@@ -137,7 +137,7 @@ def tile_list_pilot_envelope_reliability_kernel(
             nc.sync.dma_start(out=nv_four[a - 1][:], in_=nv[PASS * a : PASS * (a + 1)].rearrange("(p t) -> p t", t=4))
         load_wq(4)
         for q in range(4):
-            nc.sync.dma_start(out=wgs_four[32 * q : 32 * q + 32, :], in_=wgs.rearrange("(r t) j -> r (t j)", t=4))
+            nc.sync.dma_start(out=wgs_four[32 * q : 32 * q + 32, 0 : 4 * S], in_=wgs.rearrange("(r t) j -> r (t j)", t=4))
         load_wr(3)
         nc.sync.dma_start(out=err_b[:], in_=err[PASS : 2 * PASS, :].rearrange("(p t) m -> p (t m)", t=4))
         nc.sync.dma_start(out=wm_w[:].rearrange("p (a c) -> p a c", a=3), in_=wm_words.rearrange("a p c i -> p a (c i)").bitcast(I32))
@@ -205,15 +205,15 @@ def tile_list_pilot_envelope_reliability_kernel(
         def by_rows(buf):
             return buf.rearrange("j (t i h p) -> j i h t p", i=4, h=2, t=4)
 
-        def scatter(t, j0, width, values, weights):
-            nc.vector.tensor_tensor(out=pages[t % 2][:].indirect(entries(slots, j0, width)), in0=values, in1=weights, op=ALU.mult)
+        def scatter(page, j0, width, values, weights):
+            nc.vector.tensor_tensor(out=pages[page][:].indirect(entries(slots, j0, width)), in0=values, in1=weights, op=ALU.mult)
 
-        def scatter_four(t, values):
-            scatter(t, 0, S, values, quarter(wgs_four, t))
+        def scatter_four(page, t, values):
+            scatter(page, 0, S, values, quarter(wgs_four, t))
 
-        def gather(t, m0, width, dst, errors):
+        def gather(page, t, m0, width, dst, errors):
             nc.vector.tensor_tensor(
-                out=dst, in0=pages[t % 2][:].indirect(entries(carriers, m0, width)), in1=quarter(errors, t, width, m0), op=ALU.add
+                out=dst, in0=pages[page][:].indirect(entries(carriers, m0, width)), in1=quarter(errors, t, width, m0), op=ALU.add
             )
 
         def quantise_z(a, m0, width, grouped):
@@ -242,12 +242,16 @@ def tile_list_pilot_envelope_reliability_kernel(
                 )
             quantise_z(0, 0, M, grouped)
 
+        def late_page(tag):
+            page = sb.tile([P, T2], F32, name="page%d" % len(pages), tag=tag, align_bytes=64)
+            nc.gpsimd.memset(page[:], 0.0)
+            pages.append(page)
+
         nc.vector.tensor_copy(out=v_s[:], in_=tab_s[:].indirect(pilots[:]))
         quantise_wq(0, wq_first[:])
         for j0, width in FIRST_PIECES:
             nc.vector.tensor_copy(out=v_w[:, j0 : j0 + width], in_=tab_w[:].bitcast(U32).indirect(entries(pilots, j0, width)))
-        pages.append(sb.tile([P, T2], F32, name="page1", tag="words_then_page", align_bytes=64))
-        nc.vector.memset(pages[1][:].bitcast(I32), 0)
+        late_page("words_then_page")
         steps = [(0, j0, width) for j0, width in FIRST_PIECES] + [(b, j0, PASS) for b in range(1, 4) for j0 in (0, PASS)]
         squares = [
             quarter(buf_b, 0), early[0][:], quarter(buf_b, 2), quarter(buf_b, 3), early[1][:],
@@ -262,18 +266,20 @@ def tile_list_pilot_envelope_reliability_kernel(
             if b < 2:
                 scatter(b, j0, width, quarter(env_a, b, width, j0), wgs_nat[:, j0 : j0 + width])
             elif j0 > 0:
-                scatter(b, 0, S, quarter(env_a, b), wgs_nat[:])
+                scatter(b % 2, 0, S, quarter(env_a, b), wgs_nat[:])
             if step == 0:
                 quantise_wq(1, squares[0][:, 0:256].bitcast(BF16))
             if step == 2:
                 quantise_wq(2, squares[1][:, 0:512].bitcast(BF16))
+                late_page("early_then_page0")
             if step == 4:
                 quantise_wq(3, squares[4].bitcast(BF16))
+                late_page("early_then_page1")
             if step == 8:
                 quantise_wq(4, squares[8].bitcast(BF16))
             if step in (4, 8):
-                gather(b - 1, 0, M, z_nat[b - 1], err_a)
-                gather(b, 0, M, z_nat[b], err_a)
+                gather(0, b - 1, 0, M, z_nat[b - 1], err_a)
+                gather(1, b, 0, M, z_nat[b], err_a)
 
         for half, buf in enumerate((buf_a[:], buf_b)):
             view = by_pilots(buf)
@@ -283,12 +289,12 @@ def tile_list_pilot_envelope_reliability_kernel(
                 root(1, t, quarter(env_b, t, PASS, PASS * half))
         for pair in ((0, 1), (2, 3)):
             for t in pair:
-                scatter_four(t, quarter(env_b, t))
+                scatter_four(t % 2, t, quarter(env_b, t))
             for t in pair:
-                gather(t, 0, M, quarter(buf_b, t), err_b)
+                gather(t % 2, t, 0, M, quarter(buf_b, t), err_b)
         nc.sync.dma_start(out=err_a[:], in_=err[2 * PASS : 3 * PASS, :].rearrange("(p t) m -> p (t m)", t=4))
 
-        env_last = [quarter(env_a, 0), quarter(env_a, 1), buf_b_long[:, 0:S], quarter(env_a, 3)]
+        env_last = [quarter(env_a, 0), quarter(env_a, 1), buf_b_long[:, 0:S], quarter(wgs_four, 4)]
         view = by_pilots(buf_c[:])
         squares_of_pass(2, 0, view)
         for t in range(4):
@@ -300,15 +306,13 @@ def tile_list_pilot_envelope_reliability_kernel(
         grouped_1 = buf_c[:, 0 : 2 * M].bitcast(BF16)
         for t in range(4):
             if t == 2:
-                gather(0, 0, M, quarter(env_b, 0), err_a)
-                gather(1, 0, M, quarter(env_b, 1), err_a)
                 interleave(nc.scalar.copy, grouped_1, buf_b)
                 quantise_z(1, 0, M, grouped_1)
             sum_of_squares(t, view)
             root(2, t, env_last[t][:, PASS:S])
-            scatter_four(t, env_last[t])
+            scatter_four(t, t, env_last[t])
 
-        places = (0, 256, 0, 256, 384)
+        picked = [quarter(wgs_four, 3, M, 768), quarter(wgs_four, 3), quarter(wgs_four, 3, M, 768), quarter(wgs_four, 3, PASS), quarter(wgs_four, 3, PASS, 768)]
         grouped = [buf_a[:, 2 * M + 2 * m0 : 2 * M + 2 * (m0 + width)].bitcast(BF16) for m0, width in CHUNKS]
         out_n = out.rearrange("(i p) m -> p i m", p=P)
         open_banks = []
@@ -334,10 +338,10 @@ def tile_list_pilot_envelope_reliability_kernel(
             engine_copy(out=staged, in_=banks[bank][:, 0 : count * width])
             nc.sync.dma_start(out=out_n[:, i0 : i0 + count, m0 : m0 + width], in_=staged.rearrange("p (i m) -> p i m", i=count))
 
-        def gather_chunk(c):
+        def gather_chunk(c, row_tiles):
             m0, width = CHUNKS[c]
-            for t in (2, 3):
-                gather(t, m0, width, quarter(env_b, t, width, places[c]), err_a)
+            for t in row_tiles:
+                gather(t, t, m0, width, picked[c][:, width * t : width * (t + 1)], err_a)
 
         def last_pass(c, closing):
             m0, width = CHUNKS[c]
@@ -345,45 +349,39 @@ def tile_list_pilot_envelope_reliability_kernel(
             products(c, range(5), (2,), closing)
 
         def round_chunk(c, engine_copy):
-            m0, width = CHUNKS[c]
-            if places[c] == m0:
-                src = env_b[:].rearrange("p (i j m) -> p i j m", i=2, j=2)[:, :, :, m0 : m0 + width]
-            else:
-                span = 2 * M + places[c] - m0
-                src = env_b[:, m0 : m0 + 2 * span].rearrange("p (i g y) -> p i g y", i=2, y=width)[:, :, 0 : M // width + 1 : M // width, :]
-            engine_copy(
-                out=grouped[c].rearrange("p (c x i j) -> p c i j x", x=4, i=2, j=2), in_=src.rearrange("p i j (c x) -> p c i j x", x=4)
-            )
+            interleave(engine_copy, grouped[c], picked[c])
 
         staged = [err_b[:, PASS * n : PASS * (n + 1)] for n in range(8)] + [buf_d[:, PASS * n : PASS * (n + 1)] for n in range(4)]
         for c in range(3):
             products(c, range(5), (0, 1), ())
         products(3, (4,), (0, 1), ())
-        gather_chunk(0)
+        gather_chunk(0, range(4))
         round_chunk(0, nc.scalar.copy)
-        gather_chunk(1)
-        round_chunk(1, nc.scalar.copy)
+        gather_chunk(1, (0, 1, 2))
         last_pass(0, (1, 3))
         store(nc.scalar.copy, 0, staged[0], 0, 2, 0, 256)
-        gather_chunk(2)
-        round_chunk(2, nc.scalar.copy)
-        last_pass(1, (1, 3, 4))
+        gather_chunk(1, (3,))
+        round_chunk(1, nc.scalar.copy)
         store(nc.scalar.copy, 1, staged[1], 2, 2, 0, 256)
         products(3, range(4), (0, 1), ())
         products(4, range(3), (0, 1), ())
+        gather_chunk(2, (1, 2, 3))
+        last_pass(1, (1, 3, 4))
         store(nc.scalar.copy, 3, staged[2], 0, 2, 256, 256)
-        products(4, (3, 4), (0, 1), ())
-        gather_chunk(3)
-        gather_chunk(4)
-        last_pass(2, (1, 3))
-        round_chunk(3, nc.vector.tensor_copy)
-        round_chunk(4, nc.vector.tensor_copy)
-        last_pass(3, (3, 4))
-        last_pass(4, (2, 4))
+        gather_chunk(2, (0,))
+        round_chunk(2, nc.scalar.copy)
         store(nc.scalar.copy, 4, staged[3], 2, 2, 256, 256)
+        products(4, (3, 4), (0, 1), ())
+        gather_chunk(3, range(4))
+        round_chunk(3, nc.scalar.copy)
         store(nc.scalar.copy, 2, staged[4], 4, 1, 0, PASS)
+        last_pass(2, (1, 3))
+        gather_chunk(4, range(4))
         store(nc.scalar.copy, 5, staged[5], 0, 2, 512, 256)
-        store(nc.vector.tensor_copy, 6, staged[6], 2, 2, 512, 256)
+        store(nc.scalar.copy, 6, staged[6], 2, 2, 512, 256)
+        last_pass(3, (3, 4))
+        round_chunk(4, nc.vector.tensor_copy)
+        last_pass(4, (2, 4))
         store(nc.vector.tensor_copy, 0, staged[7], 0, 4, 768, 128)
         store(nc.scalar.copy, 7, staged[8][:, 0:384], 4, 1, 512, 384)
         store(nc.scalar.copy, 1, staged[9][:, 0:384], 0, 3, 896, 128)

@@ -21,6 +21,7 @@ P = 128
 PASS = 512
 LIST_ROWS = 16
 FIRST_PIECES = ((0, 256), (256, 256), (512, 512))
+WQ_LOADS = ((0, 128), (128, 128), (256, 256), (512, 256), (768, 256), (1024, 512))
 WQ_PARTS = ((0, 128), (128, 128), (256, 256), (512, 512), (1024, 512))
 WR_PARTS = ((0, 128), (128, 384), (512, 512), (1024, 512))
 CHUNKS = ((0, 256), (256, 256), (512, 256), (768, 128), (896, 128))
@@ -65,7 +66,7 @@ def tile_list_pilot_envelope_reliability_kernel(
         nv_four = [tile("nv_four%d" % a, 4, F32) for a in (1, 2)]
         ident = tile("ident", P, F32)
         wgs_nat = tile("wgs_nat", S, F32)
-        wgs_four = tile("wgs_four", 5 * S, F32)
+        wgs_four = tile("wgs_four", 4 * S, F32)
         pages = [tile("page0", T2, F32)]
         early = [sb.tile([P, M], F32, name="early%d" % i, tag="early_then_page%d" % i, align_bytes=64) for i in range(2)]
         env_a = tile("env_a", 4 * S, F32)
@@ -73,11 +74,10 @@ def tile_list_pilot_envelope_reliability_kernel(
         err_a = tile("err_a", 4 * M, F32)
         err_b = tile("err_b", 4 * M, F32)
         buf_a = tile("buf_a", 4 * M, F32)
-        buf_b_long = tile("buf_b_long", PASS + 4 * M, F32)
-        buf_b = buf_b_long[:, PASS : PASS + 4 * M]
+        buf_b = tile("buf_b", 4 * M, F32)
         buf_c = tile("buf_c", 4 * M, F32)
         buf_d = tile("buf_d", 4 * M, F32)
-        wq_first = tile("wq_first", 4 * P, BF16)
+        wq_first = tile("wq_first", 8 * P, BF16)
         z_rows = [tile("z_rows%d" % i, PASS, BF16) for i in range(2)]
         z_w = [tile("z_w%d" % a, M, U32) for a in range(3)]
         z_s = [tile("z_s%d" % a, M, U8) for a in range(3)]
@@ -87,12 +87,15 @@ def tile_list_pilot_envelope_reliability_kernel(
             for q in range(4):
                 nc.sync.dma_start(out=plane[32 * q : 32 * q + 4, :].bitcast(I32), in_=rows[4 * q : 4 * q + 4, :].bitcast(I32))
 
-        wq_raw = [buf_c[:, 0:512], buf_c[:, 512:1024], buf_c[:, 1024:2048], buf_d[:, 0:2048], buf_d[:, 2048:4096]]
+        wq_raw = [
+            quarter(buf_c, 0, PASS), quarter(buf_c, 0, PASS, PASS), quarter(buf_c, 1),
+            quarter(buf_d, 0), quarter(buf_d, 1), buf_d[:, 2 * M : 4 * M],
+        ]
         wq_k = wq.rearrange("(p i) c -> p i c", i=4)
 
-        def load_wq(part):
-            c0, width = WQ_PARTS[part]
-            nc.sync.dma_start(out=wq_raw[part].rearrange("p (i c) -> p i c", i=4), in_=wq_k[:, :, c0 : c0 + width])
+        def load_wq(load):
+            c0, width = WQ_LOADS[load]
+            nc.sync.dma_start(out=wq_raw[load].rearrange("p (i c) -> p i c", i=4), in_=wq_k[:, :, c0 : c0 + width])
 
         def load_wr(part):
             c0, width = WR_PARTS[part]
@@ -101,43 +104,44 @@ def tile_list_pilot_envelope_reliability_kernel(
         def interleave(engine_copy, dst, src):
             engine_copy(out=dst.rearrange("p (c x i) -> p c i x", x=4, i=4), in_=src.rearrange("p (i c x) -> p c i x", i=4, x=4))
 
-        def quantise_wq(part, rounded):
-            interleave(nc.scalar.copy, rounded, wq_raw[part])
+        def quantise_wq(part, loads, rounded):
+            for n, load in enumerate(loads):
+                width = 4 * WQ_LOADS[load][1]
+                interleave(nc.scalar.copy, rounded[:, width * n : width * (n + 1)], wq_raw[load])
             nc.vector.quantize_mx(out=wq_w[part][:].bitcast(E4M3), scales=wq_s[part][:], in_=rounded)
 
         warm = tile("warm", 2, F32)
+        nc.gpsimd.memset(tab_s[:].bitcast(I32), 0)
         nc.vector.memset(warm[:, 0:1], 1.0)
         nc.vector.memset(wr_s[:].bitcast(I32), 0)
         nc.scalar.activation(out=warm[:, 1:2], in_=warm[:, 0:1], func=ACT.Sqrt)
         nc.sync.dma_start(pilots[:], offs)
-        for q in range(4):
-            nc.sync.dma_start(
-                out=tab_s[32 * q : 32 * q + 32, :].bitcast(I32),
-                in_=tab_scales[0][4 * q : 4 * q + 4, :].bitcast(I32).partition_broadcast(8),
-            )
+        load_scale_rows(tab_s, tab_scales[0])
         load_wq(0)
-        load_wr(0)
         nc.sync.dma_start(out=tab_w[:], in_=tab_words[0].rearrange("p t i -> p (t i)").bitcast(I32))
+        load_wr(0)
         load_scale_rows(wr_s, wr_scales[0])
+        load_wq(1)
         with nc.allow_non_contiguous_dma(reason="one noise power a partition"):
             nc.sync.dma_start(out=nv_first[:], in_=nv[0:P].rearrange("(b p) -> p b", p=P))
         nc.sync.dma_start(slots[:], offs2)
-        load_wq(1)
-        nc.sync.dma_start(out=wgs_nat[:, 0:256], in_=wgs[:, 0:256])
-        nc.sync.dma_start(out=wgs_nat[:, 256:1024], in_=wgs[:, 256:1024])
+        first_width = FIRST_PIECES[0][1]
+        nc.sync.dma_start(out=wgs_nat[:, 0:first_width], in_=wgs[:, 0:first_width])
+        nc.sync.dma_start(out=wgs_nat[:, first_width:S], in_=wgs[:, first_width:S])
         load_wq(2)
         load_wr(1)
         with nc.allow_non_contiguous_dma(reason="one noise power a partition"):
             nc.sync.dma_start(out=nv_nat[:], in_=nv[P:PASS].rearrange("(b p) -> p b", p=P))
-        load_wq(3)
+        for load in (3, 4):
+            load_wq(load)
         nc.sync.dma_start(carriers[:], offs3)
         nc.sync.dma_start(out=err_a[:].rearrange("p (t m) -> p t m", t=4), in_=err[0:PASS, :].rearrange("(t p) m -> p t m", p=P))
         load_wr(2)
         for a in (1, 2):
             nc.sync.dma_start(out=nv_four[a - 1][:], in_=nv[PASS * a : PASS * (a + 1)].rearrange("(p t) -> p t", t=4))
-        load_wq(4)
+        load_wq(5)
         for q in range(4):
-            nc.sync.dma_start(out=wgs_four[32 * q : 32 * q + 32, 0 : 4 * S], in_=wgs.rearrange("(r t) j -> r (t j)", t=4))
+            nc.sync.dma_start(out=wgs_four[32 * q : 32 * q + 32, :], in_=wgs.rearrange("(r t) j -> r (t j)", t=4))
         load_wr(3)
         nc.sync.dma_start(out=err_b[:], in_=err[PASS : 2 * PASS, :].rearrange("(p t) m -> p (t m)", t=4))
         nc.sync.dma_start(out=wm_w[:].rearrange("p (a c) -> p a c", a=3), in_=wm_words.rearrange("a p c i -> p a (c i)").bitcast(I32))
@@ -179,52 +183,47 @@ def tile_list_pilot_envelope_reliability_kernel(
             per_bank = width // (2 * P)
             for n, bank in enumerate(product_banks):
                 for i in range(per_bank):
-                    first_products(bank[:, 2 * P * i : 2 * P * i + P], bank[:, 2 * P * i + P : 2 * P * (i + 1)], j0 + P * (per_bank * n + i), P * b, P)
+                    first_products(
+                        bank[:, 2 * P * i : 2 * P * i + P], bank[:, 2 * P * i + P : 2 * P * (i + 1)], j0 + P * (per_bank * n + i), P * b, P
+                    )
                 nc.scalar.activation(out=squares[:, width * n : width * (n + 1)], in_=bank[:, 0:width], func=ACT.Square)
             for i in range(width // P):
                 add_turned(bank_sum[:, P * i : P * (i + 1)], squares[:, 2 * P * i : 2 * P * i + P], squares[:, 2 * P * i + P : 2 * P * (i + 1)])
-            nc.scalar.activation(out=quarter(env_a, b, width, j0), in_=bank_sum[:, 0:width], func=ACT.Sqrt, bias=nv_first[:] if b == 0 else nv_nat[:, b - 1 : b])
+            bias = nv_first[:] if b == 0 else nv_nat[:, b - 1 : b]
+            nc.scalar.activation(out=quarter(env_a, b, width, j0), in_=bank_sum[:, 0:width], func=ACT.Sqrt, bias=bias)
 
-        def squares_of_pass(a, j0, view):
+        def squares_of_pass(a, j0, buf):
+            view = buf[:].rearrange("j (i h t p) -> j i h t p", i=4, h=2, t=4)
             for i in range(4):
                 bank_re, bank_im = banks[2 * (i % 2)], banks[2 * (i % 2) + 1]
                 first_products(bank_re[:], bank_im[:], j0 + P * i, PASS * a, PASS)
                 for half, bank in enumerate((bank_re, bank_im)):
                     nc.scalar.activation(out=view[:, i, half, :, :], in_=bank[:].rearrange("j (p t) -> j t p", t=4), func=ACT.Square)
+            return view
 
-        def sum_of_squares(t, view):
+        def envelope_four(a, t, view, dst):
+            bank_sum = banks[4 + t % 2]
             for i in range(4):
-                add_turned(banks[4 + t % 2][:, P * i : P * (i + 1)], view[:, i, 0, t, :], view[:, i, 1, t, :])
-
-        def root(a, t, dst):
-            nc.scalar.activation(out=dst, in_=banks[4 + t % 2][:], func=ACT.Sqrt, bias=nv_four[a - 1][:, t : t + 1])
-
-        def by_pilots(buf):
-            return buf.rearrange("j (i h t p) -> j i h t p", i=4, h=2, t=4)
-
-        def by_rows(buf):
-            return buf.rearrange("j (t i h p) -> j i h t p", i=4, h=2, t=4)
+                add_turned(bank_sum[:, P * i : P * (i + 1)], view[:, i, 0, t, :], view[:, i, 1, t, :])
+            nc.scalar.activation(out=dst, in_=bank_sum[:], func=ACT.Sqrt, bias=nv_four[a - 1][:, t : t + 1])
 
         def scatter(page, j0, width, values, weights):
             nc.vector.tensor_tensor(out=pages[page][:].indirect(entries(slots, j0, width)), in0=values, in1=weights, op=ALU.mult)
-
-        def scatter_four(page, t, values):
-            scatter(page, 0, S, values, quarter(wgs_four, t))
 
         def gather(page, t, m0, width, dst, errors):
             nc.vector.tensor_tensor(
                 out=dst, in0=pages[page][:].indirect(entries(carriers, m0, width)), in1=quarter(errors, t, width, m0), op=ALU.add
             )
 
-        def quantise_z(a, m0, width, grouped):
-            nc.vector.quantize_mx(out=z_w[a][:, m0 : m0 + width].bitcast(E4M3), scales=z_s[a][:, m0 : m0 + width], in_=grouped)
+        def quantise_z(a, m0, width, rounded):
+            nc.vector.quantize_mx(out=z_w[a][:, m0 : m0 + width].bitcast(E4M3), scales=z_s[a][:, m0 : m0 + width], in_=rounded)
 
-        def turn_first_pass(z_nat, grouped):
-            words = grouped.bitcast(F32)
-            for pair in range(4):
-                bank_back = banks[6 + pair % 2]
+        def turn_first_pass(z_nat, rounded):
+            pairs = rounded.bitcast(F32)
+            for group in range(4):
+                bank_back = banks[6 + group % 2]
                 for i in range(2):
-                    m0 = 2 * P * pair + P * i
+                    m0 = 2 * P * group + P * i
                     bank_in = banks[4 + i]
                     for t in range(4):
                         nc.tensor.transpose(bank_in[:, P * t : P * (t + 1)], z_nat[t][:, m0 : m0 + P], ident[:])
@@ -237,10 +236,10 @@ def tile_list_pilot_envelope_reliability_kernel(
                             bank_back[:, P * (2 * i + u) : P * (2 * i + u + 1)], z_rows[i][:].bitcast(F32)[:, P * u : P * (u + 1)], ident[:]
                         )
                 nc.scalar.copy(
-                    out=words[:, PASS * pair : PASS * (pair + 1)].rearrange("p (i m u) -> p i m u", i=2, u=2),
+                    out=pairs[:, PASS * group : PASS * (group + 1)].rearrange("p (i m u) -> p i m u", i=2, u=2),
                     in_=bank_back[:].rearrange("p (i u m) -> p i m u", i=2, u=2),
                 )
-            quantise_z(0, 0, M, grouped)
+            quantise_z(0, 0, M, rounded)
 
         def late_page(tag):
             page = sb.tile([P, T2], F32, name="page%d" % len(pages), tag=tag, align_bytes=64)
@@ -248,18 +247,20 @@ def tile_list_pilot_envelope_reliability_kernel(
             pages.append(page)
 
         nc.vector.tensor_copy(out=v_s[:], in_=tab_s[:].indirect(pilots[:]))
-        quantise_wq(0, wq_first[:])
+        quantise_wq(0, (0,), wq_first[:, 0:PASS])
         for j0, width in FIRST_PIECES:
             nc.vector.tensor_copy(out=v_w[:, j0 : j0 + width], in_=tab_w[:].bitcast(U32).indirect(entries(pilots, j0, width)))
         late_page("words_then_page")
+        quantise_wq(1, (1,), wq_first[:, PASS : 2 * PASS])
         steps = [(0, j0, width) for j0, width in FIRST_PIECES] + [(b, j0, PASS) for b in range(1, 4) for j0 in (0, PASS)]
+        end_of_tile_0, end_of_tile_1, end_of_tile_3 = 2, 4, 8
         squares = [
             quarter(buf_b, 0), early[0][:], quarter(buf_b, 2), quarter(buf_b, 3), early[1][:],
             quarter(buf_b, 1), quarter(buf_b, 0), quarter(buf_b, 2), quarter(buf_c, 3),
         ]
         z_nat = [quarter(buf_d, t) for t in range(4)]
         for step, (b, j0, width) in enumerate(steps):
-            if step == 2:
+            if step == end_of_tile_0:
                 envelope_rows(b, j0, width, [banks[4], banks[1]], banks[6], squares[step])
             else:
                 envelope_rows(b, j0, width, banks[2 * (step % 2) : 2 * (step % 2) + 2], banks[4 + step % 2], squares[step])
@@ -267,65 +268,59 @@ def tile_list_pilot_envelope_reliability_kernel(
                 scatter(b, j0, width, quarter(env_a, b, width, j0), wgs_nat[:, j0 : j0 + width])
             elif j0 > 0:
                 scatter(b % 2, 0, S, quarter(env_a, b), wgs_nat[:])
-            if step == 0:
-                quantise_wq(1, squares[0][:, 0:256].bitcast(BF16))
-            if step == 2:
-                quantise_wq(2, squares[1][:, 0:512].bitcast(BF16))
+            if step == end_of_tile_0:
+                quantise_wq(2, (2,), squares[1][:, 0:PASS].bitcast(BF16))
                 late_page("early_then_page0")
-            if step == 4:
-                quantise_wq(3, squares[4].bitcast(BF16))
+            if step == end_of_tile_1:
+                quantise_wq(3, (3, 4), squares[step].bitcast(BF16))
                 late_page("early_then_page1")
-            if step == 8:
-                quantise_wq(4, squares[8].bitcast(BF16))
-            if step in (4, 8):
+            if step == end_of_tile_3:
+                quantise_wq(4, (5,), squares[step].bitcast(BF16))
+            if step in (end_of_tile_1, end_of_tile_3):
                 gather(0, b - 1, 0, M, z_nat[b - 1], err_a)
                 gather(1, b, 0, M, z_nat[b], err_a)
 
-        for half, buf in enumerate((buf_a[:], buf_b)):
-            view = by_pilots(buf)
-            squares_of_pass(1, PASS * half, view)
+        for j0, buf in ((0, buf_a), (PASS, buf_b)):
+            view = squares_of_pass(1, j0, buf)
             for t in range(4):
-                sum_of_squares(t, view)
-                root(1, t, quarter(env_b, t, PASS, PASS * half))
+                envelope_four(1, t, view, quarter(env_b, t, PASS, j0))
         for pair in ((0, 1), (2, 3)):
             for t in pair:
-                scatter_four(t % 2, t, quarter(env_b, t))
+                scatter(t % 2, 0, S, quarter(env_b, t), quarter(wgs_four, t))
             for t in pair:
                 gather(t % 2, t, 0, M, quarter(buf_b, t), err_b)
         nc.sync.dma_start(out=err_a[:], in_=err[2 * PASS : 3 * PASS, :].rearrange("(p t) m -> p (t m)", t=4))
 
-        env_last = [quarter(env_a, 0), quarter(env_a, 1), buf_b_long[:, 0:S], quarter(wgs_four, 4)]
-        view = by_pilots(buf_c[:])
-        squares_of_pass(2, 0, view)
+        view = squares_of_pass(2, 0, buf_c)
         for t in range(4):
-            sum_of_squares(t, view)
-            root(2, t, env_last[t][:, 0:PASS])
+            envelope_four(2, t, view, quarter(env_a, t, PASS))
         turn_first_pass(z_nat, buf_a[:, 2 * M : 4 * M].bitcast(BF16))
-        view = by_rows(buf_c[:])
-        squares_of_pass(2, PASS, view)
-        grouped_1 = buf_c[:, 0 : 2 * M].bitcast(BF16)
+        view = squares_of_pass(2, PASS, buf_c)
         for t in range(4):
-            if t == 2:
-                interleave(nc.scalar.copy, grouped_1, buf_b)
-                quantise_z(1, 0, M, grouped_1)
-            sum_of_squares(t, view)
-            root(2, t, env_last[t][:, PASS:S])
-            scatter_four(t, t, env_last[t])
+            envelope_four(2, t, view, quarter(env_a, t, PASS, PASS))
+            scatter(t, 0, S, quarter(env_a, t), quarter(wgs_four, t))
+        rounded_1 = buf_c[:, 0 : 2 * M].bitcast(BF16)
+        interleave(nc.scalar.copy, rounded_1, buf_b[:])
+        quantise_z(1, 0, M, rounded_1)
 
-        picked = [quarter(wgs_four, 3, M, 768), quarter(wgs_four, 3), quarter(wgs_four, 3, M, 768), quarter(wgs_four, 3, PASS), quarter(wgs_four, 3, PASS, 768)]
-        grouped = [buf_a[:, 2 * M + 2 * m0 : 2 * M + 2 * (m0 + width)].bitcast(BF16) for m0, width in CHUNKS]
+        shared = 3 * 256
+        picked = [
+            buf_b[:, shared : shared + M], buf_b[:, 0:M], buf_b[:, shared : shared + M], buf_b[:, 0:PASS], buf_b[:, shared : shared + PASS],
+        ]
+        rounded_2 = [buf_a[:, 2 * M + 2 * m0 : 2 * M + 2 * (m0 + width)].bitcast(BF16) for m0, width in CHUNKS]
+        staged = [err_b[:, PASS * n : PASS * (n + 1)] for n in range(8)] + [buf_d[:, PASS * n : PASS * (n + 1)] for n in range(3)]
         out_n = out.rearrange("(i p) m -> p i m", p=P)
         open_banks = []
 
-        def products(c, tiles_i, passes, closing):
+        def products(c, out_tiles, passes, closing=()):
             m0, width = CHUNKS[c]
             for a in passes:
-                for i in tiles_i:
+                for i in out_tiles:
                     bank, col = PLACES[c][i]
                     start = bank not in open_banks
                     if start:
                         open_banks.append(bank)
-                    stop = a == 2 and i in closing
+                    stop = i in closing
                     if stop:
                         open_banks.remove(bank)
                     nc.tensor.matmul_mx(
@@ -334,55 +329,57 @@ def tile_list_pilot_envelope_reliability_kernel(
                         rhs=z_w[a][:, m0 : m0 + width].bitcast(E4M3), rhs_scale=z_s[a][:, m0 : m0 + width], start=start, stop=stop,
                     )
 
-        def store(engine_copy, bank, staged, i0, count, m0, width):
-            engine_copy(out=staged, in_=banks[bank][:, 0 : count * width])
-            nc.sync.dma_start(out=out_n[:, i0 : i0 + count, m0 : m0 + width], in_=staged.rearrange("p (i m) -> p i m", i=count))
+        def store(engine_copy, bank, i0, count, m0, width):
+            result = staged.pop(0)[:, 0 : count * width]
+            engine_copy(out=result, in_=banks[bank][:, 0 : count * width])
+            nc.sync.dma_start(out=out_n[:, i0 : i0 + count, m0 : m0 + width], in_=result.rearrange("p (i m) -> p i m", i=count))
 
         def gather_chunk(c, row_tiles):
             m0, width = CHUNKS[c]
             for t in row_tiles:
                 gather(t, t, m0, width, picked[c][:, width * t : width * (t + 1)], err_a)
 
+        def round_chunk(c, engine_copy):
+            interleave(engine_copy, rounded_2[c], picked[c])
+
         def last_pass(c, closing):
             m0, width = CHUNKS[c]
-            quantise_z(2, m0, width, grouped[c])
+            quantise_z(2, m0, width, rounded_2[c])
             products(c, range(5), (2,), closing)
 
-        def round_chunk(c, engine_copy):
-            interleave(engine_copy, grouped[c], picked[c])
-
-        staged = [err_b[:, PASS * n : PASS * (n + 1)] for n in range(8)] + [buf_d[:, PASS * n : PASS * (n + 1)] for n in range(4)]
-        for c in range(3):
-            products(c, range(5), (0, 1), ())
-        products(3, (4,), (0, 1), ())
+        for a in (0, 1):
+            for c in range(3):
+                products(c, range(5), (a,))
+            products(3, (4,), (a,))
         gather_chunk(0, range(4))
         round_chunk(0, nc.scalar.copy)
         gather_chunk(1, (0, 1, 2))
         last_pass(0, (1, 3))
-        store(nc.scalar.copy, 0, staged[0], 0, 2, 0, 256)
+        store(nc.scalar.copy, 0, 0, 2, 0, 256)
         gather_chunk(1, (3,))
         round_chunk(1, nc.scalar.copy)
-        store(nc.scalar.copy, 1, staged[1], 2, 2, 0, 256)
-        products(3, range(4), (0, 1), ())
-        products(4, range(3), (0, 1), ())
+        store(nc.scalar.copy, 1, 2, 2, 0, 256)
+        products(3, range(4), (0, 1))
+        products(4, range(3), (0, 1))
         gather_chunk(2, (1, 2, 3))
         last_pass(1, (1, 3, 4))
-        store(nc.scalar.copy, 3, staged[2], 0, 2, 256, 256)
+        store(nc.scalar.copy, 3, 0, 2, 256, 256)
         gather_chunk(2, (0,))
         round_chunk(2, nc.scalar.copy)
-        store(nc.scalar.copy, 4, staged[3], 2, 2, 256, 256)
-        products(4, (3, 4), (0, 1), ())
+        store(nc.scalar.copy, 4, 2, 2, 256, 256)
+        products(4, (3, 4), (0, 1))
         gather_chunk(3, range(4))
-        round_chunk(3, nc.scalar.copy)
-        store(nc.scalar.copy, 2, staged[4], 4, 1, 0, PASS)
+        store(nc.scalar.copy, 2, 4, 1, 0, 512)
         last_pass(2, (1, 3))
-        gather_chunk(4, range(4))
-        store(nc.scalar.copy, 5, staged[5], 0, 2, 512, 256)
-        store(nc.scalar.copy, 6, staged[6], 2, 2, 512, 256)
+        round_chunk(3, nc.vector.tensor_copy)
+        gather_chunk(4, (0, 1))
         last_pass(3, (3, 4))
+        gather_chunk(4, (2, 3))
+        store(nc.scalar.copy, 5, 0, 2, 512, 256)
+        store(nc.scalar.copy, 6, 2, 2, 512, 256)
         round_chunk(4, nc.vector.tensor_copy)
         last_pass(4, (2, 4))
-        store(nc.vector.tensor_copy, 0, staged[7], 0, 4, 768, 128)
-        store(nc.scalar.copy, 7, staged[8][:, 0:384], 4, 1, 512, 384)
-        store(nc.scalar.copy, 1, staged[9][:, 0:384], 0, 3, 896, 128)
-        store(nc.vector.tensor_copy, 3, staged[10][:, 0:256], 3, 2, 896, 128)
+        store(nc.vector.tensor_copy, 0, 0, 4, 768, 128)
+        store(nc.scalar.copy, 7, 4, 1, 512, 384)
+        store(nc.scalar.copy, 1, 0, 3, 896, 128)
+        store(nc.vector.tensor_copy, 3, 3, 2, 896, 128)

@@ -23,7 +23,7 @@ LIST_ROWS = 16
 FIRST_PIECES = ((0, 256), (256, 256), (512, 512))
 WQ_LOADS = ((0, 128), (128, 128), (256, 256), (512, 256), (768, 256), (1024, 512))
 WQ_PARTS = ((0, 128), (128, 128), (256, 256), (512, 512), (1024, 512))
-WR_PARTS = ((0, 128), (128, 384), (512, 512), (1024, 512))
+WR_PARTS = ((0, 256), (256, 256), (512, 512), (1024, 512))
 CHUNKS = ((0, 256), (256, 256), (512, 256), (768, 128), (896, 128))
 PLACES = (
     ((0, 0), (0, 256), (1, 0), (1, 256), (2, 0)),
@@ -51,7 +51,7 @@ def tile_list_pilot_envelope_reliability_kernel(
         pilots = tile("pilots", S // LIST_ROWS, U16)
         slots = tile("slots", S // LIST_ROWS, U16)
         carriers = tile("carriers", M // LIST_ROWS, U16)
-        tab_w = sb.tile([P, T], I32, name="tab_w", tag="words_then_page", align_bytes=64)
+        tab_w = sb.tile([P, T], I32, name="tab_w", tag="early_then_page1", align_bytes=64)
         tab_s = tile("tab_s", T, U8)
         v_w = tile("v_w", S, U32)
         v_s = tile("v_s", S, U8)
@@ -60,15 +60,14 @@ def tile_list_pilot_envelope_reliability_kernel(
         wq_w = [tile("wq_w%d" % c0, width, U32) for c0, width in WQ_PARTS]
         wq_s = [tile("wq_s%d" % c0, width, U8) for c0, width in WQ_PARTS]
         wm_w = tile("wm_w", 3 * N, I32)
-        wm_s = tile("wm_s", 3 * N, U8)
-        nv_first = tile("nv_first", 1, F32)
-        nv_nat = tile("nv_nat", 3, F32)
+        nv_first = tile("nv_first", 2, F32)
+        nv_nat = tile("nv_nat", 2, F32)
         nv_four = [tile("nv_four%d" % a, 4, F32) for a in (1, 2)]
         ident = tile("ident", P, F32)
         wgs_nat = tile("wgs_nat", S, F32)
         wgs_four = tile("wgs_four", 4 * S, F32)
-        pages = [tile("page0", T2, F32)]
-        early = [sb.tile([P, M], F32, name="early%d" % i, tag="early_then_page%d" % i, align_bytes=64) for i in range(2)]
+        pages = [tile("page%d" % i, T2, F32) for i in range(2)]
+        early = [sb.tile([P, M], F32, name="early0", tag="early_then_page0", align_bytes=64)]
         env_a = tile("env_a", 4 * S, F32)
         env_b = tile("env_b", 4 * S, F32)
         err_a = tile("err_a", 4 * M, F32)
@@ -77,7 +76,7 @@ def tile_list_pilot_envelope_reliability_kernel(
         buf_b = tile("buf_b", 4 * M, F32)
         buf_c = tile("buf_c", 4 * M, F32)
         buf_d = tile("buf_d", 4 * M, F32)
-        wq_first = tile("wq_first", 8 * P, BF16)
+        wq_first = sb.tile([P, 8 * P], BF16, name="wq_first", tag="wq_first_then_wm_s", align_bytes=64)
         z_rows = [tile("z_rows%d" % i, PASS, BF16) for i in range(2)]
         z_w = [tile("z_w%d" % a, M, U32) for a in range(3)]
         z_s = [tile("z_s%d" % a, M, U8) for a in range(3)]
@@ -111,19 +110,19 @@ def tile_list_pilot_envelope_reliability_kernel(
             nc.vector.quantize_mx(out=wq_w[part][:].bitcast(E4M3), scales=wq_s[part][:], in_=rounded)
 
         warm = tile("warm", 2, F32)
-        nc.gpsimd.memset(tab_s[:].bitcast(I32), 0)
+        nc.vector.memset(tab_s[:].bitcast(I32), 0)
         nc.vector.memset(warm[:, 0:1], 1.0)
         nc.vector.memset(wr_s[:].bitcast(I32), 0)
         nc.scalar.activation(out=warm[:, 1:2], in_=warm[:, 0:1], func=ACT.Sqrt)
         nc.sync.dma_start(pilots[:], offs)
-        load_scale_rows(tab_s, tab_scales[0])
         load_wq(0)
-        nc.sync.dma_start(out=tab_w[:], in_=tab_words[0].rearrange("p t i -> p (t i)").bitcast(I32))
         load_wr(0)
+        load_scale_rows(tab_s, tab_scales[0])
+        nc.sync.dma_start(out=tab_w[:], in_=tab_words[0].rearrange("p t i -> p (t i)").bitcast(I32))
         load_scale_rows(wr_s, wr_scales[0])
         load_wq(1)
         with nc.allow_non_contiguous_dma(reason="one noise power a partition"):
-            nc.sync.dma_start(out=nv_first[:], in_=nv[0:P].rearrange("(b p) -> p b", p=P))
+            nc.sync.dma_start(out=nv_first[:], in_=nv[0 : 2 * P].rearrange("(b p) -> p b", p=P))
         nc.sync.dma_start(slots[:], offs2)
         first_width = FIRST_PIECES[0][1]
         nc.sync.dma_start(out=wgs_nat[:, 0:first_width], in_=wgs[:, 0:first_width])
@@ -131,7 +130,7 @@ def tile_list_pilot_envelope_reliability_kernel(
         load_wq(2)
         load_wr(1)
         with nc.allow_non_contiguous_dma(reason="one noise power a partition"):
-            nc.sync.dma_start(out=nv_nat[:], in_=nv[P:PASS].rearrange("(b p) -> p b", p=P))
+            nc.sync.dma_start(out=nv_nat[:], in_=nv[2 * P : PASS].rearrange("(b p) -> p b", p=P))
         for load in (3, 4):
             load_wq(load)
         nc.sync.dma_start(carriers[:], offs3)
@@ -146,13 +145,8 @@ def tile_list_pilot_envelope_reliability_kernel(
         nc.sync.dma_start(out=err_b[:], in_=err[PASS : 2 * PASS, :].rearrange("(p t) m -> p (t m)", t=4))
         nc.sync.dma_start(out=wm_w[:].rearrange("p (a c) -> p a c", a=3), in_=wm_words.rearrange("a p c i -> p a (c i)").bitcast(I32))
         make_identity(nc, ident[:])
-        nc.vector.memset(pages[0][:].bitcast(I32), 0)
-        nc.gpsimd.memset(wm_s[:].bitcast(I32), 0)
-        for q in range(4):
-            nc.sync.dma_start(
-                out=wm_s[32 * q : 32 * q + 4, :].bitcast(I32).rearrange("p (a c) -> p a c", a=3),
-                in_=wm_scales[:, 4 * q : 4 * q + 4, :].rearrange("a r c -> r a c").bitcast(I32),
-            )
+        for page in pages:
+            nc.vector.memset(page[:].bitcast(I32), 0)
 
         def entries(lst, j0, width):
             return lst[:, j0 // LIST_ROWS : (j0 + width) // LIST_ROWS]
@@ -189,7 +183,7 @@ def tile_list_pilot_envelope_reliability_kernel(
                 nc.scalar.activation(out=squares[:, width * n : width * (n + 1)], in_=bank[:, 0:width], func=ACT.Square)
             for i in range(width // P):
                 add_turned(bank_sum[:, P * i : P * (i + 1)], squares[:, 2 * P * i : 2 * P * i + P], squares[:, 2 * P * i + P : 2 * P * (i + 1)])
-            bias = nv_first[:] if b == 0 else nv_nat[:, b - 1 : b]
+            bias = nv_first[:, b : b + 1] if b < 2 else nv_nat[:, b - 2 : b - 1]
             nc.scalar.activation(out=quarter(env_a, b, width, j0), in_=bank_sum[:, 0:width], func=ACT.Sqrt, bias=bias)
 
         def squares_of_pass(a, j0, buf):
@@ -250,26 +244,31 @@ def tile_list_pilot_envelope_reliability_kernel(
         quantise_wq(0, (0,), wq_first[:, 0:PASS])
         for j0, width in FIRST_PIECES:
             nc.vector.tensor_copy(out=v_w[:, j0 : j0 + width], in_=tab_w[:].bitcast(U32).indirect(entries(pilots, j0, width)))
-        late_page("words_then_page")
         quantise_wq(1, (1,), wq_first[:, PASS : 2 * PASS])
-        steps = [(0, j0, width) for j0, width in FIRST_PIECES] + [(b, j0, PASS) for b in range(1, 4) for j0 in (0, PASS)]
-        end_of_tile_0, end_of_tile_1, end_of_tile_3 = 2, 4, 8
+        early.append(sb.tile([P, M], F32, name="early1", tag="early_then_page1", align_bytes=64))
+        wm_s = sb.tile([P, 3 * N], U8, name="wm_s", tag="wq_first_then_wm_s", align_bytes=64)
+        nc.gpsimd.memset(wm_s[:].bitcast(I32), 0)
+        for q in range(4):
+            nc.sync.dma_start(
+                out=wm_s[32 * q : 32 * q + 4, :].bitcast(I32).rearrange("p (a c) -> p a c", a=3),
+                in_=wm_scales[:, 4 * q : 4 * q + 4, :].rearrange("a r c -> r a c").bitcast(I32),
+            )
+        steps = [(0, 0, 256), (0, 256, 256), (1, 0, 256), (0, 512, 256), (1, 256, 256), (0, 768, 256), (1, 512, 512)]
+        steps = steps + [(b, j0, PASS) for b in (2, 3) for j0 in (0, PASS)]
+        end_of_tile_0, end_of_tile_1, end_of_tile_3 = 3, 6, 10
         squares = [
-            quarter(buf_b, 0), early[0][:], quarter(buf_b, 2), quarter(buf_b, 3), early[1][:],
-            quarter(buf_b, 1), quarter(buf_b, 0), quarter(buf_b, 2), quarter(buf_c, 3),
+            quarter(buf_b, 0), quarter(buf_b, 1), quarter(buf_b, 2), early[0][:], quarter(buf_b, 3), quarter(buf_b, 0), early[1][:],
+            quarter(buf_b, 1), quarter(buf_b, 2), quarter(buf_b, 3), quarter(buf_c, 3),
         ]
         z_nat = [quarter(buf_d, t) for t in range(4)]
         for step, (b, j0, width) in enumerate(steps):
-            if step == end_of_tile_0:
-                envelope_rows(b, j0, width, [banks[4], banks[1]], banks[6], squares[step])
-            else:
-                envelope_rows(b, j0, width, banks[2 * (step % 2) : 2 * (step % 2) + 2], banks[4 + step % 2], squares[step])
+            envelope_rows(b, j0, width, banks[2 * (step % 2) : 2 * (step % 2) + 2], banks[4 + step % 2], squares[step])
             if b < 2:
                 scatter(b, j0, width, quarter(env_a, b, width, j0), wgs_nat[:, j0 : j0 + width])
             elif j0 > 0:
                 scatter(b % 2, 0, S, quarter(env_a, b), wgs_nat[:])
             if step == end_of_tile_0:
-                quantise_wq(2, (2,), squares[1][:, 0:PASS].bitcast(BF16))
+                quantise_wq(2, (2,), squares[step][:, 0:PASS].bitcast(BF16))
                 late_page("early_then_page0")
             if step == end_of_tile_1:
                 quantise_wq(3, (3, 4), squares[step].bitcast(BF16))

@@ -20,9 +20,10 @@ ALU = mybir.AluOpType
 P = 128
 PASS = 512
 LIST_ROWS = 16
+SCALES_AHEAD = 768
 FIRST_PIECES = ((0, 256), (256, 256), (512, 512))
-WQ_LOADS = ((0, 128), (128, 128), (256, 256), (512, 256), (768, 256), (1024, 512))
-WQ_PARTS = ((0, 128), (128, 128), (256, 256), (512, 512), (1024, 512))
+WQ_LOADS = ((0, 256), (256, 256), (512, 256), (768, 256), (1024, 512))
+WQ_PARTS = ((0, 256), (256, 256), (512, 512), (1024, 512))
 WR_PARTS = ((0, 256), (256, 256), (512, 512), (1024, 512))
 CHUNKS = ((0, 256), (256, 256), (512, 256), (768, 128), (896, 128))
 PLACES = (
@@ -52,9 +53,10 @@ def tile_list_pilot_envelope_reliability_kernel(
         slots = tile("slots", S // LIST_ROWS, U16)
         carriers = tile("carriers", M // LIST_ROWS, U16)
         tab_w = sb.tile([P, T], I32, name="tab_w", tag="early_then_page1", align_bytes=64)
-        tab_s = tile("tab_s", T, U8)
+        tab_s = sb.tile([P, T], U8, name="tab_s", tag="tab_s_then_wm_s", align_bytes=64)
         v_w = tile("v_w", S, U32)
-        v_s = tile("v_s", S, U8)
+        v_s = [tile("v_s0", SCALES_AHEAD, U8)]
+        first_squares = sb.tile([P, 2 * P], F32, name="first_squares", tag="squares_then_scales", align_bytes=64)
         wr_w = [tile("wr_w%d" % c0, 2 * width, U8) for c0, width in WR_PARTS]
         wr_s = tile("wr_s", H, U8)
         wq_w = [tile("wq_w%d" % c0, width, U32) for c0, width in WQ_PARTS]
@@ -76,7 +78,7 @@ def tile_list_pilot_envelope_reliability_kernel(
         buf_b = tile("buf_b", 4 * M, F32)
         buf_c = tile("buf_c", 4 * M, F32)
         buf_d = tile("buf_d", 4 * M, F32)
-        wq_first = sb.tile([P, 8 * P], BF16, name="wq_first", tag="wq_first_then_wm_s", align_bytes=64)
+        wq_first = tile("wq_first", 8 * P, BF16)
         z_rows = [tile("z_rows%d" % i, PASS, BF16) for i in range(2)]
         z_w = [tile("z_w%d" % a, M, U32) for a in range(3)]
         z_s = [tile("z_s%d" % a, M, U8) for a in range(3)]
@@ -87,7 +89,7 @@ def tile_list_pilot_envelope_reliability_kernel(
                 nc.sync.dma_start(out=plane[32 * q : 32 * q + 4, :].bitcast(I32), in_=rows[4 * q : 4 * q + 4, :].bitcast(I32))
 
         wq_raw = [
-            quarter(buf_c, 0, PASS), quarter(buf_c, 0, PASS, PASS), quarter(buf_c, 1),
+            quarter(buf_c, 0), quarter(buf_c, 1),
             quarter(buf_d, 0), quarter(buf_d, 1), buf_d[:, 2 * M : 4 * M],
         ]
         wq_k = wq.rearrange("(p i) c -> p i c", i=4)
@@ -116,29 +118,28 @@ def tile_list_pilot_envelope_reliability_kernel(
         nc.scalar.activation(out=warm[:, 1:2], in_=warm[:, 0:1], func=ACT.Sqrt)
         nc.sync.dma_start(pilots[:], offs)
         load_wq(0)
-        load_wr(0)
         load_scale_rows(tab_s, tab_scales[0])
         nc.sync.dma_start(out=tab_w[:], in_=tab_words[0].rearrange("p t i -> p (t i)").bitcast(I32))
+        load_wr(0)
         load_scale_rows(wr_s, wr_scales[0])
-        load_wq(1)
         with nc.allow_non_contiguous_dma(reason="one noise power a partition"):
             nc.sync.dma_start(out=nv_first[:], in_=nv[0 : 2 * P].rearrange("(b p) -> p b", p=P))
         nc.sync.dma_start(slots[:], offs2)
         first_width = FIRST_PIECES[0][1]
         nc.sync.dma_start(out=wgs_nat[:, 0:first_width], in_=wgs[:, 0:first_width])
         nc.sync.dma_start(out=wgs_nat[:, first_width:S], in_=wgs[:, first_width:S])
-        load_wq(2)
+        load_wq(1)
         load_wr(1)
         with nc.allow_non_contiguous_dma(reason="one noise power a partition"):
             nc.sync.dma_start(out=nv_nat[:], in_=nv[2 * P : PASS].rearrange("(b p) -> p b", p=P))
-        for load in (3, 4):
+        for load in (2, 3):
             load_wq(load)
         nc.sync.dma_start(carriers[:], offs3)
         nc.sync.dma_start(out=err_a[:].rearrange("p (t m) -> p t m", t=4), in_=err[0:PASS, :].rearrange("(t p) m -> p t m", p=P))
         load_wr(2)
         for a in (1, 2):
             nc.sync.dma_start(out=nv_four[a - 1][:], in_=nv[PASS * a : PASS * (a + 1)].rearrange("(p t) -> p t", t=4))
-        load_wq(5)
+        load_wq(4)
         for q in range(4):
             nc.sync.dma_start(out=wgs_four[32 * q : 32 * q + 32, :], in_=wgs.rearrange("(r t) j -> r (t j)", t=4))
         load_wr(3)
@@ -157,7 +158,7 @@ def tile_list_pilot_envelope_reliability_kernel(
 
         def first_products(out_re, out_im, j0, c0, width):
             lhs = v_w[:, j0 : j0 + P].bitcast(E4M3)
-            lhs_s = v_s[:, j0 : j0 + P]
+            lhs_s = v_s[0][:, j0 : j0 + P] if j0 < SCALES_AHEAD else v_s[1][:, j0 - SCALES_AHEAD : j0 - SCALES_AHEAD + P]
             part, c = columns(WQ_PARTS, c0)
             nc.tensor.matmul_mx(
                 out=out_im, lhsT=lhs, lhsT_scale=lhs_s,
@@ -180,9 +181,10 @@ def tile_list_pilot_envelope_reliability_kernel(
                     first_products(
                         bank[:, 2 * P * i : 2 * P * i + P], bank[:, 2 * P * i + P : 2 * P * (i + 1)], j0 + P * (per_bank * n + i), P * b, P
                     )
-                nc.scalar.activation(out=squares[:, width * n : width * (n + 1)], in_=bank[:, 0:width], func=ACT.Square)
+                nc.scalar.activation(out=squares[n], in_=bank[:, 0:width], func=ACT.Square)
             for i in range(width // P):
-                add_turned(bank_sum[:, P * i : P * (i + 1)], squares[:, 2 * P * i : 2 * P * i + P], squares[:, 2 * P * i + P : 2 * P * (i + 1)])
+                n, c = divmod(2 * P * i, width)
+                add_turned(bank_sum[:, P * i : P * (i + 1)], squares[n][:, c : c + P], squares[n][:, c + P : c + 2 * P])
             bias = nv_first[:, b : b + 1] if b < 2 else nv_nat[:, b - 2 : b - 1]
             nc.scalar.activation(out=quarter(env_a, b, width, j0), in_=bank_sum[:, 0:width], func=ACT.Sqrt, bias=bias)
 
@@ -240,41 +242,55 @@ def tile_list_pilot_envelope_reliability_kernel(
             nc.gpsimd.memset(page[:], 0.0)
             pages.append(page)
 
-        nc.vector.tensor_copy(out=v_s[:], in_=tab_s[:].indirect(pilots[:]))
-        quantise_wq(0, (0,), wq_first[:, 0:PASS])
-        for j0, width in FIRST_PIECES:
+        def gather_scales(dst, j0, width):
+            nc.vector.tensor_copy(out=dst[:], in_=tab_s[:].indirect(entries(pilots, j0, width)))
+
+        def gather_words(j0, width):
             nc.vector.tensor_copy(out=v_w[:, j0 : j0 + width], in_=tab_w[:].bitcast(U32).indirect(entries(pilots, j0, width)))
-        quantise_wq(1, (1,), wq_first[:, PASS : 2 * PASS])
+
+        gather_scales(v_s[0], 0, SCALES_AHEAD)
+        quantise_wq(0, (0,), wq_first[:])
+        gather_words(0, 256)
+        gather_words(256, 256)
+        gather_words(512, 512)
         early.append(sb.tile([P, M], F32, name="early1", tag="early_then_page1", align_bytes=64))
-        wm_s = sb.tile([P, 3 * N], U8, name="wm_s", tag="wq_first_then_wm_s", align_bytes=64)
-        nc.gpsimd.memset(wm_s[:].bitcast(I32), 0)
-        for q in range(4):
-            nc.sync.dma_start(
-                out=wm_s[32 * q : 32 * q + 4, :].bitcast(I32).rearrange("p (a c) -> p a c", a=3),
-                in_=wm_scales[:, 4 * q : 4 * q + 4, :].rearrange("a r c -> r a c").bitcast(I32),
-            )
-        steps = [(0, 0, 256), (0, 256, 256), (1, 0, 256), (0, 512, 256), (1, 256, 256), (0, 768, 256), (1, 512, 512)]
+        steps = [(b, j0, 256) for j0 in range(0, S, 256) for b in (0, 1)]
         steps = steps + [(b, j0, PASS) for b in (2, 3) for j0 in (0, PASS)]
-        end_of_tile_0, end_of_tile_1, end_of_tile_3 = 3, 6, 10
+        end_of_tile_0, end_of_tile_1, end_of_tile_3 = 5, 7, 11
         squares = [
-            quarter(buf_b, 0), quarter(buf_b, 1), quarter(buf_b, 2), early[0][:], quarter(buf_b, 3), quarter(buf_b, 0), early[1][:],
-            quarter(buf_b, 1), quarter(buf_b, 2), quarter(buf_b, 3), quarter(buf_c, 3),
+            quarter(buf_b, 0), quarter(buf_b, 1), quarter(buf_b, 2), quarter(buf_b, 3), quarter(buf_b, 0), early[0][:], quarter(buf_b, 1),
+            early[1][:], quarter(buf_b, 2), quarter(buf_b, 3), quarter(buf_b, 0), quarter(buf_c, 3),
         ]
         z_nat = [quarter(buf_d, t) for t in range(4)]
         for step, (b, j0, width) in enumerate(steps):
-            envelope_rows(b, j0, width, banks[2 * (step % 2) : 2 * (step % 2) + 2], banks[4 + step % 2], squares[step])
+            halves = [squares[step][:, width * n : width * (n + 1)] for n in range(2)]
+            if step == 0:
+                halves[0] = first_squares[:]
+            if step == end_of_tile_1:
+                halves[1] = squares[step][:, PASS : PASS + width]
+            envelope_rows(b, j0, width, banks[2 * (step % 2) : 2 * (step % 2) + 2], banks[4 + step % 2], halves)
+            if step == 0:
+                v_s.append(sb.tile([P, S - SCALES_AHEAD], U8, name="v_s1", tag="squares_then_scales", align_bytes=64))
+                gather_scales(v_s[1], SCALES_AHEAD, S - SCALES_AHEAD)
+                wm_s = sb.tile([P, 3 * N], U8, name="wm_s", tag="tab_s_then_wm_s", align_bytes=64)
+                nc.gpsimd.memset(wm_s[:].bitcast(I32), 0)
+                for q in range(4):
+                    nc.sync.dma_start(
+                        out=wm_s[32 * q : 32 * q + 4, :].bitcast(I32).rearrange("p (a c) -> p a c", a=3),
+                        in_=wm_scales[:, 4 * q : 4 * q + 4, :].rearrange("a r c -> r a c").bitcast(I32),
+                    )
             if b < 2:
                 scatter(b, j0, width, quarter(env_a, b, width, j0), wgs_nat[:, j0 : j0 + width])
             elif j0 > 0:
                 scatter(b % 2, 0, S, quarter(env_a, b), wgs_nat[:])
             if step == end_of_tile_0:
-                quantise_wq(2, (2,), squares[step][:, 0:PASS].bitcast(BF16))
+                quantise_wq(1, (1,), squares[step][:, 0:PASS].bitcast(BF16))
                 late_page("early_then_page0")
             if step == end_of_tile_1:
-                quantise_wq(3, (3, 4), squares[step].bitcast(BF16))
+                quantise_wq(2, (2, 3), squares[step].bitcast(BF16))
                 late_page("early_then_page1")
             if step == end_of_tile_3:
-                quantise_wq(4, (5,), squares[step].bitcast(BF16))
+                quantise_wq(3, (4,), squares[step].bitcast(BF16))
             if step in (end_of_tile_1, end_of_tile_3):
                 gather(0, b - 1, 0, M, z_nat[b - 1], err_a)
                 gather(1, b, 0, M, z_nat[b], err_a)
@@ -284,8 +300,9 @@ def tile_list_pilot_envelope_reliability_kernel(
             for t in range(4):
                 envelope_four(1, t, view, quarter(env_b, t, PASS, j0))
         for pair in ((0, 1), (2, 3)):
-            for t in pair:
-                scatter(t % 2, 0, S, quarter(env_b, t), quarter(wgs_four, t))
+            for j0, width in (((0, PASS), (PASS, PASS)) if pair[0] == 0 else ((0, S),)):
+                for t in pair:
+                    scatter(t % 2, j0, width, quarter(env_b, t, width, j0), quarter(wgs_four, t, width, j0))
             for t in pair:
                 gather(t % 2, t, 0, M, quarter(buf_b, t), err_b)
         nc.sync.dma_start(out=err_a[:], in_=err[2 * PASS : 3 * PASS, :].rearrange("(p t) m -> p (t m)", t=4))

@@ -67,7 +67,7 @@ def tile_list_pilot_envelope_reliability_kernel(
         nv_four = [tile("nv_four%d" % a, 4, F32) for a in (1, 2)]
         ident = tile("ident", P, F32)
         wgs_nat = tile("wgs_nat", S, F32)
-        wgs_four = tile("wgs_four", 4 * S, F32)
+        wgs_four = sb.tile([P, 4 * S], F32, name="wgs_four", tag="run0", align_bytes=64)
         pages = [tile("page%d" % i, T2, F32) for i in range(2)]
         early = [sb.tile([P, M], F32, name="early0", tag="early_then_page0", align_bytes=64)]
         env_a = tile("env_a", 4 * S, F32)
@@ -80,7 +80,7 @@ def tile_list_pilot_envelope_reliability_kernel(
         buf_d = tile("buf_d", 4 * M, F32)
         wq_first = tile("wq_first", 8 * P, BF16)
         z_rows = [tile("z_rows%d" % i, PASS, BF16) for i in range(2)]
-        z_w = [tile("z_w%d" % a, M, U32) for a in range(3)]
+        z_w = tile("z_w", M, U32)
         z_s = [tile("z_s%d" % a, M, U8) for a in range(3)]
         banks = [ps.tile([P, PASS], F32, name="bank%d" % i) for i in range(8)]
 
@@ -211,8 +211,8 @@ def tile_list_pilot_envelope_reliability_kernel(
                 out=dst, in0=pages[page][:].indirect(entries(carriers, m0, width)), in1=quarter(errors, t, width, m0), op=ALU.add
             )
 
-        def quantise_z(a, m0, width, rounded):
-            nc.vector.quantize_mx(out=z_w[a][:, m0 : m0 + width].bitcast(E4M3), scales=z_s[a][:, m0 : m0 + width], in_=rounded)
+        def quantise_z(a, m0, width, words, rounded):
+            nc.vector.quantize_mx(out=words.bitcast(E4M3), scales=z_s[a][:, m0 : m0 + width], in_=rounded)
 
         def turn_first_pass(z_nat, rounded):
             pairs = rounded.bitcast(F32)
@@ -235,7 +235,6 @@ def tile_list_pilot_envelope_reliability_kernel(
                     out=pairs[:, PASS * group : PASS * (group + 1)].rearrange("p (i m u) -> p i m u", i=2, u=2),
                     in_=bank_back[:].rearrange("p (i u m) -> p i m u", i=2, u=2),
                 )
-            quantise_z(0, 0, M, rounded)
 
         def late_page(tag):
             page = sb.tile([P, T2], F32, name="page%d" % len(pages), tag=tag, align_bytes=64)
@@ -310,20 +309,36 @@ def tile_list_pilot_envelope_reliability_kernel(
         view = squares_of_pass(2, 0, buf_c)
         for t in range(4):
             envelope_four(2, t, view, quarter(env_a, t, PASS))
-        turn_first_pass(z_nat, buf_a[:, 2 * M : 4 * M].bitcast(BF16))
+        rounded_0 = buf_a[:, 2 * M : 4 * M].bitcast(BF16)
+        turn_first_pass(z_nat, rounded_0)
         view = squares_of_pass(2, PASS, buf_c)
         for t in range(4):
             envelope_four(2, t, view, quarter(env_a, t, PASS, PASS))
             scatter(t, 0, S, quarter(env_a, t), quarter(wgs_four, t))
         rounded_1 = buf_c[:, 0 : 2 * M].bitcast(BF16)
         interleave(nc.scalar.copy, rounded_1, buf_b[:])
-        quantise_z(1, 0, M, rounded_1)
 
-        shared = 3 * 256
-        picked = [
-            buf_b[:, shared : shared + M], buf_b[:, 0:M], buf_b[:, shared : shared + M], buf_b[:, 0:PASS], buf_b[:, shared : shared + PASS],
-        ]
-        rounded_2 = [buf_a[:, 2 * M + 2 * m0 : 2 * M + 2 * (m0 + width)].bitcast(BF16) for m0, width in CHUNKS]
+        shift = 768
+        picked = [buf_b[:, shift : shift + M], buf_b[:, 0:M], buf_b[:, shift : shift + M], buf_b[:, 0:PASS], buf_b[:, shift : shift + PASS]]
+        rounded_2 = [sb.tile([P, 4 * width], BF16, name="rounded_2_%d" % c, tag="run%d" % (c + 1), align_bytes=64)[:] if c != 3 else None for c, (m0, width) in enumerate(CHUNKS)]
+        rounded_2[3] = buf_b[:, shift + 768 : shift + M].bitcast(BF16)
+        runs = []
+
+        def z_words(a, m0, width):
+            if a == 2:
+                return z_w[:, m0 : m0 + width]
+            run, col = divmod(m0, 256)
+            return runs[run][:, 256 * a + col : 256 * a + col + width]
+
+        def early_pass(a, chunks):
+            m0 = CHUNKS[chunks[0]][0]
+            width = sum(CHUNKS[c][1] for c in chunks)
+            if len(runs) == m0 // 256:
+                runs.append(sb.tile([P, PASS], U32, name="z_early%d" % len(runs), tag="run%d" % len(runs), align_bytes=64))
+            quantise_z(a, m0, width, z_words(a, m0, width), (rounded_0, rounded_1)[a][:, 4 * m0 : 4 * (m0 + width)])
+            for c in chunks:
+                products(c, range(5), (a,))
+
         staged = [err_b[:, PASS * n : PASS * (n + 1)] for n in range(8)] + [buf_d[:, PASS * n : PASS * (n + 1)] for n in range(3)]
         out_n = out.rearrange("(i p) m -> p i m", p=P)
         open_banks = []
@@ -342,7 +357,7 @@ def tile_list_pilot_envelope_reliability_kernel(
                     nc.tensor.matmul_mx(
                         out=banks[bank][:, col : col + width],
                         lhsT=wm_w[:, N * a + P * i : N * a + P * (i + 1)].bitcast(E4M3), lhsT_scale=wm_s[:, N * a + P * i : N * a + P * (i + 1)],
-                        rhs=z_w[a][:, m0 : m0 + width].bitcast(E4M3), rhs_scale=z_s[a][:, m0 : m0 + width], start=start, stop=stop,
+                        rhs=z_words(a, m0, width).bitcast(E4M3), rhs_scale=z_s[a][:, m0 : m0 + width], start=start, stop=stop,
                     )
 
         def store(engine_copy, bank, i0, count, m0, width):
@@ -360,39 +375,42 @@ def tile_list_pilot_envelope_reliability_kernel(
 
         def last_pass(c, closing):
             m0, width = CHUNKS[c]
-            quantise_z(2, m0, width, rounded_2[c])
+            quantise_z(2, m0, width, z_words(2, m0, width), rounded_2[c])
             products(c, range(5), (2,), closing)
 
-        for a in (0, 1):
-            for c in range(3):
-                products(c, range(5), (a,))
-            products(3, (4,), (a,))
         gather_chunk(0, range(4))
         round_chunk(0, nc.scalar.copy)
+        early_pass(0, (0,))
+        early_pass(1, (0,))
         gather_chunk(1, (0, 1, 2))
         last_pass(0, (1, 3))
-        store(nc.scalar.copy, 0, 0, 2, 0, 256)
         gather_chunk(1, (3,))
         round_chunk(1, nc.scalar.copy)
+        store(nc.scalar.copy, 0, 0, 2, 0, 256)
         store(nc.scalar.copy, 1, 2, 2, 0, 256)
-        products(3, range(4), (0, 1))
-        products(4, range(3), (0, 1))
+        early_pass(0, (1,))
+        early_pass(1, (1,))
         gather_chunk(2, (1, 2, 3))
         last_pass(1, (1, 3, 4))
-        store(nc.scalar.copy, 3, 0, 2, 256, 256)
         gather_chunk(2, (0,))
         round_chunk(2, nc.scalar.copy)
+        store(nc.scalar.copy, 3, 0, 2, 256, 256)
         store(nc.scalar.copy, 4, 2, 2, 256, 256)
-        products(4, (3, 4), (0, 1))
-        gather_chunk(3, range(4))
         store(nc.scalar.copy, 2, 4, 1, 0, 512)
+        gather_chunk(3, range(4))
+        early_pass(0, (2,))
+        early_pass(1, (2,))
         last_pass(2, (1, 3))
-        round_chunk(3, nc.vector.tensor_copy)
-        gather_chunk(4, (0, 1))
-        last_pass(3, (3, 4))
-        gather_chunk(4, (2, 3))
         store(nc.scalar.copy, 5, 0, 2, 512, 256)
         store(nc.scalar.copy, 6, 2, 2, 512, 256)
+        gather_chunk(4, (0,))
+        round_chunk(3, nc.vector.tensor_copy)
+        early_pass(0, (3, 4))
+        early_pass(1, (3,))
+        gather_chunk(4, (1,))
+        last_pass(3, (3, 4))
+        gather_chunk(4, (2, 3))
+        early_pass(1, (4,))
         round_chunk(4, nc.vector.tensor_copy)
         last_pass(4, (2, 4))
         store(nc.vector.tensor_copy, 0, 0, 4, 768, 128)

@@ -250,23 +250,20 @@ def tile_list_pilot_envelope_reliability_kernel(
         gather_scales(v_s[0], 0, SCALES_AHEAD)
         quantise_wq(0, (0,), wq_first[:])
         gather_words(0, 256)
-        gather_words(256, 256)
-        gather_words(512, 512)
+        gather_words(256, 768)
         early.append(sb.tile([P, M], F32, name="early1", tag="early_then_page1", align_bytes=64))
-        steps = [(b, j0, 256) for j0 in range(0, S, 256) for b in (0, 1)]
+        steps = [(b, j0, width) for j0, width in FIRST_PIECES for b in (0, 1)]
         steps = steps + [(b, j0, PASS) for b in (2, 3) for j0 in (0, PASS)]
-        end_of_tile_0, end_of_tile_1, end_of_tile_3 = 5, 7, 11
+        end_of_tile_0, end_of_tile_1, end_of_tile_3 = 4, 5, 9
         squares = [
-            quarter(buf_b, 0), quarter(buf_b, 1), quarter(buf_b, 2), quarter(buf_b, 3), quarter(buf_b, 0), early[0][:], quarter(buf_b, 1),
-            early[1][:], quarter(buf_b, 2), quarter(buf_b, 3), quarter(buf_b, 0), quarter(buf_c, 3),
+            quarter(buf_b, 0), quarter(buf_b, 1), quarter(buf_b, 2), quarter(buf_b, 3), early[0][:],
+            early[1][:], quarter(buf_b, 0), quarter(buf_b, 1), quarter(buf_b, 2), quarter(buf_c, 3),
         ]
         z_nat = [quarter(buf_d, t) for t in range(4)]
         for step, (b, j0, width) in enumerate(steps):
             halves = [squares[step][:, width * n : width * (n + 1)] for n in range(2)]
             if step == 0:
                 halves[0] = first_squares[:]
-            if step == end_of_tile_1:
-                halves[1] = squares[step][:, PASS : PASS + width]
             envelope_rows(b, j0, width, banks[2 * (step % 2) : 2 * (step % 2) + 2], banks[4 + step % 2], halves)
             if step == 0:
                 v_s.append(sb.tile([P, S - SCALES_AHEAD], U8, name="v_s1", tag="squares_then_scales", align_bytes=64))
@@ -299,9 +296,8 @@ def tile_list_pilot_envelope_reliability_kernel(
             for t in range(4):
                 envelope_four(1, t, view, quarter(env_b, t, PASS, j0))
         for pair in ((0, 1), (2, 3)):
-            for j0, width in (((0, PASS), (PASS, PASS)) if pair[0] == 0 else ((0, S),)):
-                for t in pair:
-                    scatter(t % 2, j0, width, quarter(env_b, t, width, j0), quarter(wgs_four, t, width, j0))
+            for t in pair:
+                scatter(t % 2, 0, S, quarter(env_b, t), quarter(wgs_four, t))
             for t in pair:
                 gather(t % 2, t, 0, M, quarter(buf_b, t), err_b)
         nc.sync.dma_start(out=err_a[:], in_=err[2 * PASS : 3 * PASS, :].rearrange("(p t) m -> p (t m)", t=4))
@@ -319,7 +315,8 @@ def tile_list_pilot_envelope_reliability_kernel(
         interleave(nc.scalar.copy, rounded_1, buf_b[:])
 
         shift = 768
-        picked = [buf_b[:, shift : shift + M], buf_b[:, 0:M], buf_b[:, shift : shift + M], buf_b[:, 0:PASS], buf_b[:, shift : shift + PASS]]
+        picked = [buf_b[:, shift : shift + M], buf_b[:, 0:M], buf_b[:, shift : shift + M]]
+        narrow = buf_b[:, 256 : 256 + M]
         rounded_2 = [sb.tile([P, 4 * width], BF16, name="rounded_2_%d" % c, tag="run%d" % (c + 1), align_bytes=64)[:] if c != 3 else None for c, (m0, width) in enumerate(CHUNKS)]
         rounded_2[3] = buf_b[:, shift + 768 : shift + M].bitcast(BF16)
         runs = []
@@ -370,13 +367,23 @@ def tile_list_pilot_envelope_reliability_kernel(
             for t in row_tiles:
                 gather(t, t, m0, width, picked[c][:, width * t : width * (t + 1)], err_a)
 
+        def gather_narrow(t, m0, width):
+            col = 256 * t + m0 - CHUNKS[3][0]
+            gather(t, t, m0, width, narrow[:, col : col + width], err_a)
+
         def round_chunk(c, engine_copy):
             interleave(engine_copy, rounded_2[c], picked[c])
 
-        def last_pass(c, closing):
+        def round_narrow(c):
+            nc.vector.tensor_copy(
+                out=rounded_2[c].rearrange("p (c x i) -> p c i x", x=4, i=4),
+                in_=narrow.rearrange("p (i h c x) -> p h c i x", i=4, h=2, x=4)[:, c - 3],
+            )
+
+        def last_pass(c, closing, out_tiles=range(5)):
             m0, width = CHUNKS[c]
             quantise_z(2, m0, width, z_words(2, m0, width), rounded_2[c])
-            products(c, range(5), (2,), closing)
+            products(c, out_tiles, (2,), closing)
 
         gather_chunk(0, range(4))
         round_chunk(0, nc.scalar.copy)
@@ -397,23 +404,25 @@ def tile_list_pilot_envelope_reliability_kernel(
         store(nc.scalar.copy, 3, 0, 2, 256, 256)
         store(nc.scalar.copy, 4, 2, 2, 256, 256)
         store(nc.scalar.copy, 2, 4, 1, 0, 512)
-        gather_chunk(3, range(4))
+        gather_narrow(0, 768, 256)
+        gather_narrow(1, 768, 256)
         early_pass(0, (2,))
         early_pass(1, (2,))
         last_pass(2, (1, 3))
         store(nc.scalar.copy, 5, 0, 2, 512, 256)
         store(nc.scalar.copy, 6, 2, 2, 512, 256)
-        gather_chunk(4, (0,))
-        round_chunk(3, nc.vector.tensor_copy)
+        gather_narrow(2, 768, 128)
+        gather_narrow(3, 768, 128)
         early_pass(0, (3, 4))
+        round_narrow(3)
         early_pass(1, (3,))
-        gather_chunk(4, (1,))
-        last_pass(3, (3, 4))
-        gather_chunk(4, (2, 3))
+        last_pass(3, (3, 4), (4, 0, 1, 2, 3))
+        gather_narrow(2, 896, 128)
+        gather_narrow(3, 896, 128)
         early_pass(1, (4,))
-        round_chunk(4, nc.vector.tensor_copy)
+        round_narrow(4)
         last_pass(4, (2, 4))
-        store(nc.vector.tensor_copy, 0, 0, 4, 768, 128)
         store(nc.scalar.copy, 7, 4, 1, 512, 384)
+        store(nc.vector.tensor_copy, 0, 0, 4, 768, 128)
         store(nc.scalar.copy, 1, 0, 3, 896, 128)
         store(nc.vector.tensor_copy, 3, 3, 2, 896, 128)

@@ -20,12 +20,13 @@ ALU = mybir.AluOpType
 P = 128
 PASS = 512
 LIST_ROWS = 16
+WIDE, NARROW = 256, 128
 SCALES_AHEAD = 768
 FIRST_PIECES = ((0, 256), (256, 256), (512, 512))
 WQ_LOADS = ((0, 256), (256, 256), (512, 256), (768, 256), (1024, 512))
 WQ_PARTS = ((0, 256), (256, 256), (512, 512), (1024, 512))
 WR_PARTS = ((0, 256), (256, 256), (512, 512), (1024, 512))
-CHUNKS = ((0, 256), (256, 256), (512, 256), (768, 128), (896, 128))
+CHUNKS = ((0, WIDE), (256, WIDE), (512, WIDE), (768, NARROW), (896, NARROW))
 PLACES = (
     ((0, 0), (0, 256), (1, 0), (1, 256), (2, 0)),
     ((3, 0), (3, 256), (4, 0), (4, 256), (2, 256)),
@@ -43,8 +44,8 @@ def tile_list_pilot_envelope_reliability_kernel(
         sb = ctx.enter_context(tc.tile_pool(name="sb", bufs=1))
         ps = ctx.enter_context(tc.psum_pool(name="ps", bufs=1))
 
-        def tile(name, width, dtype):
-            return sb.tile([P, width], dtype, name=name, align_bytes=64)
+        def tile(name, width, dtype, tag=None):
+            return sb.tile([P, width], dtype, name=name, tag=tag or name, align_bytes=64)
 
         def quarter(big, i, width=M, start=0):
             return big[:, M * i + start : M * i + start + width]
@@ -52,11 +53,11 @@ def tile_list_pilot_envelope_reliability_kernel(
         pilots = tile("pilots", S // LIST_ROWS, U16)
         slots = tile("slots", S // LIST_ROWS, U16)
         carriers = tile("carriers", M // LIST_ROWS, U16)
-        tab_w = sb.tile([P, T], I32, name="tab_w", tag="early_then_page1", align_bytes=64)
-        tab_s = sb.tile([P, T], U8, name="tab_s", tag="tab_s_then_wm_s", align_bytes=64)
+        tab_w = tile("tab_w", T, I32, "ends_as_page3")
+        tab_s = tile("tab_s", T, U8, "ends_as_wm_s")
         v_w = tile("v_w", S, U32)
         v_s = [tile("v_s0", SCALES_AHEAD, U8)]
-        first_squares = sb.tile([P, 2 * P], F32, name="first_squares", tag="squares_then_scales", align_bytes=64)
+        first_squares = tile("first_squares", 2 * P, F32, "ends_as_v_s1")
         wr_w = [tile("wr_w%d" % c0, 2 * width, U8) for c0, width in WR_PARTS]
         wr_s = tile("wr_s", H, U8)
         wq_w = [tile("wq_w%d" % c0, width, U32) for c0, width in WQ_PARTS]
@@ -67,9 +68,9 @@ def tile_list_pilot_envelope_reliability_kernel(
         nv_four = [tile("nv_four%d" % a, 4, F32) for a in (1, 2)]
         ident = tile("ident", P, F32)
         wgs_nat = tile("wgs_nat", S, F32)
-        wgs_four = sb.tile([P, 4 * S], F32, name="wgs_four", tag="run0", align_bytes=64)
+        wgs_four = tile("wgs_four", 4 * S, F32)
         pages = [tile("page%d" % i, T2, F32) for i in range(2)]
-        early = [sb.tile([P, M], F32, name="early0", tag="early_then_page0", align_bytes=64)]
+        before_page2 = tile("before_page2", M, F32, "ends_as_page2")
         env_a = tile("env_a", 4 * S, F32)
         env_b = tile("env_b", 4 * S, F32)
         err_a = tile("err_a", 4 * M, F32)
@@ -81,17 +82,15 @@ def tile_list_pilot_envelope_reliability_kernel(
         wq_first = tile("wq_first", 8 * P, BF16)
         z_rows = [tile("z_rows%d" % i, PASS, BF16) for i in range(2)]
         z_w = tile("z_w", M, U32)
-        z_s = [tile("z_s%d" % a, M, U8) for a in range(3)]
+        z_s = tile("z_s", M, U8)
+        z_early_s = tile("z_early_s", 2 * M, U8)
         banks = [ps.tile([P, PASS], F32, name="bank%d" % i) for i in range(8)]
 
         def load_scale_rows(plane, rows):
             for q in range(4):
                 nc.sync.dma_start(out=plane[32 * q : 32 * q + 4, :].bitcast(I32), in_=rows[4 * q : 4 * q + 4, :].bitcast(I32))
 
-        wq_raw = [
-            quarter(buf_c, 0), quarter(buf_c, 1),
-            quarter(buf_d, 0), quarter(buf_d, 1), buf_d[:, 2 * M : 4 * M],
-        ]
+        wq_raw = [quarter(buf_c, 0), quarter(buf_c, 1), quarter(buf_d, 0), quarter(buf_d, 1), buf_d[:, 2 * M : 4 * M]]
         wq_k = wq.rearrange("(p i) c -> p i c", i=4)
 
         def load_wq(load):
@@ -103,12 +102,12 @@ def tile_list_pilot_envelope_reliability_kernel(
             nc.sync.dma_start(out=wr_w[part][:].bitcast(I32), in_=wr_words[0][:, 2 * c0 : 2 * (c0 + width)].bitcast(I32))
 
         def interleave(engine_copy, dst, src):
-            engine_copy(out=dst.rearrange("p (c x i) -> p c i x", x=4, i=4), in_=src.rearrange("p (i c x) -> p c i x", i=4, x=4))
+            engine_copy(out=dst.rearrange("p (c x i) -> p c i x", x=4, i=4), in_=src.rearrange("p i (c x) -> p c i x", x=4))
 
         def quantise_wq(part, loads, rounded):
             for n, load in enumerate(loads):
                 width = 4 * WQ_LOADS[load][1]
-                interleave(nc.scalar.copy, rounded[:, width * n : width * (n + 1)], wq_raw[load])
+                interleave(nc.scalar.copy, rounded[:, width * n : width * (n + 1)], wq_raw[load].rearrange("p (i c) -> p i c", i=4))
             nc.vector.quantize_mx(out=wq_w[part][:].bitcast(E4M3), scales=wq_s[part][:], in_=rounded)
 
         warm = tile("warm", 2, F32)
@@ -211,11 +210,7 @@ def tile_list_pilot_envelope_reliability_kernel(
                 out=dst, in0=pages[page][:].indirect(entries(carriers, m0, width)), in1=quarter(errors, t, width, m0), op=ALU.add
             )
 
-        def quantise_z(a, m0, width, words, rounded):
-            nc.vector.quantize_mx(out=words.bitcast(E4M3), scales=z_s[a][:, m0 : m0 + width], in_=rounded)
-
         def turn_first_pass(z_nat, rounded):
-            pairs = rounded.bitcast(F32)
             for group in range(4):
                 bank_back = banks[6 + group % 2]
                 for i in range(2):
@@ -231,13 +226,14 @@ def tile_list_pilot_envelope_reliability_kernel(
                         nc.tensor.transpose(
                             bank_back[:, P * (2 * i + u) : P * (2 * i + u + 1)], z_rows[i][:].bitcast(F32)[:, P * u : P * (u + 1)], ident[:]
                         )
+                order = "p (a i m u) -> p a i m u" if CHUNKS[group][1] == WIDE else "p (i a m u) -> p a i m u"
                 nc.scalar.copy(
-                    out=pairs[:, PASS * group : PASS * (group + 1)].rearrange("p (i m u) -> p i m u", i=2, u=2),
+                    out=quarter(rounded, group).rearrange(order, a=2, i=2, u=2)[:, 0],
                     in_=bank_back[:].rearrange("p (i u m) -> p i m u", i=2, u=2),
                 )
 
         def late_page(tag):
-            page = sb.tile([P, T2], F32, name="page%d" % len(pages), tag=tag, align_bytes=64)
+            page = tile("page%d" % len(pages), T2, F32, tag)
             nc.gpsimd.memset(page[:], 0.0)
             pages.append(page)
 
@@ -249,15 +245,15 @@ def tile_list_pilot_envelope_reliability_kernel(
 
         gather_scales(v_s[0], 0, SCALES_AHEAD)
         quantise_wq(0, (0,), wq_first[:])
-        gather_words(0, 256)
-        gather_words(256, 768)
-        early.append(sb.tile([P, M], F32, name="early1", tag="early_then_page1", align_bytes=64))
+        gather_words(0, first_width)
+        gather_words(first_width, S - first_width)
+        before_page3 = tile("before_page3", M, F32, "ends_as_page3")
         steps = [(b, j0, width) for j0, width in FIRST_PIECES for b in (0, 1)]
         steps = steps + [(b, j0, PASS) for b in (2, 3) for j0 in (0, PASS)]
         end_of_tile_0, end_of_tile_1, end_of_tile_3 = 4, 5, 9
         squares = [
-            quarter(buf_b, 0), quarter(buf_b, 1), quarter(buf_b, 2), quarter(buf_b, 3), early[0][:],
-            early[1][:], quarter(buf_b, 0), quarter(buf_b, 1), quarter(buf_b, 2), quarter(buf_c, 3),
+            quarter(buf_b, 0), quarter(buf_b, 1), quarter(buf_b, 2), quarter(buf_b, 3), before_page2[:],
+            before_page3[:], quarter(buf_b, 0), quarter(buf_b, 1), quarter(buf_b, 2), quarter(buf_c, 3),
         ]
         z_nat = [quarter(buf_d, t) for t in range(4)]
         for step, (b, j0, width) in enumerate(steps):
@@ -266,9 +262,9 @@ def tile_list_pilot_envelope_reliability_kernel(
                 halves[0] = first_squares[:]
             envelope_rows(b, j0, width, banks[2 * (step % 2) : 2 * (step % 2) + 2], banks[4 + step % 2], halves)
             if step == 0:
-                v_s.append(sb.tile([P, S - SCALES_AHEAD], U8, name="v_s1", tag="squares_then_scales", align_bytes=64))
+                v_s.append(tile("v_s1", S - SCALES_AHEAD, U8, "ends_as_v_s1"))
                 gather_scales(v_s[1], SCALES_AHEAD, S - SCALES_AHEAD)
-                wm_s = sb.tile([P, 3 * N], U8, name="wm_s", tag="tab_s_then_wm_s", align_bytes=64)
+                wm_s = tile("wm_s", 3 * N, U8, "ends_as_wm_s")
                 nc.gpsimd.memset(wm_s[:].bitcast(I32), 0)
                 for q in range(4):
                     nc.sync.dma_start(
@@ -281,10 +277,10 @@ def tile_list_pilot_envelope_reliability_kernel(
                 scatter(b % 2, 0, S, quarter(env_a, b), wgs_nat[:])
             if step == end_of_tile_0:
                 quantise_wq(1, (1,), squares[step][:, 0:PASS].bitcast(BF16))
-                late_page("early_then_page0")
+                late_page("ends_as_page2")
             if step == end_of_tile_1:
                 quantise_wq(2, (2, 3), squares[step].bitcast(BF16))
-                late_page("early_then_page1")
+                late_page("ends_as_page3")
             if step == end_of_tile_3:
                 quantise_wq(3, (4,), squares[step].bitcast(BF16))
             if step in (end_of_tile_1, end_of_tile_3):
@@ -305,44 +301,53 @@ def tile_list_pilot_envelope_reliability_kernel(
         view = squares_of_pass(2, 0, buf_c)
         for t in range(4):
             envelope_four(2, t, view, quarter(env_a, t, PASS))
-        rounded_0 = buf_a[:, 2 * M : 4 * M].bitcast(BF16)
-        turn_first_pass(z_nat, rounded_0)
-        view = squares_of_pass(2, PASS, buf_c)
+        view = squares_of_pass(2, PASS, buf_a)
         for t in range(4):
             envelope_four(2, t, view, quarter(env_a, t, PASS, PASS))
             scatter(t, 0, S, quarter(env_a, t), quarter(wgs_four, t))
-        rounded_1 = buf_c[:, 0 : 2 * M].bitcast(BF16)
-        interleave(nc.scalar.copy, rounded_1, buf_b[:])
+        turn_first_pass(z_nat, buf_a)
+        rounded_early = buf_a[:].bitcast(BF16)
+        z_pass_1 = buf_b[:].rearrange("p (i m) -> p i m", i=4)
+        for m0, count, width in ((0, 3, WIDE), (CHUNKS[3][0], 2, NARROW)):
+            nc.scalar.copy(
+                out=rounded_early[:, 8 * m0 : 8 * (m0 + count * width)].rearrange("p (g a c x i) -> p a g c i x", g=count, a=2, x=4, i=4)[:, 1],
+                in_=z_pass_1[:, :, m0 : m0 + count * width].rearrange("p i (g c x) -> p g c i x", g=count, x=4),
+            )
 
-        shift = 768
-        picked = [buf_b[:, shift : shift + M], buf_b[:, 0:M], buf_b[:, shift : shift + M]]
-        narrow = buf_b[:, 256 : 256 + M]
-        rounded_2 = [sb.tile([P, 4 * width], BF16, name="rounded_2_%d" % c, tag="run%d" % (c + 1), align_bytes=64)[:] if c != 3 else None for c, (m0, width) in enumerate(CHUNKS)]
-        rounded_2[3] = buf_b[:, shift + 768 : shift + M].bitcast(BF16)
+        picked = [buf_b[:, WIDE * c : WIDE * c + 2 * M].rearrange("p (t m) -> p t m", t=4) for c in range(3)]
+        picked_narrow = buf_b[:, WIDE : WIDE + M].rearrange("p (t m) -> p t m", t=4)
+        rounded_2 = [tile("rounded_2_%d" % c, 4 * WIDE, BF16, "ends_as_run%d" % (c + 1))[:] for c in range(3)]
+        rounded_2.append(picked[2][:, 2, 0:WIDE].bitcast(BF16))
+        rounded_2.append(tile("rounded_2_4", 4 * NARROW, BF16)[:])
         runs = []
 
-        def z_words(a, m0, width):
+        def z_operand(a, c):
+            m0, width = CHUNKS[c]
             if a == 2:
-                return z_w[:, m0 : m0 + width]
-            run, col = divmod(m0, 256)
-            return runs[run][:, 256 * a + col : 256 * a + col + width]
+                return z_w[:, m0 : m0 + width], z_s[:, m0 : m0 + width]
+            run, col = divmod(m0, WIDE)
+            first = 2 * col + width * a
+            return runs[run][:, first : first + width], z_early_s[:, 2 * m0 + width * a : 2 * m0 + width * (a + 1)]
 
-        def early_pass(a, chunks):
-            m0 = CHUNKS[chunks[0]][0]
-            width = sum(CHUNKS[c][1] for c in chunks)
-            if len(runs) == m0 // 256:
-                runs.append(sb.tile([P, PASS], U32, name="z_early%d" % len(runs), tag="run%d" % len(runs), align_bytes=64))
-            quantise_z(a, m0, width, z_words(a, m0, width), (rounded_0, rounded_1)[a][:, 4 * m0 : 4 * (m0 + width)])
-            for c in chunks:
-                products(c, range(5), (a,))
+        def early_passes(c):
+            m0, width = CHUNKS[c]
+            run, col = divmod(m0, WIDE)
+            if len(runs) == run:
+                runs.append(tile("run%d" % run, 2 * WIDE, U32, "ends_as_run%d" % run))
+            nc.vector.quantize_mx(
+                out=runs[run][:, 2 * col : 2 * (col + width)].bitcast(E4M3), scales=z_early_s[:, 2 * m0 : 2 * (m0 + width)],
+                in_=rounded_early[:, 8 * m0 : 8 * (m0 + width)],
+            )
+            products(c, range(5), (0, 1))
 
         staged = [err_b[:, PASS * n : PASS * (n + 1)] for n in range(8)] + [buf_d[:, PASS * n : PASS * (n + 1)] for n in range(3)]
         out_n = out.rearrange("(i p) m -> p i m", p=P)
         open_banks = []
 
         def products(c, out_tiles, passes, closing=()):
-            m0, width = CHUNKS[c]
+            width = CHUNKS[c][1]
             for a in passes:
+                words, plane = z_operand(a, c)
                 for i in out_tiles:
                     bank, col = PLACES[c][i]
                     start = bank not in open_banks
@@ -354,7 +359,7 @@ def tile_list_pilot_envelope_reliability_kernel(
                     nc.tensor.matmul_mx(
                         out=banks[bank][:, col : col + width],
                         lhsT=wm_w[:, N * a + P * i : N * a + P * (i + 1)].bitcast(E4M3), lhsT_scale=wm_s[:, N * a + P * i : N * a + P * (i + 1)],
-                        rhs=z_words(a, m0, width).bitcast(E4M3), rhs_scale=z_s[a][:, m0 : m0 + width], start=start, stop=stop,
+                        rhs=words.bitcast(E4M3), rhs_scale=plane, start=start, stop=stop,
                     )
 
         def store(engine_copy, bank, i0, count, m0, width):
@@ -362,64 +367,59 @@ def tile_list_pilot_envelope_reliability_kernel(
             engine_copy(out=result, in_=banks[bank][:, 0 : count * width])
             nc.sync.dma_start(out=out_n[:, i0 : i0 + count, m0 : m0 + width], in_=result.rearrange("p (i m) -> p i m", i=count))
 
-        def gather_chunk(c, row_tiles):
-            m0, width = CHUNKS[c]
-            for t in row_tiles:
-                gather(t, t, m0, width, picked[c][:, width * t : width * (t + 1)], err_a)
+        def gather_wide(t, c, count=1):
+            gather(t, t, CHUNKS[c][0], count * WIDE, picked[c][:, t, 0 : count * WIDE], err_a)
 
-        def gather_narrow(t, m0, width):
-            col = 256 * t + m0 - CHUNKS[3][0]
-            gather(t, t, m0, width, narrow[:, col : col + width], err_a)
+        def gather_narrow(t, c, count=1):
+            col = NARROW * (c - 3)
+            gather(t, t, CHUNKS[c][0], count * NARROW, picked_narrow[:, t, col : col + count * NARROW], err_a)
 
-        def round_chunk(c, engine_copy):
-            interleave(engine_copy, rounded_2[c], picked[c])
+        def round_wide(c):
+            interleave(nc.scalar.copy, rounded_2[c], picked[c][:, :, 0:WIDE])
 
         def round_narrow(c):
-            nc.vector.tensor_copy(
-                out=rounded_2[c].rearrange("p (c x i) -> p c i x", x=4, i=4),
-                in_=narrow.rearrange("p (i h c x) -> p h c i x", i=4, h=2, x=4)[:, c - 3],
-            )
+            interleave(nc.vector.tensor_copy, rounded_2[c], picked_narrow[:, :, NARROW * (c - 3) : NARROW * (c - 2)])
 
         def last_pass(c, closing, out_tiles=range(5)):
-            m0, width = CHUNKS[c]
-            quantise_z(2, m0, width, z_words(2, m0, width), rounded_2[c])
+            words, plane = z_operand(2, c)
+            nc.vector.quantize_mx(out=words.bitcast(E4M3), scales=plane, in_=rounded_2[c])
             products(c, out_tiles, (2,), closing)
 
-        gather_chunk(0, range(4))
-        round_chunk(0, nc.scalar.copy)
-        early_pass(0, (0,))
-        early_pass(1, (0,))
-        gather_chunk(1, (0, 1, 2))
+        gather_wide(0, 0, 2)
+        gather_wide(1, 0, 2)
+        gather_wide(2, 0)
+        gather_wide(3, 0)
+        round_wide(0)
+        early_passes(0)
+        gather_wide(2, 1)
+        gather_wide(3, 1, 2)
+        round_wide(1)
         last_pass(0, (1, 3))
-        gather_chunk(1, (3,))
-        round_chunk(1, nc.scalar.copy)
         store(nc.scalar.copy, 0, 0, 2, 0, 256)
         store(nc.scalar.copy, 1, 2, 2, 0, 256)
-        early_pass(0, (1,))
-        early_pass(1, (1,))
-        gather_chunk(2, (1, 2, 3))
+        gather_wide(0, 2)
+        early_passes(1)
+        gather_wide(1, 2)
+        gather_wide(2, 2)
+        round_wide(2)
         last_pass(1, (1, 3, 4))
-        gather_chunk(2, (0,))
-        round_chunk(2, nc.scalar.copy)
         store(nc.scalar.copy, 3, 0, 2, 256, 256)
         store(nc.scalar.copy, 4, 2, 2, 256, 256)
         store(nc.scalar.copy, 2, 4, 1, 0, 512)
-        gather_narrow(0, 768, 256)
-        gather_narrow(1, 768, 256)
-        early_pass(0, (2,))
-        early_pass(1, (2,))
+        gather_narrow(0, 3, 2)
+        early_passes(2)
+        gather_narrow(2, 3, 2)
         last_pass(2, (1, 3))
         store(nc.scalar.copy, 5, 0, 2, 512, 256)
         store(nc.scalar.copy, 6, 2, 2, 512, 256)
-        gather_narrow(2, 768, 128)
-        gather_narrow(3, 768, 128)
-        early_pass(0, (3, 4))
+        gather_narrow(1, 3)
+        gather_narrow(3, 3)
+        early_passes(3)
         round_narrow(3)
-        early_pass(1, (3,))
+        gather_narrow(1, 4)
         last_pass(3, (3, 4), (4, 0, 1, 2, 3))
-        gather_narrow(2, 896, 128)
-        gather_narrow(3, 896, 128)
-        early_pass(1, (4,))
+        gather_narrow(3, 4)
+        early_passes(4)
         round_narrow(4)
         last_pass(4, (2, 4))
         store(nc.scalar.copy, 7, 4, 1, 512, 384)

@@ -70,7 +70,7 @@ def tile_list_pilot_envelope_reliability_kernel(
         wgs_nat = tile("wgs_nat", S, F32)
         wgs_four = tile("wgs_four", 4 * S, F32)
         pages = [tile("page%d" % i, T2, F32) for i in range(2)]
-        before_page2 = tile("before_page2", M, F32, "ends_as_page2")
+        before_page2 = tile("before_page2", 2 * M, F32, "ends_as_page2")
         env_a = tile("env_a", 4 * S, F32)
         env_b = tile("env_b", 4 * S, F32)
         err_a = tile("err_a", 4 * M, F32)
@@ -174,15 +174,16 @@ def tile_list_pilot_envelope_reliability_kernel(
             nc.tensor.matmul(out=dst, lhsT=second, rhs=ident[:], is_transpose=True, start=False, stop=True)
 
         def envelope_rows(b, j0, width, product_banks, bank_sum, squares):
-            per_bank = width // (2 * P)
+            per_bank = width // (len(product_banks) * P)
+            used = 2 * P * per_bank
             for n, bank in enumerate(product_banks):
                 for i in range(per_bank):
                     first_products(
                         bank[:, 2 * P * i : 2 * P * i + P], bank[:, 2 * P * i + P : 2 * P * (i + 1)], j0 + P * (per_bank * n + i), P * b, P
                     )
-                nc.scalar.activation(out=squares[n], in_=bank[:, 0:width], func=ACT.Square)
+                nc.scalar.activation(out=squares[n], in_=bank[:, 0:used], func=ACT.Square)
             for i in range(width // P):
-                n, c = divmod(2 * P * i, width)
+                n, c = divmod(2 * P * i, used)
                 add_turned(bank_sum[:, P * i : P * (i + 1)], squares[n][:, c : c + P], squares[n][:, c + P : c + 2 * P])
             bias = nv_first[:, b : b + 1] if b < 2 else nv_nat[:, b - 2 : b - 1]
             nc.scalar.activation(out=quarter(env_a, b, width, j0), in_=bank_sum[:, 0:width], func=ACT.Sqrt, bias=bias)
@@ -248,44 +249,60 @@ def tile_list_pilot_envelope_reliability_kernel(
         gather_words(0, first_width)
         gather_words(first_width, S - first_width)
         before_page3 = tile("before_page3", M, F32, "ends_as_page3")
-        steps = [(b, j0, width) for j0, width in FIRST_PIECES for b in (0, 1)]
-        steps = steps + [(b, j0, PASS) for b in (2, 3) for j0 in (0, PASS)]
-        end_of_tile_0, end_of_tile_1, end_of_tile_3 = 4, 5, 9
-        squares = [
-            quarter(buf_b, 0), quarter(buf_b, 1), quarter(buf_b, 2), quarter(buf_b, 3), before_page2[:],
-            before_page3[:], quarter(buf_b, 0), quarter(buf_b, 1), quarter(buf_b, 2), quarter(buf_c, 3),
-        ]
+
+        def both_tiles(block, bank, dst):
+            first_products(bank[:, 0 : 2 * P], bank[:, 2 * P : 4 * P], P * block, 0, 2 * P)
+            nc.scalar.activation(out=dst, in_=bank[:].rearrange("j (h t p) -> j h t p", h=2, t=2), func=ACT.Square)
+
+        def envelope_piece(b, block0, views, bank_sum):
+            j0, width = P * block0, P * len(views)
+            for i, view in enumerate(views):
+                add_turned(bank_sum[:, P * i : P * (i + 1)], view[:, 0, b, :], view[:, 1, b, :])
+            nc.scalar.activation(out=quarter(env_a, b, width, j0), in_=bank_sum[:, 0:width], func=ACT.Sqrt, bias=nv_first[:, b : b + 1])
+            scatter(b, j0, width, quarter(env_a, b, width, j0), wgs_nat[:, j0 : j0 + width])
+
+        envelope_rows(0, 0, first_width, banks[0:2], banks[3], [first_squares[:], quarter(buf_b, 0, first_width)])
+        v_s.append(tile("v_s1", S - SCALES_AHEAD, U8, "ends_as_v_s1"))
+        gather_scales(v_s[1], SCALES_AHEAD, S - SCALES_AHEAD)
+        wm_s = tile("wm_s", 3 * N, U8, "ends_as_wm_s")
+        nc.gpsimd.memset(wm_s[:].bitcast(I32), 0)
+        for q in range(4):
+            nc.sync.dma_start(
+                out=wm_s[32 * q : 32 * q + 4, :].bitcast(I32).rearrange("p (a c) -> p a c", a=3),
+                in_=wm_scales[:, 4 * q : 4 * q + 4, :].rearrange("a r c -> r a c").bitcast(I32),
+            )
+        scatter(0, 0, first_width, quarter(env_a, 0, first_width), wgs_nat[:, 0:first_width])
+        envelope_rows(1, 0, first_width, banks[2:3], banks[4], [quarter(buf_b, 1, 2 * first_width)])
+        scatter(1, 0, first_width, quarter(env_a, 1, first_width), wgs_nat[:, 0:first_width])
+
+        early = before_page3[:].rearrange("j (i h t p) -> j i h t p", i=2, h=2, t=2)
+        late = before_page2[:].rearrange("j (t i h p) -> j i h t p", t=2, i=4, h=2)
+        views = {block: early[:, block - 2] if block < 4 else late[:, block - 4] for block in range(2, 8)}
+        for block in (2, 3, 4):
+            both_tiles(block, banks[block], views[block])
+        for b in (0, 1):
+            envelope_piece(b, 2, [views[2], views[3]], banks[2 + b])
+        for block, bank in ((5, 4), (6, 2), (7, 3)):
+            both_tiles(block, banks[bank], views[block])
+        envelope_piece(0, 4, [views[block] for block in range(4, 8)], banks[4])
+        quantise_wq(1, (1,), before_page2[:, PASS:M].bitcast(BF16))
+        envelope_piece(1, 4, [views[block] for block in range(4, 8)], banks[3])
+        quantise_wq(2, (2, 3), before_page2[:, M : 2 * M].bitcast(BF16))
+        late_page("ends_as_page2")
+        late_page("ends_as_page3")
         z_nat = [quarter(buf_d, t) for t in range(4)]
-        for step, (b, j0, width) in enumerate(steps):
-            halves = [squares[step][:, width * n : width * (n + 1)] for n in range(2)]
-            if step == 0:
-                halves[0] = first_squares[:]
-            envelope_rows(b, j0, width, banks[2 * (step % 2) : 2 * (step % 2) + 2], banks[4 + step % 2], halves)
-            if step == 0:
-                v_s.append(tile("v_s1", S - SCALES_AHEAD, U8, "ends_as_v_s1"))
-                gather_scales(v_s[1], SCALES_AHEAD, S - SCALES_AHEAD)
-                wm_s = tile("wm_s", 3 * N, U8, "ends_as_wm_s")
-                nc.gpsimd.memset(wm_s[:].bitcast(I32), 0)
-                for q in range(4):
-                    nc.sync.dma_start(
-                        out=wm_s[32 * q : 32 * q + 4, :].bitcast(I32).rearrange("p (a c) -> p a c", a=3),
-                        in_=wm_scales[:, 4 * q : 4 * q + 4, :].rearrange("a r c -> r a c").bitcast(I32),
-                    )
-            if b < 2:
-                scatter(b, j0, width, quarter(env_a, b, width, j0), wgs_nat[:, j0 : j0 + width])
-            elif j0 > 0:
+        for b in (0, 1):
+            gather(b, b, 0, M, z_nat[b], err_a)
+
+        squares = [quarter(buf_b, 0), quarter(buf_b, 1), quarter(buf_b, 2), quarter(buf_c, 3)]
+        for step, (b, j0) in enumerate((b, j0) for b in (2, 3) for j0 in (0, PASS)):
+            halves = [squares[step][:, PASS * n : PASS * (n + 1)] for n in range(2)]
+            envelope_rows(b, j0, PASS, banks[2 * (step % 2) : 2 * (step % 2) + 2], banks[4 + step % 2], halves)
+            if j0 > 0:
                 scatter(b % 2, 0, S, quarter(env_a, b), wgs_nat[:])
-            if step == end_of_tile_0:
-                quantise_wq(1, (1,), squares[step][:, 0:PASS].bitcast(BF16))
-                late_page("ends_as_page2")
-            if step == end_of_tile_1:
-                quantise_wq(2, (2, 3), squares[step].bitcast(BF16))
-                late_page("ends_as_page3")
-            if step == end_of_tile_3:
-                quantise_wq(3, (4,), squares[step].bitcast(BF16))
-            if step in (end_of_tile_1, end_of_tile_3):
-                gather(0, b - 1, 0, M, z_nat[b - 1], err_a)
-                gather(1, b, 0, M, z_nat[b], err_a)
+        quantise_wq(3, (4,), squares[3].bitcast(BF16))
+        for b in (2, 3):
+            gather(b % 2, b, 0, M, z_nat[b], err_a)
 
         for j0, buf in ((0, buf_a), (PASS, buf_b)):
             view = squares_of_pass(1, j0, buf)

@@ -70,15 +70,14 @@ def tile_list_pilot_envelope_reliability_kernel(
         wgs_nat = tile("wgs_nat", S, F32)
         wgs_four = tile("wgs_four", 4 * S, F32)
         pages = [tile("page%d" % i, T2, F32) for i in range(2)]
-        before_page2 = tile("before_page2", 2 * M, F32, "ends_as_page2")
-        env_a = tile("env_a", 4 * S, F32)
-        env_b = tile("env_b", 4 * S, F32)
+        before_page2 = tile("before_page2", PASS, F32, "ends_as_page2")
+        env = tile("env", 4 * S, F32)
         err_a = tile("err_a", 4 * M, F32)
         err_b = tile("err_b", 4 * M, F32)
-        buf_a = tile("buf_a", 4 * M, F32)
-        buf_b = tile("buf_b", 4 * M, F32)
-        buf_c = tile("buf_c", 4 * M, F32)
-        buf_d = tile("buf_d", 4 * M, F32)
+        sq_nat = tile("sq_nat", 4 * S, F32)
+        sq = tile("sq", 16 * S, F32)
+        im_1, re_1, re_2, im_2 = (sq[:, 4 * S * n : 4 * S * (n + 1)] for n in range(4))
+        z_late = sq[:, 6 * S : 10 * S]
         wq_first = tile("wq_first", 8 * P, BF16)
         z_rows = [tile("z_rows%d" % i, PASS, BF16) for i in range(2)]
         z_w = tile("z_w", M, U32)
@@ -90,7 +89,7 @@ def tile_list_pilot_envelope_reliability_kernel(
             for q in range(4):
                 nc.sync.dma_start(out=plane[32 * q : 32 * q + 4, :].bitcast(I32), in_=rows[4 * q : 4 * q + 4, :].bitcast(I32))
 
-        wq_raw = [quarter(buf_c, 0), quarter(buf_c, 1), quarter(buf_d, 0), quarter(buf_d, 1), buf_d[:, 2 * M : 4 * M]]
+        wq_raw = [quarter(env, 2), quarter(env, 3), quarter(re_2, 0), quarter(re_2, 1), re_2[:, 2 * M : 4 * M]]
         wq_k = wq.rearrange("(p i) c -> p i c", i=4)
 
         def load_wq(load):
@@ -104,10 +103,13 @@ def tile_list_pilot_envelope_reliability_kernel(
         def interleave(engine_copy, dst, src):
             engine_copy(out=dst.rearrange("p (c x i) -> p c i x", x=4, i=4), in_=src.rearrange("p i (c x) -> p c i x", x=4))
 
-        def quantise_wq(part, loads, rounded):
-            for n, load in enumerate(loads):
-                width = 4 * WQ_LOADS[load][1]
-                interleave(nc.scalar.copy, rounded[:, width * n : width * (n + 1)], wq_raw[load].rearrange("p (i c) -> p i c", i=4))
+        def quantise_wq(part, loads, rounded, step):
+            done = 0
+            for load in loads:
+                raw = wq_raw[load].rearrange("p (i c) -> p i c", i=4)
+                for c0 in range(0, WQ_LOADS[load][1], step):
+                    interleave(nc.scalar.copy, rounded[:, 4 * done : 4 * (done + step)], raw[:, :, c0 : c0 + step])
+                    done = done + step
             nc.vector.quantize_mx(out=wq_w[part][:].bitcast(E4M3), scales=wq_s[part][:], in_=rounded)
 
         warm = tile("warm", 2, F32)
@@ -131,18 +133,31 @@ def tile_list_pilot_envelope_reliability_kernel(
         load_wr(1)
         with nc.allow_non_contiguous_dma(reason="one noise power a partition"):
             nc.sync.dma_start(out=nv_nat[:], in_=nv[2 * P : PASS].rearrange("(b p) -> p b", p=P))
+        nc.sync.dma_start(carriers[:], offs3)
+        err_nat = err[0:PASS, :].rearrange("(t p) m -> p t m", p=P)
+        err_four = err[PASS : 2 * PASS, :].rearrange("(p t) m -> p (t m)", t=4)
+        wgs_rows = wgs.rearrange("(r t) j -> r (t j)", t=4)
+
+        def load_err_nat(t0):
+            nc.sync.dma_start(out=err_a[:, M * t0 : M * (t0 + 2)].rearrange("p (t m) -> p t m", t=2), in_=err_nat[:, t0 : t0 + 2, :])
+
+        def load_wgs_four(t0):
+            for q in range(4):
+                nc.sync.dma_start(out=wgs_four[32 * q : 32 * q + 32, S * t0 : S * (t0 + 2)], in_=wgs_rows[:, S * t0 : S * (t0 + 2)])
+
+        load_err_nat(0)
         for load in (2, 3):
             load_wq(load)
-        nc.sync.dma_start(carriers[:], offs3)
-        nc.sync.dma_start(out=err_a[:].rearrange("p (t m) -> p t m", t=4), in_=err[0:PASS, :].rearrange("(t p) m -> p t m", p=P))
         load_wr(2)
         for a in (1, 2):
             nc.sync.dma_start(out=nv_four[a - 1][:], in_=nv[PASS * a : PASS * (a + 1)].rearrange("(p t) -> p t", t=4))
+        load_wgs_four(0)
+        load_err_nat(2)
         load_wq(4)
-        for q in range(4):
-            nc.sync.dma_start(out=wgs_four[32 * q : 32 * q + 32, :], in_=wgs.rearrange("(r t) j -> r (t j)", t=4))
+        load_wgs_four(2)
+        nc.sync.dma_start(out=err_b[:, 0 : 2 * M], in_=err_four[:, 0 : 2 * M])
         load_wr(3)
-        nc.sync.dma_start(out=err_b[:], in_=err[PASS : 2 * PASS, :].rearrange("(p t) m -> p (t m)", t=4))
+        nc.sync.dma_start(out=err_b[:, 2 * M : 4 * M], in_=err_four[:, 2 * M : 4 * M])
         nc.sync.dma_start(out=wm_w[:].rearrange("p (a c) -> p a c", a=3), in_=wm_words.rearrange("a p c i -> p a (c i)").bitcast(I32))
         make_identity(nc, ident[:])
         for page in pages:
@@ -185,23 +200,25 @@ def tile_list_pilot_envelope_reliability_kernel(
             for i in range(width // P):
                 n, c = divmod(2 * P * i, used)
                 add_turned(bank_sum[:, P * i : P * (i + 1)], squares[n][:, c : c + P], squares[n][:, c + P : c + 2 * P])
-            bias = nv_first[:, b : b + 1] if b < 2 else nv_nat[:, b - 2 : b - 1]
-            nc.scalar.activation(out=quarter(env_a, b, width, j0), in_=bank_sum[:, 0:width], func=ACT.Sqrt, bias=bias)
+            nc.scalar.activation(out=quarter(env, b, width, j0), in_=bank_sum[:, 0:width], func=ACT.Sqrt, bias=nv_first[:, b : b + 1])
 
-        def squares_of_pass(a, j0, buf):
-            view = buf[:].rearrange("j (i h t p) -> j i h t p", i=4, h=2, t=4)
-            for i in range(4):
-                bank_re, bank_im = banks[2 * (i % 2)], banks[2 * (i % 2) + 1]
-                first_products(bank_re[:], bank_im[:], j0 + P * i, PASS * a, PASS)
-                for half, bank in enumerate((bank_re, bank_im)):
-                    nc.scalar.activation(out=view[:, i, half, :, :], in_=bank[:].rearrange("j (p t) -> j t p", t=4), func=ACT.Square)
-            return view
+        product_banks = [banks[n] for n in (0, 1, 2, 4)]
 
-        def envelope_four(a, t, view, dst):
-            bank_sum = banks[4 + t % 2]
-            for i in range(4):
-                add_turned(bank_sum[:, P * i : P * (i + 1)], view[:, i, 0, t, :], view[:, i, 1, t, :])
-            nc.scalar.activation(out=dst, in_=bank_sum[:], func=ACT.Sqrt, bias=nv_four[a - 1][:, t : t + 1])
+        def squares_of_block(a, block, halves):
+            pair = product_banks[2:4] if block % 2 == 0 else product_banks[0:2]
+            first_products(pair[0][:], pair[1][:], P * block, PASS * a, PASS)
+            for half, bank in zip(halves, pair):
+                nc.scalar.activation(
+                    out=half.rearrange("j (t i p) -> j i t p", t=4, p=P)[:, block],
+                    in_=bank[:].rearrange("j (p t) -> j t p", t=4), func=ACT.Square,
+                )
+
+        def envelope(b, j0, squares_re, squares_im, bank_sum):
+            width = squares_re.shape[1]
+            for c in range(0, width, P):
+                add_turned(bank_sum[:, c : c + P], squares_re[:, c : c + P], squares_im[:, c : c + P])
+            bias = nv_nat[:, b - 2 : b - 1] if b < 4 else nv_four[b // 4 - 1][:, b % 4 : b % 4 + 1]
+            nc.scalar.activation(out=quarter(env, b % 4, width, j0), in_=bank_sum[:, 0:width], func=ACT.Sqrt, bias=bias)
 
         def scatter(page, j0, width, values, weights):
             nc.vector.tensor_tensor(out=pages[page][:].indirect(entries(slots, j0, width)), in0=values, in1=weights, op=ALU.mult)
@@ -215,10 +232,9 @@ def tile_list_pilot_envelope_reliability_kernel(
             for group in range(4):
                 bank_back = banks[6 + group % 2]
                 for i in range(2):
-                    m0 = 2 * P * group + P * i
                     bank_in = banks[4 + i]
                     for t in range(4):
-                        nc.tensor.transpose(bank_in[:, P * t : P * (t + 1)], z_nat[t][:, m0 : m0 + P], ident[:])
+                        nc.tensor.transpose(bank_in[:, P * t : P * (t + 1)], z_nat(t, group)[:, P * i : P * (i + 1)], ident[:])
                     nc.scalar.copy(
                         out=z_rows[i][:].rearrange("m (u p e) -> m u p e", u=2, e=2),
                         in_=bank_in[:].rearrange("m (p u e) -> m u p e", u=2, e=2),
@@ -245,23 +261,23 @@ def tile_list_pilot_envelope_reliability_kernel(
             nc.vector.tensor_copy(out=v_w[:, j0 : j0 + width], in_=tab_w[:].bitcast(U32).indirect(entries(pilots, j0, width)))
 
         gather_scales(v_s[0], 0, SCALES_AHEAD)
-        quantise_wq(0, (0,), wq_first[:])
+        quantise_wq(0, (0,), wq_first[:], 2 * P)
         gather_words(0, first_width)
         gather_words(first_width, S - first_width)
-        before_page3 = tile("before_page3", M, F32, "ends_as_page3")
+        before_page3 = tile("before_page3", PASS, F32, "ends_as_page3")
 
-        def both_tiles(block, bank, dst):
-            first_products(bank[:, 0 : 2 * P], bank[:, 2 * P : 4 * P], P * block, 0, 2 * P)
+        def both_tiles(block, bank, dst, c0=0):
+            first_products(bank[:, 0 : 2 * P], bank[:, 2 * P : 4 * P], P * block, c0, 2 * P)
             nc.scalar.activation(out=dst, in_=bank[:].rearrange("j (h t p) -> j h t p", h=2, t=2), func=ACT.Square)
 
         def envelope_piece(b, block0, views, bank_sum):
             j0, width = P * block0, P * len(views)
             for i, view in enumerate(views):
                 add_turned(bank_sum[:, P * i : P * (i + 1)], view[:, 0, b, :], view[:, 1, b, :])
-            nc.scalar.activation(out=quarter(env_a, b, width, j0), in_=bank_sum[:, 0:width], func=ACT.Sqrt, bias=nv_first[:, b : b + 1])
-            scatter(b, j0, width, quarter(env_a, b, width, j0), wgs_nat[:, j0 : j0 + width])
+            nc.scalar.activation(out=quarter(env, b, width, j0), in_=bank_sum[:, 0:width], func=ACT.Sqrt, bias=nv_first[:, b : b + 1])
+            scatter(b, j0, width, quarter(env, b, width, j0), wgs_nat[:, j0 : j0 + width])
 
-        envelope_rows(0, 0, first_width, banks[0:2], banks[3], [first_squares[:], quarter(buf_b, 0, first_width)])
+        envelope_rows(0, 0, first_width, banks[0:2], banks[3], [first_squares[:], im_2[:, 0:first_width]])
         v_s.append(tile("v_s1", S - SCALES_AHEAD, U8, "ends_as_v_s1"))
         gather_scales(v_s[1], SCALES_AHEAD, S - SCALES_AHEAD)
         wm_s = tile("wm_s", 3 * N, U8, "ends_as_wm_s")
@@ -271,68 +287,79 @@ def tile_list_pilot_envelope_reliability_kernel(
                 out=wm_s[32 * q : 32 * q + 4, :].bitcast(I32).rearrange("p (a c) -> p a c", a=3),
                 in_=wm_scales[:, 4 * q : 4 * q + 4, :].rearrange("a r c -> r a c").bitcast(I32),
             )
-        scatter(0, 0, first_width, quarter(env_a, 0, first_width), wgs_nat[:, 0:first_width])
-        envelope_rows(1, 0, first_width, banks[2:3], banks[4], [quarter(buf_b, 1, 2 * first_width)])
-        scatter(1, 0, first_width, quarter(env_a, 1, first_width), wgs_nat[:, 0:first_width])
+        scatter(0, 0, first_width, quarter(env, 0, first_width), wgs_nat[:, 0:first_width])
+        envelope_rows(1, 0, first_width, banks[2:3], banks[4], [im_2[:, PASS:M]])
+        scatter(1, 0, first_width, quarter(env, 1, first_width), wgs_nat[:, 0:first_width])
 
-        early = before_page3[:].rearrange("j (i h t p) -> j i h t p", i=2, h=2, t=2)
-        late = before_page2[:].rearrange("j (t i h p) -> j i h t p", t=2, i=4, h=2)
-        views = {block: early[:, block - 2] if block < 4 else late[:, block - 4] for block in range(2, 8)}
+        late_squares = im_2[:, M : 3 * M]
+        late = late_squares.rearrange("j (t i h p) -> j i h t p", t=2, i=4, h=2)
+        views = {block: late[:, block - 4] for block in range(4, 8)}
+        for block, early in ((2, before_page3), (3, before_page2)):
+            views[block] = early[:].rearrange("j (h t p) -> j h t p", h=2, t=2)
         for block in (2, 3, 4):
             both_tiles(block, banks[block], views[block])
         for b in (0, 1):
             envelope_piece(b, 2, [views[2], views[3]], banks[2 + b])
+        late_page("ends_as_page2")
+        late_page("ends_as_page3")
         for block, bank in ((5, 4), (6, 2), (7, 3)):
             both_tiles(block, banks[bank], views[block])
         envelope_piece(0, 4, [views[block] for block in range(4, 8)], banks[4])
-        quantise_wq(1, (1,), before_page2[:, PASS:M].bitcast(BF16))
+        quantise_wq(1, (1,), late_squares[:, PASS:M].bitcast(BF16), 2 * P)
         envelope_piece(1, 4, [views[block] for block in range(4, 8)], banks[3])
-        quantise_wq(2, (2, 3), before_page2[:, M : 2 * M].bitcast(BF16))
-        late_page("ends_as_page2")
-        late_page("ends_as_page3")
-        z_nat = [quarter(buf_d, t) for t in range(4)]
-        for b in (0, 1):
-            gather(b, b, 0, M, z_nat[b], err_a)
 
-        squares = [quarter(buf_b, 0), quarter(buf_b, 1), quarter(buf_b, 2), quarter(buf_c, 3)]
-        for step, (b, j0) in enumerate((b, j0) for b in (2, 3) for j0 in (0, PASS)):
-            halves = [squares[step][:, PASS * n : PASS * (n + 1)] for n in range(2)]
-            envelope_rows(b, j0, PASS, banks[2 * (step % 2) : 2 * (step % 2) + 2], banks[4 + step % 2], halves)
-            if j0 > 0:
-                scatter(b % 2, 0, S, quarter(env_a, b), wgs_nat[:])
-        quantise_wq(3, (4,), squares[3].bitcast(BF16))
-        for b in (2, 3):
-            gather(b % 2, b, 0, M, z_nat[b], err_a)
+        def squares_at(b, piece):
+            if b < 4:
+                c = WIDE * (2 * piece + b - 2)
+                return sq_nat[:, c : c + WIDE], sq_nat[:, 2 * S + c : 2 * S + c + WIDE]
+            halves = (re_1, im_1) if b < 8 else (re_2, im_2)
+            return tuple(quarter(half, b % 4, WIDE, WIDE * piece) for half in halves)
 
-        for j0, buf in ((0, buf_a), (PASS, buf_b)):
-            view = squares_of_pass(1, j0, buf)
-            for t in range(4):
-                envelope_four(1, t, view, quarter(env_b, t, PASS, j0))
-        for pair in ((0, 1), (2, 3)):
-            for t in pair:
-                scatter(t % 2, 0, S, quarter(env_b, t), quarter(wgs_four, t))
-            for t in pair:
-                gather(t % 2, t, 0, M, quarter(buf_b, t), err_b)
+        def z_nat(b, piece):
+            return squares_at(b + 2, piece)[0]
+
+        nat = sq_nat[:].rearrange("j (h q t i p) -> j q i h t p", h=2, q=4, t=2, i=2)
+
+        def squares_of_piece(b, piece):
+            for block in (2 * piece, 2 * piece + 1):
+                if b == 2:
+                    both_tiles(block, product_banks[block % 4], nat[:, piece, block % 2], 2 * P)
+                else:
+                    squares_of_block(b // 4, block, (re_1, im_1) if b == 4 else (re_2, im_2))
+
+        def woven(pair, after_first=None):
+            for piece in range(4):
+                j0 = WIDE * piece
+                if pair[0] in (2, 4, 8):
+                    squares_of_piece(pair[0], piece)
+                for b in pair:
+                    envelope(b, j0, *squares_at(b, piece), banks[3])
+                    gather((b - 2) % 4, (b - 2) % 4, j0, WIDE, z_nat(b - 2, piece), err_b if 4 <= b - 2 < 8 else err_a)
+                    weights = wgs_nat[:, j0 : j0 + WIDE] if b < 4 else quarter(wgs_four, b % 4, WIDE, j0)
+                    scatter(b % 4, j0, WIDE, quarter(env, b % 4, WIDE, j0), weights)
+                    if after_first and piece == 0 and b == pair[0]:
+                        after_first()
+
+        woven((2, 3), lambda: quantise_wq(2, (2, 3), late_squares[:, M : 2 * M].bitcast(BF16), P))
+        woven((4, 5), lambda: quantise_wq(3, (4,), sq_nat[:, 3 * S : 4 * S].bitcast(BF16), P))
         nc.sync.dma_start(out=err_a[:], in_=err[2 * PASS : 3 * PASS, :].rearrange("(p t) m -> p (t m)", t=4))
-
-        view = squares_of_pass(2, 0, buf_c)
-        for t in range(4):
-            envelope_four(2, t, view, quarter(env_a, t, PASS))
-        view = squares_of_pass(2, PASS, buf_a)
-        for t in range(4):
-            envelope_four(2, t, view, quarter(env_a, t, PASS, PASS))
-            scatter(t, 0, S, quarter(env_a, t), quarter(wgs_four, t))
-        turn_first_pass(z_nat, buf_a)
-        rounded_early = buf_a[:].bitcast(BF16)
-        z_pass_1 = buf_b[:].rearrange("p (i m) -> p i m", i=4)
+        woven((6, 7))
+        woven((8, 9))
+        for b in (10, 11):
+            for j0, bank in ((0, 3), (PASS, 5)):
+                envelope(b, j0, quarter(re_2, b % 4, PASS, j0), quarter(im_2, b % 4, PASS, j0), banks[bank])
+            scatter(b % 4, 0, S, quarter(env, b % 4), quarter(wgs_four, b % 4))
+        turn_first_pass(z_nat, im_2)
+        rounded_early = im_2.bitcast(BF16)
+        z_pass_1 = z_late.rearrange("p (i m) -> p i m", i=4)
         for m0, count, width in ((0, 3, WIDE), (CHUNKS[3][0], 2, NARROW)):
             nc.scalar.copy(
                 out=rounded_early[:, 8 * m0 : 8 * (m0 + count * width)].rearrange("p (g a c x i) -> p a g c i x", g=count, a=2, x=4, i=4)[:, 1],
                 in_=z_pass_1[:, :, m0 : m0 + count * width].rearrange("p i (g c x) -> p g c i x", g=count, x=4),
             )
 
-        picked = [buf_b[:, WIDE * c : WIDE * c + 2 * M].rearrange("p (t m) -> p t m", t=4) for c in range(3)]
-        picked_narrow = buf_b[:, WIDE : WIDE + M].rearrange("p (t m) -> p t m", t=4)
+        picked = [z_late[:, WIDE * c : WIDE * c + 2 * M].rearrange("p (t m) -> p t m", t=4) for c in range(3)]
+        picked_narrow = z_late[:, WIDE : WIDE + M].rearrange("p (t m) -> p t m", t=4)
         rounded_2 = [tile("rounded_2_%d" % c, 4 * WIDE, BF16, "ends_as_run%d" % (c + 1))[:] for c in range(3)]
         rounded_2.append(picked[2][:, 2, 0:WIDE].bitcast(BF16))
         rounded_2.append(tile("rounded_2_4", 4 * NARROW, BF16)[:])
@@ -357,7 +384,7 @@ def tile_list_pilot_envelope_reliability_kernel(
             )
             products(c, range(5), (0, 1))
 
-        staged = [err_b[:, PASS * n : PASS * (n + 1)] for n in range(8)] + [buf_d[:, PASS * n : PASS * (n + 1)] for n in range(3)]
+        staged = [err_b[:, PASS * n : PASS * (n + 1)] for n in range(8)] + [im_1[:, PASS * n : PASS * (n + 1)] for n in range(3)]
         out_n = out.rearrange("(i p) m -> p i m", p=P)
         open_banks = []
 

@@ -266,14 +266,17 @@ def tile_list_pilot_envelope_reliability_kernel(
         gather_words(first_width, S - first_width)
         before_page3 = tile("before_page3", PASS, F32, "ends_as_page3")
 
-        def both_tiles(block, bank, dst, c0=0):
-            first_products(bank[:, 0 : 2 * P], bank[:, 2 * P : 4 * P], P * block, c0, 2 * P)
+        def both_tiles(block, bank, dst, c0=0, im_first=False):
+            halves = (bank[:, 0 : 2 * P], bank[:, 2 * P : 4 * P])
+            first_products(halves[int(im_first)], halves[1 - int(im_first)], P * block, c0, 2 * P)
             nc.scalar.activation(out=dst, in_=bank[:].rearrange("j (h t p) -> j h t p", h=2, t=2), func=ACT.Square)
 
-        def envelope_piece(b, block0, views, bank_sum):
+        def envelope_piece(b, block0, views, bank_sum, between=None):
             j0, width = P * block0, P * len(views)
             for i, view in enumerate(views):
                 add_turned(bank_sum[:, P * i : P * (i + 1)], view[:, 0, b, :], view[:, 1, b, :])
+            if between:
+                between()
             nc.scalar.activation(out=quarter(env, b, width, j0), in_=bank_sum[:, 0:width], func=ACT.Sqrt, bias=nv_first[:, b : b + 1])
             scatter(b, j0, width, quarter(env, b, width, j0), wgs_nat[:, j0 : j0 + width])
 
@@ -304,30 +307,33 @@ def tile_list_pilot_envelope_reliability_kernel(
         late_page("ends_as_page3")
         for block, bank in ((5, 4), (6, 2), (7, 3)):
             both_tiles(block, banks[bank], views[block])
-        envelope_piece(0, 4, [views[block] for block in range(4, 8)], banks[4])
-        quantise_wq(1, (1,), late_squares[:, PASS:M].bitcast(BF16), 2 * P)
+        envelope_piece(
+            0, 4, [views[block] for block in range(4, 8)], banks[4],
+            lambda: quantise_wq(1, (1,), late_squares[:, WIDE : 3 * WIDE].bitcast(BF16), 2 * P),
+        )
         envelope_piece(1, 4, [views[block] for block in range(4, 8)], banks[3])
 
         def squares_at(b, piece):
             if b < 4:
-                c = WIDE * (2 * piece + b - 2)
-                return sq_nat[:, c : c + WIDE], sq_nat[:, 2 * S + c : 2 * S + c + WIDE]
+                c = S * piece + WIDE * (b - 2)
+                low, high = sq_nat[:, c : c + WIDE], sq_nat[:, PASS + c : PASS + c + WIDE]
+                return (low, high) if piece % 2 == 0 else (high, low)
             halves = (re_1, im_1) if b < 8 else (re_2, im_2)
             return tuple(quarter(half, b % 4, WIDE, WIDE * piece) for half in halves)
 
         def z_nat(b, piece):
             return squares_at(b + 2, piece)[0]
 
-        nat = sq_nat[:].rearrange("j (h q t i p) -> j q i h t p", h=2, q=4, t=2, i=2)
+        nat = sq_nat[:].rearrange("j (q h t i p) -> j q i h t p", h=2, q=4, t=2, i=2)
 
         def squares_of_piece(b, piece):
             for block in (2 * piece, 2 * piece + 1):
                 if b == 2:
-                    both_tiles(block, product_banks[block % 4], nat[:, piece, block % 2], 2 * P)
+                    both_tiles(block, product_banks[block % 4], nat[:, piece, block % 2], 2 * P, piece % 2 == 1)
                 else:
                     squares_of_block(b // 4, block, (re_1, im_1) if b == 4 else (re_2, im_2))
 
-        def woven(pair, after_first=None):
+        def woven(pair):
             for piece in range(4):
                 j0 = WIDE * piece
                 if pair[0] in (2, 4, 8):
@@ -337,11 +343,13 @@ def tile_list_pilot_envelope_reliability_kernel(
                     gather((b - 2) % 4, (b - 2) % 4, j0, WIDE, z_nat(b - 2, piece), err_b if 4 <= b - 2 < 8 else err_a)
                     weights = wgs_nat[:, j0 : j0 + WIDE] if b < 4 else quarter(wgs_four, b % 4, WIDE, j0)
                     scatter(b % 4, j0, WIDE, quarter(env, b % 4, WIDE, j0), weights)
-                    if after_first and piece == 0 and b == pair[0]:
-                        after_first()
+                    if (b, piece) == (2, 0):
+                        quantise_wq(2, (2, 3), late_squares[:, M : 2 * M].bitcast(BF16), P)
+                    if (b, piece) == (3, 1):
+                        quantise_wq(3, (4,), sq_nat[:, PASS : PASS + S].bitcast(BF16), P)
 
-        woven((2, 3), lambda: quantise_wq(2, (2, 3), late_squares[:, M : 2 * M].bitcast(BF16), P))
-        woven((4, 5), lambda: quantise_wq(3, (4,), sq_nat[:, 3 * S : 4 * S].bitcast(BF16), P))
+        woven((2, 3))
+        woven((4, 5))
         nc.sync.dma_start(out=err_a[:], in_=err[2 * PASS : 3 * PASS, :].rearrange("(p t) m -> p (t m)", t=4))
         woven((6, 7))
         woven((8, 9))

@@ -26,6 +26,7 @@ FIRST_PIECES = ((0, 256), (256, 256), (512, 512))
 WQ_LOADS = ((0, 256), (256, 256), (512, 256), (768, 256), (1024, 512))
 WQ_PARTS = ((0, 256), (256, 256), (512, 512), (1024, 512))
 WR_PARTS = ((0, 256), (256, 256), (512, 512), (1024, 512))
+RE_ORDER = (2, 0, 3, 1)
 CHUNKS = ((0, WIDE), (256, WIDE), (512, WIDE), (768, NARROW), (896, NARROW))
 PLACES = (
     ((0, 0), (0, 256), (1, 0), (1, 256), (2, 0)),
@@ -74,10 +75,18 @@ def tile_list_pilot_envelope_reliability_kernel(
         env = tile("env", 4 * S, F32)
         err_a = tile("err_a", 4 * M, F32)
         err_b = tile("err_b", 4 * M, F32)
-        sq_nat = tile("sq_nat", 4 * S, F32)
-        sq = tile("sq", 16 * S, F32)
-        im_1, re_1, re_2, im_2 = (sq[:, 4 * S * n : 4 * S * (n + 1)] for n in range(4))
-        z_late = sq[:, 6 * S : 10 * S]
+        sq = tile("sq", 19 * S, F32)
+        im_2 = sq[:, 0 : 3 * S]
+        im_2_last = tile("im_2_last", S, F32, "ends_as_words0")
+        re_late = sq[:, 3 * S : 11 * S]
+        sq_nat = sq[:, 11 * S : 15 * S]
+        im_1 = sq[:, 15 * S : 19 * S]
+        raw_2 = tile("raw_2", 2 * M, F32)
+        runs = sq[:].rearrange("p (n m) -> p n m", m=WIDE)
+
+        def re_piece(piece):
+            return re_late[:, 2 * S * RE_ORDER.index(piece) : 2 * S * (RE_ORDER.index(piece) + 1)]
+
         wq_first = tile("wq_first", 8 * P, BF16)
         z_rows = [tile("z_rows%d" % i, PASS, BF16) for i in range(2)]
         z_w = tile("z_w", M, U32)
@@ -89,7 +98,7 @@ def tile_list_pilot_envelope_reliability_kernel(
             for q in range(4):
                 nc.sync.dma_start(out=plane[32 * q : 32 * q + 4, :].bitcast(I32), in_=rows[4 * q : 4 * q + 4, :].bitcast(I32))
 
-        wq_raw = [quarter(env, 2), quarter(env, 3), quarter(re_2, 0), quarter(re_2, 1), re_2[:, 2 * M : 4 * M]]
+        wq_raw = [quarter(env, 2), quarter(env, 3), quarter(im_1, 0), quarter(im_1, 1), raw_2[:]]
         wq_k = wq.rearrange("(p i) c -> p i c", i=4)
 
         def load_wq(load):
@@ -151,9 +160,9 @@ def tile_list_pilot_envelope_reliability_kernel(
         load_wr(2)
         for a in (1, 2):
             nc.sync.dma_start(out=nv_four[a - 1][:], in_=nv[PASS * a : PASS * (a + 1)].rearrange("(p t) -> p t", t=4))
+        load_wq(4)
         load_wgs_four(0)
         load_err_nat(2)
-        load_wq(4)
         load_wgs_four(2)
         nc.sync.dma_start(out=err_b[:, 0 : 2 * M], in_=err_four[:, 0 : 2 * M])
         load_wr(3)
@@ -204,21 +213,29 @@ def tile_list_pilot_envelope_reliability_kernel(
 
         product_banks = [banks[n] for n in (0, 1, 2, 4)]
 
-        def squares_of_block(a, block, halves):
+        def im_2_piece(piece):
+            return quarter(im_2, piece) if piece < 3 else im_2_last[:]
+
+        def squares_of_block(a, block):
             pair = product_banks[2:4] if block % 2 == 0 else product_banks[0:2]
             first_products(pair[0][:], pair[1][:], P * block, PASS * a, PASS)
+            piece, i = divmod(block, 2)
+            halves = (quarter(re_piece(piece), a - 1), quarter(im_1, piece) if a == 1 else im_2_piece(piece))
             for half, bank in zip(halves, pair):
                 nc.scalar.activation(
-                    out=half.rearrange("j (t i p) -> j i t p", t=4, p=P)[:, block],
+                    out=half.rearrange("j (t i p) -> j i t p", t=4, p=P)[:, i],
                     in_=bank[:].rearrange("j (p t) -> j t p", t=4), func=ACT.Square,
                 )
 
-        def envelope(b, j0, squares_re, squares_im, bank_sum):
-            width = squares_re.shape[1]
-            for c in range(0, width, P):
-                add_turned(bank_sum[:, c : c + P], squares_re[:, c : c + P], squares_im[:, c : c + P])
+        def envelope(b, pieces, dst, between=None):
+            for n, piece in enumerate(pieces):
+                squares_re, squares_im = squares_at(b, piece)
+                for c in (0, P):
+                    add_turned(banks[3][:, WIDE * n + c : WIDE * n + c + P], squares_re[:, c : c + P], squares_im[:, c : c + P])
+            if between:
+                between()
             bias = nv_nat[:, b - 2 : b - 1] if b < 4 else nv_four[b // 4 - 1][:, b % 4 : b % 4 + 1]
-            nc.scalar.activation(out=quarter(env, b % 4, width, j0), in_=bank_sum[:, 0:width], func=ACT.Sqrt, bias=bias)
+            nc.scalar.activation(out=dst, in_=banks[3][:, 0 : WIDE * len(pieces)], func=ACT.Sqrt, bias=bias)
 
         def scatter(page, j0, width, values, weights):
             nc.vector.tensor_tensor(out=pages[page][:].indirect(entries(slots, j0, width)), in0=values, in1=weights, op=ALU.mult)
@@ -228,11 +245,11 @@ def tile_list_pilot_envelope_reliability_kernel(
                 out=dst, in0=pages[page][:].indirect(entries(carriers, m0, width)), in1=quarter(errors, t, width, m0), op=ALU.add
             )
 
-        def turn_first_pass(z_nat, rounded):
+        def turn_first_pass(z_nat, rounded_at):
             for group in range(4):
                 bank_back = banks[6 + group % 2]
                 for i in range(2):
-                    bank_in = banks[4 + i]
+                    bank_in = banks[3] if group < 2 and i == 0 else product_banks[2 + i]
                     for t in range(4):
                         nc.tensor.transpose(bank_in[:, P * t : P * (t + 1)], z_nat(t, group)[:, P * i : P * (i + 1)], ident[:])
                     nc.scalar.copy(
@@ -243,9 +260,8 @@ def tile_list_pilot_envelope_reliability_kernel(
                         nc.tensor.transpose(
                             bank_back[:, P * (2 * i + u) : P * (2 * i + u + 1)], z_rows[i][:].bitcast(F32)[:, P * u : P * (u + 1)], ident[:]
                         )
-                order = "p (a i m u) -> p a i m u" if CHUNKS[group][1] == WIDE else "p (i a m u) -> p a i m u"
                 nc.scalar.copy(
-                    out=quarter(rounded, group).rearrange(order, a=2, i=2, u=2)[:, 0],
+                    out=rounded_at(0, group).rearrange("p (i m u) -> p i m u", i=2, u=2),
                     in_=bank_back[:].rearrange("p (i u m) -> p i m u", i=2, u=2),
                 )
 
@@ -311,27 +327,30 @@ def tile_list_pilot_envelope_reliability_kernel(
             0, 4, [views[block] for block in range(4, 8)], banks[4],
             lambda: quantise_wq(1, (1,), late_squares[:, WIDE : 3 * WIDE].bitcast(BF16), 2 * P),
         )
-        envelope_piece(1, 4, [views[block] for block in range(4, 8)], banks[3])
+        envelope_piece(
+            1, 4, [views[block] for block in range(4, 8)], banks[3],
+            lambda: quantise_wq(2, (2, 3), late_squares[:, M : 2 * M].bitcast(BF16), P),
+        )
 
         def squares_at(b, piece):
             if b < 4:
                 c = S * piece + WIDE * (b - 2)
                 low, high = sq_nat[:, c : c + WIDE], sq_nat[:, PASS + c : PASS + c + WIDE]
                 return (low, high) if piece % 2 == 0 else (high, low)
-            halves = (re_1, im_1) if b < 8 else (re_2, im_2)
-            return tuple(quarter(half, b % 4, WIDE, WIDE * piece) for half in halves)
+            squares_im = quarter(im_1, piece) if b < 8 else im_2_piece(piece)
+            return re_piece(piece)[:, WIDE * (b - 4) : WIDE * (b - 3)], squares_im[:, WIDE * (b % 4) : WIDE * (b % 4 + 1)]
 
         def z_nat(b, piece):
             return squares_at(b + 2, piece)[0]
 
-        nat = sq_nat[:].rearrange("j (q h t i p) -> j q i h t p", h=2, q=4, t=2, i=2)
+        nat = sq_nat.rearrange("j (q h t i p) -> j q i h t p", h=2, q=4, t=2, i=2)
 
         def squares_of_piece(b, piece):
             for block in (2 * piece, 2 * piece + 1):
                 if b == 2:
                     both_tiles(block, product_banks[block % 4], nat[:, piece, block % 2], 2 * P, piece % 2 == 1)
                 else:
-                    squares_of_block(b // 4, block, (re_1, im_1) if b == 4 else (re_2, im_2))
+                    squares_of_block(b // 4, block)
 
         def woven(pair):
             for piece in range(4):
@@ -339,58 +358,87 @@ def tile_list_pilot_envelope_reliability_kernel(
                 if pair[0] in (2, 4, 8):
                     squares_of_piece(pair[0], piece)
                 for b in pair:
-                    envelope(b, j0, *squares_at(b, piece), banks[3])
+                    cast = (lambda: quantise_wq(3, (4,), sq_nat[:, PASS : PASS + S].bitcast(BF16), P)) if (b, piece) == (3, 1) else None
+                    envelope(b, (piece,), quarter(env, b % 4, WIDE, j0), cast)
                     gather((b - 2) % 4, (b - 2) % 4, j0, WIDE, z_nat(b - 2, piece), err_b if 4 <= b - 2 < 8 else err_a)
                     weights = wgs_nat[:, j0 : j0 + WIDE] if b < 4 else quarter(wgs_four, b % 4, WIDE, j0)
                     scatter(b % 4, j0, WIDE, quarter(env, b % 4, WIDE, j0), weights)
-                    if (b, piece) == (2, 0):
-                        quantise_wq(2, (2, 3), late_squares[:, M : 2 * M].bitcast(BF16), P)
-                    if (b, piece) == (3, 1):
-                        quantise_wq(3, (4,), sq_nat[:, PASS : PASS + S].bitcast(BF16), P)
 
         woven((2, 3))
         woven((4, 5))
         nc.sync.dma_start(out=err_a[:], in_=err[2 * PASS : 3 * PASS, :].rearrange("(p t) m -> p (t m)", t=4))
         woven((6, 7))
         woven((8, 9))
-        for b in (10, 11):
-            for j0, bank in ((0, 3), (PASS, 5)):
-                envelope(b, j0, quarter(re_2, b % 4, PASS, j0), quarter(im_2, b % 4, PASS, j0), banks[bank])
-            scatter(b % 4, 0, S, quarter(env, b % 4), quarter(wgs_four, b % 4))
-        turn_first_pass(z_nat, im_2)
-        rounded_early = im_2.bitcast(BF16)
-        z_pass_1 = z_late.rearrange("p (i m) -> p i m", i=4)
-        for m0, count, width in ((0, 3, WIDE), (CHUNKS[3][0], 2, NARROW)):
-            nc.scalar.copy(
-                out=rounded_early[:, 8 * m0 : 8 * (m0 + count * width)].rearrange("p (g a c x i) -> p a g c i x", g=count, a=2, x=4, i=4)[:, 1],
-                in_=z_pass_1[:, :, m0 : m0 + count * width].rearrange("p i (g c x) -> p g c i x", g=count, x=4),
+
+        rounded_early = [quarter(sq_nat, 0), quarter(sq_nat, 1), quarter(im_2, 0), quarter(im_2, 2)]
+
+        def place_of(a, piece):
+            return 1 - a if piece == 0 else a
+
+        def rounded_at(a, piece):
+            return rounded_early[piece][:, PASS * place_of(a, piece) : PASS * (place_of(a, piece) + 1)]
+
+        def round_pass_1(piece):
+            z_rows_4 = re_piece(piece)[:, 2 * WIDE : 6 * WIDE].rearrange("p (i m) -> p i m", i=4)
+            interleave(nc.scalar.copy, rounded_at(1, piece).bitcast(BF16), z_rows_4)
+
+        words_early = []
+        held = []
+
+        def quantise_early(piece, count, rounded):
+            if piece != 2:
+                words = tile("words%d" % piece, PASS * (3 if piece == 0 else 1), U32, "ends_as_words%d" % piece)
+                words_early.extend(words[:, c : c + PASS] for c in range(0, words.shape[1], PASS))
+                held.append(words)
+            words = held[-1][:, PASS * (piece % 3) : PASS * (piece % 3 + count)]
+            nc.vector.quantize_mx(
+                out=words.bitcast(E4M3), scales=z_early_s[:, PASS * piece : PASS * (piece + count)], in_=rounded.bitcast(BF16)
             )
 
-        picked = [z_late[:, WIDE * c : WIDE * c + 2 * M].rearrange("p (t m) -> p t m", t=4) for c in range(3)]
-        picked_narrow = z_late[:, WIDE : WIDE + M].rearrange("p (t m) -> p t m", t=4)
-        rounded_2 = [tile("rounded_2_%d" % c, 4 * WIDE, BF16, "ends_as_run%d" % (c + 1))[:] for c in range(3)]
-        rounded_2.append(picked[2][:, 2, 0:WIDE].bitcast(BF16))
-        rounded_2.append(tile("rounded_2_4", 4 * NARROW, BF16)[:])
-        runs = []
+        Z_RUNS = ((42, 43, 44, 45), (34, 35, 36, 37), (36, 37, 45, 46), (8, 9, 36, 37))
+
+        def gather_late(t, piece, col=0, width=WIDE):
+            gather(t, t, WIDE * piece + col, width, runs[:, Z_RUNS[piece][t], col : col + width], err_a)
+
+        def z_pass_2(c):
+            piece, col = divmod(CHUNKS[c][0], WIDE)
+            low, high = Z_RUNS[piece][0], Z_RUNS[piece][2]
+            both = sq[:, WIDE * low : WIDE * (2 * high - low)].rearrange("p (u n m) -> p u n m", u=2, m=WIDE)
+            return both[:, :, 0:2, col : col + CHUNKS[c][1]]
+
+        rounded_2 = [tile("rounded_2_%d" % c, 4 * WIDE, BF16, "ends_as_words%d" % (c + 2))[:] for c in range(3)]
+        rounded_2.extend(runs[:, n].bitcast(BF16) for n in (45, 46))
+
+        def round_late(engine_copy, c, pairs=slice(0, 2)):
+            engine_copy(
+                out=rounded_2[c].rearrange("p (c x u e) -> p c u e x", x=4, u=2, e=2)[:, :, pairs],
+                in_=z_pass_2(c).rearrange("p u e (c x) -> p c u e x", x=4)[:, :, pairs],
+            )
+
+        turn_first_pass(z_nat, rounded_at)
+        round_pass_1(1)
+        round_pass_1(0)
+        for half in range(2):
+            for b in (10, 11):
+                last = (b, half) == (11, 1)
+                values = sq[:, 36 * WIDE : 38 * WIDE] if last else quarter(env, b % 4, PASS, PASS * half)
+                envelope(b, (2 * half, 2 * half + 1), values, (lambda: round_pass_1(3)) if last else None)
+                gather_late(b - 10, half)
+                if last:
+                    quantise_early(0, 2, sq_nat[:, 0 : 2 * S])
+                    quantise_early(2, 1, rounded_early[2])
+                scatter(b % 4, PASS * half, PASS, values, quarter(wgs_four, b % 4, PASS, PASS * half))
+            round_late(nc.scalar.copy, half, slice(0, 1))
+            if half == 0:
+                round_pass_1(2)
 
         def z_operand(a, c):
             m0, width = CHUNKS[c]
             if a == 2:
                 return z_w[:, m0 : m0 + width], z_s[:, m0 : m0 + width]
-            run, col = divmod(m0, WIDE)
-            first = 2 * col + width * a
-            return runs[run][:, first : first + width], z_early_s[:, 2 * m0 + width * a : 2 * m0 + width * (a + 1)]
-
-        def early_passes(c):
-            m0, width = CHUNKS[c]
-            run, col = divmod(m0, WIDE)
-            if len(runs) == run:
-                runs.append(tile("run%d" % run, 2 * WIDE, U32, "ends_as_run%d" % run))
-            nc.vector.quantize_mx(
-                out=runs[run][:, 2 * col : 2 * (col + width)].bitcast(E4M3), scales=z_early_s[:, 2 * m0 : 2 * (m0 + width)],
-                in_=rounded_early[:, 8 * m0 : 8 * (m0 + width)],
-            )
-            products(c, range(5), (0, 1))
+            piece, col = divmod(m0, WIDE)
+            first = WIDE * place_of(a, piece) + col
+            return words_early[piece][:, first : first + width], z_early_s[:, PASS * piece + first : PASS * piece + first + width]
 
         staged = [err_b[:, PASS * n : PASS * (n + 1)] for n in range(8)] + [im_1[:, PASS * n : PASS * (n + 1)] for n in range(3)]
         out_n = out.rearrange("(i p) m -> p i m", p=P)
@@ -419,60 +467,44 @@ def tile_list_pilot_envelope_reliability_kernel(
             engine_copy(out=result, in_=banks[bank][:, 0 : count * width])
             nc.sync.dma_start(out=out_n[:, i0 : i0 + count, m0 : m0 + width], in_=result.rearrange("p (i m) -> p i m", i=count))
 
-        def gather_wide(t, c, count=1):
-            gather(t, t, CHUNKS[c][0], count * WIDE, picked[c][:, t, 0 : count * WIDE], err_a)
-
-        def gather_narrow(t, c, count=1):
-            col = NARROW * (c - 3)
-            gather(t, t, CHUNKS[c][0], count * NARROW, picked_narrow[:, t, col : col + count * NARROW], err_a)
-
-        def round_wide(c):
-            interleave(nc.scalar.copy, rounded_2[c], picked[c][:, :, 0:WIDE])
-
-        def round_narrow(c):
-            interleave(nc.vector.tensor_copy, rounded_2[c], picked_narrow[:, :, NARROW * (c - 3) : NARROW * (c - 2)])
-
         def last_pass(c, closing, out_tiles=range(5)):
             words, plane = z_operand(2, c)
             nc.vector.quantize_mx(out=words.bitcast(E4M3), scales=plane, in_=rounded_2[c])
             products(c, out_tiles, (2,), closing)
 
-        gather_wide(0, 0, 2)
-        gather_wide(1, 0, 2)
-        gather_wide(2, 0)
-        gather_wide(3, 0)
-        round_wide(0)
-        early_passes(0)
-        gather_wide(2, 1)
-        gather_wide(3, 1, 2)
-        round_wide(1)
+        for c in range(3):
+            products(c, range(5), (0, 1))
+        for c in (0, 1):
+            gather_late(2, c)
+            gather_late(3, c)
+            round_late(nc.scalar.copy, c, slice(1, 2))
+        gather_late(3, 2)
         last_pass(0, (1, 3))
+        gather_late(2, 2)
+        round_late(nc.scalar.copy, 2, slice(1, 2))
         store(nc.scalar.copy, 0, 0, 2, 0, 256)
         store(nc.scalar.copy, 1, 2, 2, 0, 256)
-        gather_wide(0, 2)
-        early_passes(1)
-        gather_wide(1, 2)
-        gather_wide(2, 2)
-        round_wide(2)
         last_pass(1, (1, 3, 4))
+        gather_late(0, 2)
+        quantise_early(3, 1, rounded_early[3])
+        products(3, range(5), (0, 1))
+        gather_late(1, 2)
+        round_late(nc.scalar.copy, 2, slice(0, 1))
         store(nc.scalar.copy, 3, 0, 2, 256, 256)
         store(nc.scalar.copy, 4, 2, 2, 256, 256)
         store(nc.scalar.copy, 2, 4, 1, 0, 512)
-        gather_narrow(0, 3, 2)
-        early_passes(2)
-        gather_narrow(2, 3, 2)
+        gather_late(0, 3)
+        gather_late(1, 3)
         last_pass(2, (1, 3))
+        products(4, range(5), (0, 1))
         store(nc.scalar.copy, 5, 0, 2, 512, 256)
         store(nc.scalar.copy, 6, 2, 2, 512, 256)
-        gather_narrow(1, 3)
-        gather_narrow(3, 3)
-        early_passes(3)
-        round_narrow(3)
-        gather_narrow(1, 4)
+        gather_late(2, 3)
+        gather_late(3, 3, 0, NARROW)
+        gather_late(3, 3, NARROW, NARROW)
+        round_late(nc.vector.tensor_copy, 3)
+        round_late(nc.vector.tensor_copy, 4)
         last_pass(3, (3, 4), (4, 0, 1, 2, 3))
-        gather_narrow(3, 4)
-        early_passes(4)
-        round_narrow(4)
         last_pass(4, (2, 4))
         store(nc.scalar.copy, 7, 4, 1, 512, 384)
         store(nc.vector.tensor_copy, 0, 0, 4, 768, 128)

@@ -77,7 +77,8 @@ def tile_list_pilot_envelope_reliability_kernel(
         err_b = tile("err_b", 4 * M, F32)
         sq = tile("sq", 19 * S, F32)
         im_2 = sq[:, 0 : 3 * S]
-        im_2_last = tile("im_2_last", S, F32, "ends_as_words0")
+        im_2_last = tile("im_2_last", 3 * WIDE, F32, "ends_as_words0")
+        im_2_end = tile("im_2_end", WIDE, F32)
         re_late = sq[:, 3 * S : 11 * S]
         sq_nat = sq[:, 11 * S : 15 * S]
         im_1 = sq[:, 15 * S : 19 * S]
@@ -213,18 +214,19 @@ def tile_list_pilot_envelope_reliability_kernel(
 
         product_banks = [banks[n] for n in (0, 1, 2, 4)]
 
-        def im_2_piece(piece):
-            return quarter(im_2, piece) if piece < 3 else im_2_last[:]
-
         def squares_of_block(a, block):
             pair = product_banks[2:4] if block % 2 == 0 else product_banks[0:2]
             first_products(pair[0][:], pair[1][:], P * block, PASS * a, PASS)
             piece, i = divmod(block, 2)
-            halves = (quarter(re_piece(piece), a - 1), quarter(im_1, piece) if a == 1 else im_2_piece(piece))
-            for half, bank in zip(halves, pair):
+            parts = [(quarter(re_piece(piece), a - 1), pair[0], 0, 4)]
+            if (a, piece) == (2, 3):
+                parts.extend([(im_2_last[:], pair[1], 0, 3), (im_2_end[:], pair[1], 3, 4)])
+            else:
+                parts.append((quarter(im_1 if a == 1 else im_2, piece), pair[1], 0, 4))
+            for dst, bank, t0, t1 in parts:
                 nc.scalar.activation(
-                    out=half.rearrange("j (t i p) -> j i t p", t=4, p=P)[:, i],
-                    in_=bank[:].rearrange("j (p t) -> j t p", t=4), func=ACT.Square,
+                    out=dst.rearrange("j (t i p) -> j i t p", i=2, p=P)[:, i],
+                    in_=bank[:].rearrange("j (p t) -> j t p", t=4)[:, t0:t1], func=ACT.Square,
                 )
 
         def envelope(b, pieces, dst, between=None):
@@ -337,8 +339,11 @@ def tile_list_pilot_envelope_reliability_kernel(
                 c = S * piece + WIDE * (b - 2)
                 low, high = sq_nat[:, c : c + WIDE], sq_nat[:, PASS + c : PASS + c + WIDE]
                 return (low, high) if piece % 2 == 0 else (high, low)
-            squares_im = quarter(im_1, piece) if b < 8 else im_2_piece(piece)
-            return re_piece(piece)[:, WIDE * (b - 4) : WIDE * (b - 3)], squares_im[:, WIDE * (b % 4) : WIDE * (b % 4 + 1)]
+            squares_re = re_piece(piece)[:, WIDE * (b - 4) : WIDE * (b - 3)]
+            if (b, piece) == (11, 3):
+                return squares_re, im_2_end[:]
+            squares_im = quarter(im_1, piece) if b < 8 else quarter(im_2, piece) if piece < 3 else im_2_last
+            return squares_re, squares_im[:, WIDE * (b % 4) : WIDE * (b % 4 + 1)]
 
         def z_nat(b, piece):
             return squares_at(b + 2, piece)[0]
@@ -406,7 +411,8 @@ def tile_list_pilot_envelope_reliability_kernel(
             both = sq[:, WIDE * low : WIDE * (2 * high - low)].rearrange("p (u n m) -> p u n m", u=2, m=WIDE)
             return both[:, :, 0:2, col : col + CHUNKS[c][1]]
 
-        rounded_2 = [tile("rounded_2_%d" % c, 4 * WIDE, BF16, "ends_as_words%d" % (c + 2))[:] for c in range(3)]
+        rounded_first = tile("rounded_first", 8 * WIDE, BF16, "ends_as_words3")
+        rounded_2 = [rounded_first[:, 0 : 4 * WIDE], rounded_first[:, 4 * WIDE : 8 * WIDE], tile("rounded_2_2", 4 * WIDE, BF16)[:]]
         rounded_2.extend(runs[:, n].bitcast(BF16) for n in (45, 46))
 
         def round_late(engine_copy, c, pairs=slice(0, 2)):
@@ -418,19 +424,23 @@ def tile_list_pilot_envelope_reliability_kernel(
         turn_first_pass(z_nat, rounded_at)
         round_pass_1(1)
         round_pass_1(0)
-        for half in range(2):
+        for piece in range(4):
+            j0, m0 = WIDE * piece, NARROW * RE_ORDER.index(piece)
             for b in (10, 11):
-                last = (b, half) == (11, 1)
-                values = sq[:, 36 * WIDE : 38 * WIDE] if last else quarter(env, b % 4, PASS, PASS * half)
-                envelope(b, (2 * half, 2 * half + 1), values, (lambda: round_pass_1(3)) if last else None)
-                gather_late(b - 10, half)
-                if last:
+                values = runs[:, 36] if (b, piece) == (11, 3) else quarter(env, b % 4, WIDE, j0)
+                envelope(b, (piece,), values)
+                gather(b - 10, b - 10, m0, NARROW, squares_at(b, piece)[0][:, NARROW:WIDE], err_a)
+                if (b, piece) == (10, 3):
                     quantise_early(0, 2, sq_nat[:, 0 : 2 * S])
                     quantise_early(2, 1, rounded_early[2])
-                scatter(b % 4, PASS * half, PASS, values, quarter(wgs_four, b % 4, PASS, PASS * half))
-            round_late(nc.scalar.copy, half, slice(0, 1))
-            if half == 0:
-                round_pass_1(2)
+                scatter(b % 4, j0, WIDE, values, quarter(wgs_four, b % 4, WIDE, j0))
+            if piece in (0, 2):
+                round_pass_1(2 + piece // 2)
+
+        nc.scalar.copy(
+            out=rounded_first[:].rearrange("p (h c x u e) -> p u h c e x", h=4, x=4, u=2, e=2)[:, 0],
+            in_=re_late.rearrange("p (h b s c x) -> p s h c b x", h=4, b=8, s=2, x=4)[:, 1, :, :, 6:8],
+        )
 
         def z_operand(a, c):
             m0, width = CHUNKS[c]

@@ -400,7 +400,7 @@ def tile_list_pilot_envelope_reliability_kernel(
                 out=words.bitcast(E4M3), scales=z_early_s[:, PASS * piece : PASS * (piece + count)], in_=rounded.bitcast(BF16)
             )
 
-        Z_RUNS = ((42, 43, 44, 45), (34, 35, 36, 37), (36, 37, 45, 46), (8, 9, 36, 37))
+        Z_RUNS = {2: (45, 46, 48, 49), 3: (45, 46, 50, 51)}
 
         def gather_late(t, piece, col=0, width=WIDE):
             gather(t, t, WIDE * piece + col, width, runs[:, Z_RUNS[piece][t], col : col + width], err_a)
@@ -411,14 +411,15 @@ def tile_list_pilot_envelope_reliability_kernel(
             both = sq[:, WIDE * low : WIDE * (2 * high - low)].rearrange("p (u n m) -> p u n m", u=2, m=WIDE)
             return both[:, :, 0:2, col : col + CHUNKS[c][1]]
 
-        rounded_first = tile("rounded_first", 8 * WIDE, BF16, "ends_as_words3")
-        rounded_2 = [rounded_first[:, 0 : 4 * WIDE], rounded_first[:, 4 * WIDE : 8 * WIDE], tile("rounded_2_2", 4 * WIDE, BF16)[:]]
-        rounded_2.extend(runs[:, n].bitcast(BF16) for n in (45, 46))
+        rounded_first = sq[:, 48 * WIDE : 52 * WIDE].bitcast(BF16)
+        rounded_2 = [rounded_first[:, 0 : 4 * WIDE], rounded_first[:, 4 * WIDE : 8 * WIDE]]
+        rounded_2.extend(tile("rounded_2_%d" % c, 4 * CHUNKS[c][1], BF16)[:] for c in (2, 3, 4))
+        env_last = tile("env_last", WIDE, F32, "ends_as_words3")
 
-        def round_late(engine_copy, c, pairs=slice(0, 2)):
+        def round_late(engine_copy, c):
             engine_copy(
-                out=rounded_2[c].rearrange("p (c x u e) -> p c u e x", x=4, u=2, e=2)[:, :, pairs],
-                in_=z_pass_2(c).rearrange("p u e (c x) -> p c u e x", x=4)[:, :, pairs],
+                out=rounded_2[c].rearrange("p (c x u e) -> p c u e x", x=4, u=2, e=2),
+                in_=z_pass_2(c).rearrange("p u e (c x) -> p c u e x", x=4),
             )
 
         turn_first_pass(z_nat, rounded_at)
@@ -427,7 +428,7 @@ def tile_list_pilot_envelope_reliability_kernel(
         for piece in range(4):
             j0, m0 = WIDE * piece, NARROW * RE_ORDER.index(piece)
             for b in (10, 11):
-                values = runs[:, 36] if (b, piece) == (11, 3) else quarter(env, b % 4, WIDE, j0)
+                values = env_last[:] if (b, piece) == (11, 3) else quarter(env, b % 4, WIDE, j0)
                 envelope(b, (piece,), values)
                 gather(b - 10, b - 10, m0, NARROW, squares_at(b, piece)[0][:, NARROW:WIDE], err_a)
                 if (b, piece) == (10, 3):
@@ -438,7 +439,7 @@ def tile_list_pilot_envelope_reliability_kernel(
                 round_pass_1(2 + piece // 2)
 
         nc.scalar.copy(
-            out=rounded_first[:].rearrange("p (h c x u e) -> p u h c e x", h=4, x=4, u=2, e=2)[:, 0],
+            out=rounded_first.rearrange("p (h c x u e) -> p u h c e x", h=4, x=4, u=2, e=2)[:, 0],
             in_=re_late.rearrange("p (h b s c x) -> p s h c b x", h=4, b=8, s=2, x=4)[:, 1, :, :, 6:8],
         )
 
@@ -482,36 +483,38 @@ def tile_list_pilot_envelope_reliability_kernel(
             nc.vector.quantize_mx(out=words.bitcast(E4M3), scales=plane, in_=rounded_2[c])
             products(c, out_tiles, (2,), closing)
 
-        for c in range(3):
+        for c in range(2):
             products(c, range(5), (0, 1))
-        for c in (0, 1):
-            gather_late(2, c)
-            gather_late(3, c)
-            round_late(nc.scalar.copy, c, slice(1, 2))
-        gather_late(3, 2)
+        for c, pair in enumerate((sq[:, 44 * WIDE : 46 * WIDE], tile("z_pair", 2 * WIDE, F32, "ends_as_words3")[:])):
+            for e in range(2):
+                gather(2 + e, 2 + e, WIDE * c, WIDE, pair[:, WIDE * e : WIDE * (e + 1)], err_a)
+            nc.scalar.copy(
+                out=rounded_2[c].rearrange("p (c x u e) -> p u c e x", x=4, u=2, e=2)[:, 1],
+                in_=pair.rearrange("p (e c x) -> p c e x", e=2, x=4),
+            )
+        gather_late(1, 2)
         last_pass(0, (1, 3))
-        gather_late(2, 2)
-        round_late(nc.scalar.copy, 2, slice(1, 2))
+        products(2, range(5), (0, 1))
         store(nc.scalar.copy, 0, 0, 2, 0, 256)
         store(nc.scalar.copy, 1, 2, 2, 0, 256)
+        for t in (0, 2, 3):
+            gather_late(t, 2)
+        round_late(nc.scalar.copy, 2)
         last_pass(1, (1, 3, 4))
-        gather_late(0, 2)
-        quantise_early(3, 1, rounded_early[3])
-        products(3, range(5), (0, 1))
-        gather_late(1, 2)
-        round_late(nc.scalar.copy, 2, slice(0, 1))
         store(nc.scalar.copy, 3, 0, 2, 256, 256)
         store(nc.scalar.copy, 4, 2, 2, 256, 256)
         store(nc.scalar.copy, 2, 4, 1, 0, 512)
-        gather_late(0, 3)
-        gather_late(1, 3)
+        quantise_early(3, 1, rounded_early[3])
+        products(3, range(5), (0, 1))
+        gather_late(2, 3)
+        gather_late(3, 3)
         last_pass(2, (1, 3))
         products(4, range(5), (0, 1))
         store(nc.scalar.copy, 5, 0, 2, 512, 256)
         store(nc.scalar.copy, 6, 2, 2, 512, 256)
-        gather_late(2, 3)
-        gather_late(3, 3, 0, NARROW)
-        gather_late(3, 3, NARROW, NARROW)
+        gather_late(0, 3)
+        gather_late(1, 3, 0, NARROW)
+        gather_late(1, 3, NARROW, NARROW)
         round_late(nc.vector.tensor_copy, 3)
         round_late(nc.vector.tensor_copy, 4)
         last_pass(3, (3, 4), (4, 0, 1, 2, 3))

from contextlib import ExitStack

import concourse.mybir as mybir
from concourse.masks import make_identity

K, H, N, T, S, T2, M = 512, 1536, 640, 2048, 1024, 2048, 1024
FLOPS = 2 * K * H * S * 2 + 2 * H * N * M

F32 = mybir.dt.float32
BF16 = mybir.dt.bfloat16
I32 = mybir.dt.int32
U32 = mybir.dt.uint32
U16 = mybir.dt.uint16
U8 = mybir.dt.uint8
E4M3 = mybir.dt.float8_e4m3fn_x4
E2M1 = mybir.dt.float4_e2m1fn_x4
ACT = mybir.ActivationFunctionType
ALU = mybir.AluOpType

P = 128
PASS = 512
LIST_ROWS = 16
WIDE, NARROW = 256, 128
SCALES_AHEAD = 768
FIRST_PIECES = ((0, 256), (256, 256), (512, 512))
WQ_LOADS = ((0, 256), (256, 256), (512, 256), (768, 256), (1024, 512))
WQ_PARTS = ((0, 256), (256, 256), (512, 512), (1024, 512))
WR_PARTS = ((0, 256), (256, 256), (512, 512), (1024, 512))
RE_ORDER = (2, 0, 3, 1)
CHUNKS = ((0, WIDE), (256, WIDE), (512, WIDE), (768, NARROW), (896, NARROW))
PLACES = (
    ((0, 0), (0, 256), (1, 0), (1, 256), (2, 0)),
    ((3, 0), (3, 256), (4, 0), (4, 256), (2, 256)),
    ((5, 0), (5, 256), (6, 0), (6, 256), (7, 0)),
    ((0, 0), (0, 128), (0, 256), (0, 384), (7, 256)),
    ((1, 0), (1, 128), (1, 256), (3, 0), (3, 128)),
)


def tile_list_pilot_envelope_reliability_kernel(
    tc, tab_words, tab_scales, offs, wr_words, wr_scales, wq, nv, wgs, offs2, offs3, err, wm_words, wm_scales, out
):
    nc = tc.nc
    with ExitStack() as ctx:
        sb = ctx.enter_context(tc.tile_pool(name="sb", bufs=1))
        ps = ctx.enter_context(tc.psum_pool(name="ps", bufs=1))

        def tile(name, width, dtype, tag=None):
            return sb.tile([P, width], dtype, name=name, tag=tag or name, align_bytes=64)

        def quarter(big, i, width=M, start=0):
            return big[:, M * i + start : M * i + start + width]

        pilots = tile("pilots", S // LIST_ROWS, U16)
        slots = tile("slots", S // LIST_ROWS, U16)
        carriers = tile("carriers", M // LIST_ROWS, U16)
        tab_w = tile("tab_w", T, I32, "ends_as_page3")
        tab_s = tile("tab_s", T, U8, "ends_as_wm_s")
        v_w = tile("v_w", S, U32)
        v_s = [tile("v_s0", SCALES_AHEAD, U8)]
        first_squares = tile("first_squares", 2 * P, F32, "ends_as_v_s1")
        wr_w = [tile("wr_w%d" % c0, 2 * width, U8) for c0, width in WR_PARTS]
        wr_s = tile("wr_s", H, U8)
        wq_w = [tile("wq_w%d" % c0, width, U32) for c0, width in WQ_PARTS]
        wq_s = [tile("wq_s%d" % c0, width, U8) for c0, width in WQ_PARTS]
        wm_w = tile("wm_w", 3 * N, I32)
        nv_first = tile("nv_first", 2, F32)
        nv_nat = tile("nv_nat", 2, F32)
        nv_four = [tile("nv_four%d" % a, 4, F32) for a in (1, 2)]
        ident = tile("ident", P, F32)
        wgs_nat = tile("wgs_nat", S, F32)
        wgs_four = tile("wgs_four", 4 * S, F32)
        pages = [tile("page%d" % i, T2, F32) for i in range(2)]
        before_page2 = tile("before_page2", PASS, F32, "ends_as_page2")
        env = tile("env", 4 * S, F32)
        err_a = tile("err_a", 4 * M, F32)
        err_b = tile("err_b", 4 * M, F32)
        sq = tile("sq", 19 * S, F32)
        im_2 = sq[:, 0 : 3 * S]
        im_2_last = tile("im_2_last", 3 * WIDE, F32, "ends_as_words0")
        im_2_end = tile("im_2_end", WIDE, F32)
        re_late = sq[:, 3 * S : 11 * S]
        sq_nat = sq[:, 11 * S : 15 * S]
        im_1 = sq[:, 15 * S : 19 * S]
        raw_2 = tile("raw_2", 2 * M, F32)
        runs = sq[:].rearrange("p (n m) -> p n m", m=WIDE)

        def re_piece(piece):
            return re_late[:, 2 * S * RE_ORDER.index(piece) : 2 * S * (RE_ORDER.index(piece) + 1)]

        wq_first = tile("wq_first", 8 * P, BF16)
        z_rows = [tile("z_rows%d" % i, PASS, BF16) for i in range(2)]
        z_w = tile("z_w", M, U32)
        z_s = tile("z_s", M, U8)
        z_early_s = tile("z_early_s", 2 * M, U8)
        banks = [ps.tile([P, PASS], F32, name="bank%d" % i) for i in range(8)]

        def load_scale_rows(plane, rows):
            for q in range(4):
                nc.sync.dma_start(out=plane[32 * q : 32 * q + 4, :].bitcast(I32), in_=rows[4 * q : 4 * q + 4, :].bitcast(I32))

        wq_raw = [quarter(env, 2), quarter(env, 3), quarter(im_1, 0), quarter(im_1, 1), raw_2[:]]
        wq_k = wq.rearrange("(p i) c -> p i c", i=4)

        def load_wq(load):
            c0, width = WQ_LOADS[load]
            nc.sync.dma_start(out=wq_raw[load].rearrange("p (i c) -> p i c", i=4), in_=wq_k[:, :, c0 : c0 + width])

        def load_wr(part):
            c0, width = WR_PARTS[part]
            nc.sync.dma_start(out=wr_w[part][:].bitcast(I32), in_=wr_words[0][:, 2 * c0 : 2 * (c0 + width)].bitcast(I32))

        def interleave(engine_copy, dst, src):
            engine_copy(out=dst.rearrange("p (c x i) -> p c i x", x=4, i=4), in_=src.rearrange("p i (c x) -> p c i x", x=4))

        def quantise_wq(part, loads, rounded, step):
            done = 0
            for load in loads:
                raw = wq_raw[load].rearrange("p (i c) -> p i c", i=4)
                for c0 in range(0, WQ_LOADS[load][1], step):
                    interleave(nc.scalar.copy, rounded[:, 4 * done : 4 * (done + step)], raw[:, :, c0 : c0 + step])
                    done = done + step
            nc.vector.quantize_mx(out=wq_w[part][:].bitcast(E4M3), scales=wq_s[part][:], in_=rounded)

        warm = tile("warm", 2, F32)
        nc.vector.memset(tab_s[:].bitcast(I32), 0)
        nc.vector.memset(warm[:, 0:1], 1.0)
        nc.vector.memset(wr_s[:].bitcast(I32), 0)
        nc.scalar.activation(out=warm[:, 1:2], in_=warm[:, 0:1], func=ACT.Sqrt)
        nc.sync.dma_start(pilots[:], offs)
        load_wq(0)
        load_scale_rows(tab_s, tab_scales[0])
        nc.sync.dma_start(out=tab_w[:], in_=tab_words[0].rearrange("p t i -> p (t i)").bitcast(I32))
        load_wr(0)
        load_scale_rows(wr_s, wr_scales[0])
        with nc.allow_non_contiguous_dma(reason="one noise power a partition"):
            nc.sync.dma_start(out=nv_first[:], in_=nv[0 : 2 * P].rearrange("(b p) -> p b", p=P))
        nc.sync.dma_start(slots[:], offs2)
        first_width = FIRST_PIECES[0][1]
        nc.sync.dma_start(out=wgs_nat[:, 0:first_width], in_=wgs[:, 0:first_width])
        nc.sync.dma_start(out=wgs_nat[:, first_width:S], in_=wgs[:, first_width:S])
        load_wq(1)
        load_wr(1)
        with nc.allow_non_contiguous_dma(reason="one noise power a partition"):
            nc.sync.dma_start(out=nv_nat[:], in_=nv[2 * P : PASS].rearrange("(b p) -> p b", p=P))
        nc.sync.dma_start(carriers[:], offs3)
        err_nat = err[0:PASS, :].rearrange("(t p) m -> p t m", p=P)
        err_four = err[PASS : 2 * PASS, :].rearrange("(p t) m -> p (t m)", t=4)
        wgs_rows = wgs.rearrange("(r t) j -> r (t j)", t=4)

        def load_err_nat(t0):
            nc.sync.dma_start(out=err_a[:, M * t0 : M * (t0 + 2)].rearrange("p (t m) -> p t m", t=2), in_=err_nat[:, t0 : t0 + 2, :])

        def load_wgs_four(t0):
            for q in range(4):
                nc.sync.dma_start(out=wgs_four[32 * q : 32 * q + 32, S * t0 : S * (t0 + 2)], in_=wgs_rows[:, S * t0 : S * (t0 + 2)])

        load_err_nat(0)
        for load in (2, 3):
            load_wq(load)
        load_wr(2)
        for a in (1, 2):
            nc.sync.dma_start(out=nv_four[a - 1][:], in_=nv[PASS * a : PASS * (a + 1)].rearrange("(p t) -> p t", t=4))
        load_wq(4)
        load_wgs_four(0)
        load_err_nat(2)
        load_wgs_four(2)
        nc.sync.dma_start(out=err_b[:, 0 : 2 * M], in_=err_four[:, 0 : 2 * M])
        load_wr(3)
        nc.sync.dma_start(out=err_b[:, 2 * M : 4 * M], in_=err_four[:, 2 * M : 4 * M])
        nc.sync.dma_start(out=wm_w[:].rearrange("p (a c) -> p a c", a=3), in_=wm_words.rearrange("a p c i -> p a (c i)").bitcast(I32))
        make_identity(nc, ident[:])
        for page in pages:
            nc.vector.memset(page[:].bitcast(I32), 0)

        def entries(lst, j0, width):
            return lst[:, j0 // LIST_ROWS : (j0 + width) // LIST_ROWS]

        def columns(parts, c0):
            part = max(i for i in range(len(parts)) if parts[i][0] <= c0)
            return part, c0 - parts[part][0]

        def first_products(out_re, out_im, j0, c0, width):
            lhs = v_w[:, j0 : j0 + P].bitcast(E4M3)
            lhs_s = v_s[0][:, j0 : j0 + P] if j0 < SCALES_AHEAD else v_s[1][:, j0 - SCALES_AHEAD : j0 - SCALES_AHEAD + P]
            part, c = columns(WQ_PARTS, c0)
            nc.tensor.matmul_mx(
                out=out_im, lhsT=lhs, lhsT_scale=lhs_s,
                rhs=wq_w[part][:, c : c + width].bitcast(E4M3), rhs_scale=wq_s[part][:, c : c + width], start=True, stop=True,
            )
            part, c = columns(WR_PARTS, c0)
            nc.tensor.matmul_mx(
                out=out_re, lhsT=lhs, lhsT_scale=lhs_s,
                rhs=wr_w[part][:, 2 * c : 2 * (c + width)].bitcast(E2M1), rhs_scale=wr_s[:, c0 : c0 + width], start=True, stop=True,
            )

        def add_turned(dst, first, second):
            nc.tensor.matmul(out=dst, lhsT=first, rhs=ident[:], is_transpose=True, start=True, stop=False)
            nc.tensor.matmul(out=dst, lhsT=second, rhs=ident[:], is_transpose=True, start=False, stop=True)

        def envelope_rows(b, j0, width, product_banks, bank_sum, squares):
            per_bank = width // (len(product_banks) * P)
            used = 2 * P * per_bank
            for n, bank in enumerate(product_banks):
                for i in range(per_bank):
                    first_products(
                        bank[:, 2 * P * i : 2 * P * i + P], bank[:, 2 * P * i + P : 2 * P * (i + 1)], j0 + P * (per_bank * n + i), P * b, P
                    )
                nc.scalar.activation(out=squares[n], in_=bank[:, 0:used], func=ACT.Square)
            for i in range(width // P):
                n, c = divmod(2 * P * i, used)
                add_turned(bank_sum[:, P * i : P * (i + 1)], squares[n][:, c : c + P], squares[n][:, c + P : c + 2 * P])
            nc.scalar.activation(out=quarter(env, b, width, j0), in_=bank_sum[:, 0:width], func=ACT.Sqrt, bias=nv_first[:, b : b + 1])

        product_banks = [banks[n] for n in (0, 1, 2, 4)]

        def squares_of_block(a, block):
            pair = product_banks[2:4] if block % 2 == 0 else product_banks[0:2]
            first_products(pair[0][:], pair[1][:], P * block, PASS * a, PASS)
            piece, i = divmod(block, 2)
            parts = [(quarter(re_piece(piece), a - 1), pair[0], 0, 4)]
            if (a, piece) == (2, 3):
                parts.extend([(im_2_last[:], pair[1], 0, 3), (im_2_end[:], pair[1], 3, 4)])
            else:
                parts.append((quarter(im_1 if a == 1 else im_2, piece), pair[1], 0, 4))
            for dst, bank, t0, t1 in parts:
                nc.scalar.activation(
                    out=dst.rearrange("j (t i p) -> j i t p", i=2, p=P)[:, i],
                    in_=bank[:].rearrange("j (p t) -> j t p", t=4)[:, t0:t1], func=ACT.Square,
                )

        def envelope(b, pieces, dst, between=None):
            for n, piece in enumerate(pieces):
                squares_re, squares_im = squares_at(b, piece)
                for c in (0, P):
                    add_turned(banks[3][:, WIDE * n + c : WIDE * n + c + P], squares_re[:, c : c + P], squares_im[:, c : c + P])
            if between:
                between()
            bias = nv_nat[:, b - 2 : b - 1] if b < 4 else nv_four[b // 4 - 1][:, b % 4 : b % 4 + 1]
            nc.scalar.activation(out=dst, in_=banks[3][:, 0 : WIDE * len(pieces)], func=ACT.Sqrt, bias=bias)

        def scatter(page, j0, width, values, weights):
            nc.vector.tensor_tensor(out=pages[page][:].indirect(entries(slots, j0, width)), in0=values, in1=weights, op=ALU.mult)

        def gather(page, t, m0, width, dst, errors):
            nc.vector.tensor_tensor(
                out=dst, in0=pages[page][:].indirect(entries(carriers, m0, width)), in1=quarter(errors, t, width, m0), op=ALU.add
            )

        def turn_first_pass(z_nat, rounded_at):
            for group in range(4):
                bank_back = banks[6 + group % 2]
                for i in range(2):
                    bank_in = banks[3] if group < 2 and i == 0 else product_banks[2 + i]
                    for t in range(4):
                        nc.tensor.transpose(bank_in[:, P * t : P * (t + 1)], z_nat(t, group)[:, P * i : P * (i + 1)], ident[:])
                    nc.scalar.copy(
                        out=z_rows[i][:].rearrange("m (u p e) -> m u p e", u=2, e=2),
                        in_=bank_in[:].rearrange("m (p u e) -> m u p e", u=2, e=2),
                    )
                    for u in range(2):
                        nc.tensor.transpose(
                            bank_back[:, P * (2 * i + u) : P * (2 * i + u + 1)], z_rows[i][:].bitcast(F32)[:, P * u : P * (u + 1)], ident[:]
                        )
                nc.scalar.copy(
                    out=rounded_at(0, group).rearrange("p (i m u) -> p i m u", i=2, u=2),
                    in_=bank_back[:].rearrange("p (i u m) -> p i m u", i=2, u=2),
                )

        def late_page(tag):
            page = tile("page%d" % len(pages), T2, F32, tag)
            nc.gpsimd.memset(page[:], 0.0)
            pages.append(page)

        def gather_scales(dst, j0, width):
            nc.vector.tensor_copy(out=dst[:], in_=tab_s[:].indirect(entries(pilots, j0, width)))

        def gather_words(j0, width):
            nc.vector.tensor_copy(out=v_w[:, j0 : j0 + width], in_=tab_w[:].bitcast(U32).indirect(entries(pilots, j0, width)))

        gather_scales(v_s[0], 0, SCALES_AHEAD)
        quantise_wq(0, (0,), wq_first[:], 2 * P)
        gather_words(0, first_width)
        gather_words(first_width, S - first_width)
        before_page3 = tile("before_page3", PASS, F32, "ends_as_page3")

        def both_tiles(block, bank, dst, c0=0, im_first=False):
            halves = (bank[:, 0 : 2 * P], bank[:, 2 * P : 4 * P])
            first_products(halves[int(im_first)], halves[1 - int(im_first)], P * block, c0, 2 * P)
            nc.scalar.activation(out=dst, in_=bank[:].rearrange("j (h t p) -> j h t p", h=2, t=2), func=ACT.Square)

        def envelope_piece(b, block0, views, bank_sum, between=None):
            j0, width = P * block0, P * len(views)
            for i, view in enumerate(views):
                add_turned(bank_sum[:, P * i : P * (i + 1)], view[:, 0, b, :], view[:, 1, b, :])
            if between:
                between()
            nc.scalar.activation(out=quarter(env, b, width, j0), in_=bank_sum[:, 0:width], func=ACT.Sqrt, bias=nv_first[:, b : b + 1])
            scatter(b, j0, width, quarter(env, b, width, j0), wgs_nat[:, j0 : j0 + width])

        envelope_rows(0, 0, first_width, banks[0:2], banks[3], [first_squares[:], im_2[:, 0:first_width]])
        v_s.append(tile("v_s1", S - SCALES_AHEAD, U8, "ends_as_v_s1"))
        gather_scales(v_s[1], SCALES_AHEAD, S - SCALES_AHEAD)
        wm_s = tile("wm_s", 3 * N, U8, "ends_as_wm_s")
        nc.gpsimd.memset(wm_s[:].bitcast(I32), 0)
        for q in range(4):
            nc.sync.dma_start(
                out=wm_s[32 * q : 32 * q + 4, :].bitcast(I32).rearrange("p (a c) -> p a c", a=3),
                in_=wm_scales[:, 4 * q : 4 * q + 4, :].rearrange("a r c -> r a c").bitcast(I32),
            )
        scatter(0, 0, first_width, quarter(env, 0, first_width), wgs_nat[:, 0:first_width])
        envelope_rows(1, 0, first_width, banks[2:3], banks[4], [im_2[:, PASS:M]])
        scatter(1, 0, first_width, quarter(env, 1, first_width), wgs_nat[:, 0:first_width])

        late_squares = im_2[:, M : 3 * M]
        late = late_squares.rearrange("j (t i h p) -> j i h t p", t=2, i=4, h=2)
        views = {block: late[:, block - 4] for block in range(4, 8)}
        for block, early in ((2, before_page3), (3, before_page2)):
            views[block] = early[:].rearrange("j (h t p) -> j h t p", h=2, t=2)
        for block in (2, 3, 4):
            both_tiles(block, banks[block], views[block])
        for b in (0, 1):
            envelope_piece(b, 2, [views[2], views[3]], banks[2 + b])
        late_page("ends_as_page2")
        late_page("ends_as_page3")
        for block, bank in ((5, 4), (6, 2), (7, 3)):
            both_tiles(block, banks[bank], views[block])
        envelope_piece(
            0, 4, [views[block] for block in range(4, 8)], banks[4],
            lambda: quantise_wq(1, (1,), late_squares[:, WIDE : 3 * WIDE].bitcast(BF16), 2 * P),
        )
        envelope_piece(
            1, 4, [views[block] for block in range(4, 8)], banks[3],
            lambda: quantise_wq(2, (2, 3), late_squares[:, M : 2 * M].bitcast(BF16), P),
        )

        def squares_at(b, piece):
            if b < 4:
                c = S * piece + WIDE * (b - 2)
                low, high = sq_nat[:, c : c + WIDE], sq_nat[:, PASS + c : PASS + c + WIDE]
                return (low, high) if piece % 2 == 0 else (high, low)
            squares_re = re_piece(piece)[:, WIDE * (b - 4) : WIDE * (b - 3)]
            if (b, piece) == (11, 3):
                return squares_re, im_2_end[:]
            squares_im = quarter(im_1, piece) if b < 8 else quarter(im_2, piece) if piece < 3 else im_2_last
            return squares_re, squares_im[:, WIDE * (b % 4) : WIDE * (b % 4 + 1)]

        def z_nat(b, piece):
            return squares_at(b + 2, piece)[0]

        nat = sq_nat.rearrange("j (q h t i p) -> j q i h t p", h=2, q=4, t=2, i=2)

        def squares_of_piece(b, piece):
            for block in (2 * piece, 2 * piece + 1):
                if b == 2:
                    both_tiles(block, product_banks[block % 4], nat[:, piece, block % 2], 2 * P, piece % 2 == 1)
                else:
                    squares_of_block(b // 4, block)

        def woven(pair):
            for piece in range(4):
                j0 = WIDE * piece
                if pair[0] in (2, 4, 8):
                    squares_of_piece(pair[0], piece)
                for b in pair:
                    cast = (lambda: quantise_wq(3, (4,), sq_nat[:, PASS : PASS + S].bitcast(BF16), P)) if (b, piece) == (3, 1) else None
                    envelope(b, (piece,), quarter(env, b % 4, WIDE, j0), cast)
                    gather((b - 2) % 4, (b - 2) % 4, j0, WIDE, z_nat(b - 2, piece), err_b if 4 <= b - 2 < 8 else err_a)
                    weights = wgs_nat[:, j0 : j0 + WIDE] if b < 4 else quarter(wgs_four, b % 4, WIDE, j0)
                    scatter(b % 4, j0, WIDE, quarter(env, b % 4, WIDE, j0), weights)

        woven((2, 3))
        woven((4, 5))
        nc.sync.dma_start(out=err_a[:], in_=err[2 * PASS : 3 * PASS, :].rearrange("(p t) m -> p (t m)", t=4))
        woven((6, 7))
        woven((8, 9))

        rounded_early = [quarter(sq_nat, 0), quarter(sq_nat, 1), quarter(im_2, 0), quarter(im_2, 2)]

        def place_of(a, piece):
            return 1 - a if piece == 0 else a

        def rounded_at(a, piece):
            return rounded_early[piece][:, PASS * place_of(a, piece) : PASS * (place_of(a, piece) + 1)]

        def round_pass_1(piece):
            z_rows_4 = re_piece(piece)[:, 2 * WIDE : 6 * WIDE].rearrange("p (i m) -> p i m", i=4)
            interleave(nc.scalar.copy, rounded_at(1, piece).bitcast(BF16), z_rows_4)

        words_early = []
        held = []

        def quantise_early(piece, count, rounded):
            if piece != 2:
                words = tile("words%d" % piece, PASS * (3 if piece == 0 else 1), U32, "ends_as_words%d" % piece)
                words_early.extend(words[:, c : c + PASS] for c in range(0, words.shape[1], PASS))
                held.append(words)
            words = held[-1][:, PASS * (piece % 3) : PASS * (piece % 3 + count)]
            nc.vector.quantize_mx(
                out=words.bitcast(E4M3), scales=z_early_s[:, PASS * piece : PASS * (piece + count)], in_=rounded.bitcast(BF16)
            )

        Z_RUNS = {2: (45, 46, 48, 49), 3: (45, 46, 50, 51)}

        def gather_late(t, piece, col=0, width=WIDE):
            gather(t, t, WIDE * piece + col, width, runs[:, Z_RUNS[piece][t], col : col + width], err_a)

        def z_pass_2(c):
            piece, col = divmod(CHUNKS[c][0], WIDE)
            low, high = Z_RUNS[piece][0], Z_RUNS[piece][2]
            both = sq[:, WIDE * low : WIDE * (2 * high - low)].rearrange("p (u n m) -> p u n m", u=2, m=WIDE)
            return both[:, :, 0:2, col : col + CHUNKS[c][1]]

        rounded_first = sq[:, 48 * WIDE : 52 * WIDE].bitcast(BF16)
        rounded_2 = [rounded_first[:, 0 : 4 * WIDE], rounded_first[:, 4 * WIDE : 8 * WIDE]]
        rounded_2.extend(tile("rounded_2_%d" % c, 4 * CHUNKS[c][1], BF16)[:] for c in (2, 3, 4))
        env_last = tile("env_last", WIDE, F32, "ends_as_words3")

        def round_late(engine_copy, c):
            engine_copy(
                out=rounded_2[c].rearrange("p (c x u e) -> p c u e x", x=4, u=2, e=2),
                in_=z_pass_2(c).rearrange("p u e (c x) -> p c u e x", x=4),
            )

        turn_first_pass(z_nat, rounded_at)
        round_pass_1(1)
        round_pass_1(0)
        for piece in range(4):
            j0, m0 = WIDE * piece, NARROW * RE_ORDER.index(piece)
            for b in (10, 11):
                values = env_last[:] if (b, piece) == (11, 3) else quarter(env, b % 4, WIDE, j0)
                envelope(b, (piece,), values)
                gather(b - 10, b - 10, m0, NARROW, squares_at(b, piece)[0][:, NARROW:WIDE], err_a)
                if (b, piece) == (10, 3):
                    quantise_early(0, 2, sq_nat[:, 0 : 2 * S])
                    quantise_early(2, 1, rounded_early[2])
                scatter(b % 4, j0, WIDE, values, quarter(wgs_four, b % 4, WIDE, j0))
            if piece in (0, 2):
                round_pass_1(2 + piece // 2)

        nc.scalar.copy(
            out=rounded_first.rearrange("p (h c x u e) -> p u h c e x", h=4, x=4, u=2, e=2)[:, 0],
            in_=re_late.rearrange("p (h b s c x) -> p s h c b x", h=4, b=8, s=2, x=4)[:, 1, :, :, 6:8],
        )

        def z_operand(a, c):
            m0, width = CHUNKS[c]
            if a == 2:
                return z_w[:, m0 : m0 + width], z_s[:, m0 : m0 + width]
            piece, col = divmod(m0, WIDE)
            first = WIDE * place_of(a, piece) + col
            return words_early[piece][:, first : first + width], z_early_s[:, PASS * piece + first : PASS * piece + first + width]

        staged = [err_b[:, PASS * n : PASS * (n + 1)] for n in range(8)] + [im_1[:, PASS * n : PASS * (n + 1)] for n in range(3)]
        out_n = out.rearrange("(i p) m -> p i m", p=P)
        open_banks = []

        def products(c, out_tiles, passes, closing=()):
            width = CHUNKS[c][1]
            for a in passes:
                words, plane = z_operand(a, c)
                for i in out_tiles:
                    bank, col = PLACES[c][i]
                    start = bank not in open_banks
                    if start:
                        open_banks.append(bank)
                    stop = i in closing
                    if stop:
                        open_banks.remove(bank)
                    nc.tensor.matmul_mx(
                        out=banks[bank][:, col : col + width],
                        lhsT=wm_w[:, N * a + P * i : N * a + P * (i + 1)].bitcast(E4M3), lhsT_scale=wm_s[:, N * a + P * i : N * a + P * (i + 1)],
                        rhs=words.bitcast(E4M3), rhs_scale=plane, start=start, stop=stop,
                    )

        def store(engine_copy, bank, i0, count, m0, width):
            result = staged.pop(0)[:, 0 : count * width]
            engine_copy(out=result, in_=banks[bank][:, 0 : count * width])
            nc.sync.dma_start(out=out_n[:, i0 : i0 + count, m0 : m0 + width], in_=result.rearrange("p (i m) -> p i m", i=count))

        def last_pass(c, closing, out_tiles=range(5)):
            words, plane = z_operand(2, c)
            nc.vector.quantize_mx(out=words.bitcast(E4M3), scales=plane, in_=rounded_2[c])
            products(c, out_tiles, (2,), closing)

        for c in range(2):
            products(c, range(5), (0, 1))
        for c, pair in enumerate((sq[:, 44 * WIDE : 46 * WIDE], tile("z_pair", 2 * WIDE, F32, "ends_as_words3")[:])):
            for e in range(2):
                gather(2 + e, 2 + e, WIDE * c, WIDE, pair[:, WIDE * e : WIDE * (e + 1)], err_a)
            nc.scalar.copy(
                out=rounded_2[c].rearrange("p (c x u e) -> p u c e x", x=4, u=2, e=2)[:, 1],
                in_=pair.rearrange("p (e c x) -> p c e x", e=2, x=4),
            )
        gather_late(1, 2)
        last_pass(0, (1, 3))
        products(2, range(5), (0, 1))
        store(nc.scalar.copy, 0, 0, 2, 0, 256)
        store(nc.scalar.copy, 1, 2, 2, 0, 256)
        for t in (0, 2, 3):
            gather_late(t, 2)
        round_late(nc.scalar.copy, 2)
        last_pass(1, (1, 3, 4))
        store(nc.scalar.copy, 3, 0, 2, 256, 256)
        store(nc.scalar.copy, 4, 2, 2, 256, 256)
        store(nc.scalar.copy, 2, 4, 1, 0, 512)
        quantise_early(3, 1, rounded_early[3])
        products(3, range(5), (0, 1))
        gather_late(2, 3)
        gather_late(3, 3)
        last_pass(2, (1, 3))
        products(4, range(5), (0, 1))
        store(nc.scalar.copy, 5, 0, 2, 512, 256)
        store(nc.scalar.copy, 6, 2, 2, 512, 256)
        gather_late(0, 3)
        gather_late(1, 3, 0, NARROW)
        gather_late(1, 3, NARROW, NARROW)
        round_late(nc.vector.tensor_copy, 3)
        round_late(nc.vector.tensor_copy, 4)
        last_pass(3, (3, 4), (4, 0, 1, 2, 3))
        last_pass(4, (2, 4))
        store(nc.scalar.copy, 7, 4, 1, 512, 384)
        store(nc.vector.tensor_copy, 0, 0, 4, 768, 128)
        store(nc.scalar.copy, 1, 0, 3, 896, 128)
        store(nc.vector.tensor_copy, 3, 3, 2, 896, 128)
